import numpy as np, ml_dtypes
CORES = [2,6,10,14,18,22,26,30]
N = 8
BF = ml_dtypes.bfloat16
W, S, H, R, CAP, HOP, ST = 4096, 256, 2048, 3, 512, 2, 683
P, E = W + R * S, S // N
AT = np.arange(W)
def hashed(u, lo, A):
    m = (61 * np.arange(16) + 7)[:, None]; u = u[:, :, None, :]
    return lo + (((u * u >> 5) + m * u + A[:, :, None, None]) & (W - 1))
def older(rng, *shape):
    return AT - 1 - np.minimum((AT * rng.random(shape + (W,)) ** 2).astype(np.int64), np.maximum(AT - 1, 0))
def parts(rng):
    off = rng.integers(-12, 9, (N, 8, 1, 1))
    X = np.clip(70 + rng.integers(-20, 21, (N, 8, 1, W)) + rng.integers(-60, 61, (N, 8, 16, W)), 0, 255)
    a = 2 * (70 + off + rng.integers(-20, 21, (N, 8, 1, S)) + rng.integers(-60, 61, (N, 8, 16, S))) + rng.integers(0, 2, (N, 8, 16, S))
    b = 80 + off + rng.integers(-50, 51, (N, 8, 1, (R - 1) * S)) + rng.integers(-100, 101, (N, 8, 16, (R - 1) * S))
    D = np.where(rng.random((N, 8, 16, W)) < 0.75, older(rng, N, 8, 16), -1); C = np.where(rng.random((N, 8, W)) < 0.9, older(rng, N, 8), -1)
    n = np.clip(W + S - 1 - ((W + S) * rng.random((N, 8, (R - 1) * S)) ** 2).astype(np.int64), 0, W + S - 1)
    return X, np.clip(np.concatenate([a, b], axis=3), 0, 255), D, C, n
def pack(X, a, D, C, n):
    return {"x0": X.reshape(N, 128, W).astype(np.float32).astype(BF), "come": a.reshape(N, 128, R * S).astype(np.float32).astype(BF),
            "dl0": np.ascontiguousarray(D[..., W - H:]).reshape(N, 128, H).astype(np.int32), "cd0": C.astype(np.int32), "age": n.astype(np.int32)}
def setup_inputs(rng):
    return pack(*parts(rng))
def setup_inputs_spread(rng):
    X = (256 * rng.random((N, 8, 16, W)) * np.exp2(-rng.integers(0, 7, (N, 8, 1, W)))).astype(np.int64)
    a = (256 * rng.random((N, 8, 16, R * S)) * np.exp2(-rng.integers(0, 5, (N, 8, 1, R * S)))).astype(np.int64)
    D = np.minimum(((AT + 1) * rng.random((N, 8, 16, W))).astype(np.int64), AT) - 1; C = np.minimum(((AT + 1) * rng.random((N, 8, W))).astype(np.int64), AT) - 1
    return pack(np.clip(X, 0, 255), np.clip(a, 0, 255), D, C, rng.integers(0, W + S, (N, 8, (R - 1) * S)))
def setup_inputs_ends(rng):
    X, a, D, C, n = parts(rng)
    def two(k):
        kind = rng.integers(0, 4, (N, 8, 1, k))
        return 255 * np.where(kind == 0, 0, np.where(kind == 1, 1, rng.integers(0, 2, (N, 8, 16, k))))
    X, a = two(W), two(R * S)
    r = rng.random(D.shape); D = np.where(r < 0.64, -1, np.where(r < 0.84, AT - 1, D))
    r = rng.random(C.shape); C = np.where(r < 0.64, -1, np.where(r < 0.84, AT - 1, C))
    n = (W + S - 1) * rng.integers(0, 2, n.shape)
    c = hashed(np.full((N, 8, 1), 16 * 127), 0, np.zeros((N, 8), np.int64))[0, 0, :, 0]
    X[..., c] = 255; C[..., c] = -1; X[:, 7, :, 0] = 255; X[:, 7, :, W - 1] = 255
    D[..., W - 1] = np.where(np.arange(16) % 2 == 0, W - 2, -1); C[:, ::2, W - 1] = -1; C[:, 1::2, W - 1] = W - 2
    last = np.arange(E - 1, S, E); a[..., last] = 255; a[..., S + last] = 255; n[..., last] = W + S - 1
    X[:, 5] = 0; X[:, 6] = 0; X[:, 6, :, W - 1] = 255; X[0, 7] = 0
    s = 4000 + np.array([11, 21, 27, 37, 43, 53, 59, 69]); h = hashed(np.zeros((N, 8, 8), np.int64) + s, S, np.zeros((N, 8), np.int64))[0, 0]
    good = h[15][h[15] < W]; half = 255 * (np.arange(16) % 2 == 0).astype(np.int64)[:, None]
    X4 = X[:, 4]; X4[:, :6] = 255; X4[..., h[h < W]] = half; X4[..., S] = half[:, 0]; X4[..., good] = 255
    C[:, 4, good] = -1; C[:, 4, int(np.min(good))] = S
    a[:, 4, :, :S] = 255; n[:, 4, :S] = W + S - 1; n[:, 4, S + 1:2 * S:2] = W + S - 1
    u = rng.integers(3841, 4075, (N, S)); u[:, 1::2] = s[np.arange(S // 2) & 7]; short = 4080 - u
    lack = (short >> 4)[:, None, :] + (((np.arange(16)[:, None] + np.arange(S)) & 15) < (short & 15)[:, None, :]).astype(np.int64)
    a[:, 4, :, S:2 * S] = 255 - 2 * lack
    a[:, 4, :6, 2 * S:] = 0; a[:, 4, :, 2 * S + 1:3 * S:2] = 255; a[:, 4, :6, 2 * S + 1:3 * S:2] = 253
    return pack(X, a, D, C, n)
def setup_inputs_corners(rng):
    X, a, D, C, n = parts(rng); X = 128 + (X >> 1); F = W // 8
    kind = rng.integers(0, 4, (N, 8, 1, W))
    D = np.where(kind == 0, -1, np.where(kind == 1, D[:, :, :1], D)); C[:, 1::3] = AT - 1
    edge = np.array([W - 1, ST - 1, ST])
    for q in range(N):
        for g in range(8):
            xg, dg, cg = X[q, g], D[q, g], C[q, g]
            dead = np.unique(np.append(rng.integers(1, F, 7), 0)); xg[:, dead] = 0
            cg[np.isin(cg, dead)] = -1
            k = (0, 1, CAP - 1, CAP, CAP + 1, W - F, CAP, CAP + 1)[(g + q) % 8]
            o = np.append(edge, rng.permutation(np.setdiff1d(np.arange(F, W), edge)))[:k]
            cg[o] = rng.choice(dead, len(o))
            gone = np.flatnonzero(kind[q, g, 0] == 2); gone = gone[gone >= F]; dg[:, gone] = rng.choice(dead, (16, len(gone)))
    x = a[..., :S] >> 1; c = hashed(np.add.reduce(x, axis=2), 0, np.zeros((N, 8), np.int64))
    live = np.max(X, axis=2) > 0; ok = np.take_along_axis(live, c.reshape(N, 8, 16 * S), 2).reshape(c.shape)
    up = np.max(np.where(ok, c, -1), axis=2); up2 = np.take_along_axis(C, np.maximum(up, 0), 2)
    y, y2 = W + S - 1 - up, W + S - 1 - up2
    n[..., :S] = np.clip(np.choose(rng.integers(0, 6, up.shape), [y, y - 1, y2, y2 - 1, 0 * y, 0 * y + W + S - 1]), 0, W + S - 1)
    return pack(X, a, D, C, n)
def setup_inputs_crowd(rng):
    X, a, D, C, n = parts(rng)
    for q in range(N):
        for g in range(8):
            k = (g + q) % 8; xg, ag, dg, cg = X[q, g], a[q, g], D[q, g], C[q, g]
            if k == 0: xg[:] = 0
            elif k == 1:
                xg[:] = 0; xg[:, int(rng.choice(np.array([0, 1, W - 2, W - 1])))] = 255
            elif k == 2 or k == 3:
                e = q & 1
                xg[:] = 128 + (xg >> 1); xg[:, e] = 0; xg[:, 1 - e] = 255; cg[1 + e:] = e; dg[:, 2:] = 1 - e
                if e == 1: cg[2:W >> 1] = -1
                if k == 3:
                    cg[W - 1] = -1; dg[:15, 2:] = -1
            elif k == 4:
                ag[:] = np.repeat(ag[:, ::S], S, axis=1); n[q, g] = W + S - 1
            elif k == 5:
                b = int(rng.integers(0, S)); us = rng.permutation(np.arange(400, 3600)); tab = np.zeros(S, np.int64)
                tab[(us * us >> 5) & (S - 1)] = us; u = tab[(b - AT) & (S - 1)]
                xg[:] = (u >> 4) + (np.arange(16)[:, None] < (u & 15)).astype(np.int64)
            elif k == 6:
                cg[:] = AT - 1; dg[:] = AT - 1
            else:
                xg[:] = 60 + (xg >> 2); ag[:, :S] = ag[:, :S] >> 2; ag[:, S:2 * S] = 254; ag[:, 2 * S:3 * S] = 0
                if q & 1: xg[:, int(rng.choice(np.array([S, W - 1])))] = 255
    return pack(X, a, D, C, n)
def setup_inputs_ties(rng):
    X, a, D, C, n = parts(rng)
    X = 60 + rng.integers(0, 2, (N, 8, 1, 1)) + rng.integers(0, 4, X.shape); a = 60 + rng.integers(0, 4, a.shape)
    a[..., :S] = 120 + rng.integers(0, 8, (N, 8, 16, S))
    o = np.argsort(rng.random((N, 2, 16, S)), axis=2); k = rng.integers(4, 8, (N, 2, 1, S))
    X[:, 2:4] = 62
    lower = 62 - (o[:, 0] < k[:, 0]).astype(np.int64)
    both = 62 + (o[:, 1] < k[:, 1]).astype(np.int64) - (o[:, 1] >= 10).astype(np.int64)
    a[:, 2, :, :S] = 2 * lower + rng.integers(0, 2, lower.shape); a[:, 3, :, :S] = 2 * both + rng.integers(0, 2, both.shape)
    return pack(X, a, D, C, n)
def check_inputs(d):
    bad = []
    for k, lo, hi in (("x0", 0, 255), ("come", 0, 255), ("dl0", -1, W - 2), ("cd0", -1, W - 2), ("age", 0, W + S - 1)):
        v = np.asarray(d[k]).astype(np.float64)
        if not np.all((v >= lo) & (v <= hi)): bad.append("range of " + k)
        elif not np.all(v == np.floor(v)): bad.append("whole numbers in " + k)
    if np.any(np.asarray(d["dl0"]) >= np.arange(W - H, W)): bad.append("the witnesses in dl0 are older places")
    if np.any(np.asarray(d["cd0"]) >= np.arange(W)): bad.append("the parents in cd0 are older places")
    return bad
def judge(X, live, c, y):
    k = c.shape[-1]; i = np.maximum(c, 0).reshape(N, 8, 16 * k)
    v = np.take_along_axis(X, i[:, :, None, :], 3).reshape(N, 8, 16, 16, k)
    more = np.add.reduce((v >= y[:, :, :, None, :]).astype(np.int32), axis=2)
    return (c >= 0) & (more >= 11) & np.take_along_axis(live, i, 2).reshape(N, 8, 16, k)
def reference(x0, come, dl0, cd0, age):
    X = np.zeros((N, 8, 16, P), np.int64); X[..., :W] = x0.astype(np.float32).astype(np.int64).reshape(N, 8, 16, W)
    D = np.full((N, 8, 16, P), -1, np.int64); D[..., W - H:W] = dl0.reshape(N, 8, 16, H)
    C = np.full((N, 8, P), -1, np.int64); C[..., :W] = cd0
    a = come.astype(np.float32).astype(np.int64).reshape(N, 8, 16, R, S); n = age.astype(np.int64).reshape(N, 8, R - 1, S)
    live = np.zeros((N, 8, P), bool); live[..., :W] = True
    z = np.zeros((N, 8, 16, S), np.int64); A = np.zeros((N, 8), np.int64)
    for t in range(R):
        lo = S * t; B = W + S * t
        live[..., :lo] = False
        x = (a[:, :, :, t] + z) >> 1; X[..., B:B + S] = x
        old = X[..., lo:B]; u = np.add.reduce(old, axis=2)
        who = ((u * u >> 5) + np.arange(lo, B)) & (S - 1)
        over = np.add.reduce((np.take_along_axis(x, who[:, :, None, :], 3) >= old).astype(np.int32), axis=2)
        die = live[..., lo:B] & (over >= 11); live[..., lo:B] = live[..., lo:B] & ~die
        c = hashed(np.add.reduce(x, axis=2), lo, A)
        c = np.where(judge(X, live, c, x), c, -1)
        D[..., B:B + S] = c; C[..., B:B + S] = np.max(c, axis=2); live[..., B:B + S] = True
        A = np.add.reduce(die.astype(np.int64), axis=2)
        cd = C[..., lo:B]
        orphan = live[..., lo:B] & (cd >= 0) & ~np.take_along_axis(live, np.maximum(cd, 0), 2)
        turn = np.roll(orphan, -ST * (t + 1), axis=2)
        turn = turn & (np.add.accumulate(turn.astype(np.int64), axis=2) <= CAP)
        taken = np.roll(turn, ST * (t + 1), axis=2)
        o = np.argsort(~taken, axis=2, kind="stable")[..., :CAP]; use = np.take_along_axis(taken, o, 2); o = o + lo
        y = np.take_along_axis(X, o[:, :, None, :], 3); d = np.take_along_axis(D, o[:, :, None, :], 3)
        left = np.where(judge(X, live, d, y), d, -1); b = np.max(left, axis=2)
        xb = np.take_along_axis(X, np.maximum(b, 0)[:, :, None, :], 3)
        y = np.where((use & (b >= 0))[:, :, None, :], (y + xb) >> 1, y)
        b = np.where(use, b, np.take_along_axis(C, o, 2)); d = np.where(use[:, :, None, :], left, d)
        np.put_along_axis(X, o[:, :, None, :], y, 3); np.put_along_axis(D, o[:, :, None, :], d, 3); np.put_along_axis(C, o, b, 2)
        if t < R - 1:
            w = np.zeros((N, 8, S), np.int64) + np.arange(B, B + S)
            for h in range(HOP):
                up = np.take_along_axis(C, w, 2)
                w = np.where((up >= 0) & (B + S - 1 - up <= n[:, :, t]), up, w)
            out = np.take_along_axis(X, w[:, :, None, :], 3).reshape(N, 8, 16, N, E)
            z = np.ascontiguousarray(out.transpose(3, 1, 2, 0, 4)).reshape(N, 8, 16, S)
    lo = S * (R - 1)
    return {"yx": np.ascontiguousarray(X[..., lo:]).reshape(N, 128, W + S).astype(np.float32).astype(BF), "yc": C[..., lo:].astype(np.float32), "ya": live[..., lo:].astype(np.float32)}

@@ -1,0 +1,657 @@
+import numpy as np
+from concourse.bass import DstId, RemoteDMATransfer
+from concourse.mybir import AluOpType as ALU, AxisListType as AX, ActivationFunctionType as AF
+
+W, S, R, CAP, ST, N = 4096, 256, 3, 512, 683, 8
+OFF = 544
+TW = OFF + W + R * S
+WK = 16384.0
+KD = 10 * WK + 8192.0
+BIG = 100000.0
+S3_ACT = (1, 3, 5, 7)
+P_ACT = (1, 3)
+J_ACT = (4, 5, 10, 11)
+J_CUT = 12
+D2_ACT, NX_ACT, Q_ACT = False, True, 1
+SAME_QUEUE_WAW = True
+
+F, B16, I32, U16 = "float32", "bfloat16", "int32", "uint16"
+SCRATCH = {}
+for _n, _c, _d in [
+    ("X", TW, B16), ("XA", TW, B16), ("C", TW + 512, B16), ("D", TW, F),
+    ("cm", 768, B16), ("cmh", 768, F), ("xi", 256, I32), ("z0", 256, B16), ("z1", 256, B16), ("zs0", 256, B16), ("zs1", 256, B16),
+    ("dli", 2048, I32), ("cdi", 288, I32), ("cdf", 288, F), ("cdh", 288, B16), ("cdl", 288, B16),
+    ("pi", 8, I32), ("pc", 16, F), ("ia", 256, F), ("ib", 128, F), ("ic", 256, F), ("kf", 512, F), ("ku", 512, U16), ("kw", 32, F),
+    ("Z1", 144, B16), ("Z16", 144, B16), ("Z128", 144, B16), ("Z256", 144, B16), ("ZW", 144, B16), ("ZH", 144, B16), ("ZM", 16 * 144, B16),
+    ("BO", 128, B16), ("B512", 128, B16), ("B256", 128, B16), ("BOF", 128, F), ("ID", 128, B16), ("NID", 128, B16), ("IDF", 128, F), ("SU", 128, B16),
+    ("rows", 2048, B16), ("col", 768, B16), ("HID", 128, B16), ("xb", 512, B16), ("md", 256, F), ("m0", 256, F), ("pw", 256, F), ("zer", 256, F), ("LVf", 32, F), ("LV", 32, U16),
+    ("wi", 256, I32), ("wj", 256, I32), ("who", 256, U16),
+    ("cmp", 4096, B16), ("G", 4096, B16), ("G4", 4096, B16), ("S4", 4096, B16), ("J", 8192, B16),
+    ("sq4", 256, F), ("i4a", 256, I32), ("i4b", 256, I32), ("c4", 256, F), ("o4", 256, U16),
+    ("V4", 256, F), ("V4s", 256, F), ("cn4", 16, F), ("V5", 256, B16),
+    ("cw", 256, U16), ("thr", 256, F), ("junk", 256, B16), ("acc", 16, F), ("O", 256, B16), ("I", 256, F), ("M", 256, F),
+    ("E0", 272, F), ("E1", 272, F), ("m2", 16, F), ("e2", 8, F), ("oc", 16, B16), ("L1", 512, B16), ("L2", 512, B16), ("L3", 512, B16),
+    ("of1", 32, U16), ("of2", 32, U16), ("ca", 32, F), ("cb", 32, F), ("cc", 32, F), ("cd", 32, F), ("corr", 32, F),
+    ("o", 32, U16), ("o2", 64, U16), ("ofb", 32, F), ("d2", 1024, F), ("V", 1024, F), ("oj", 512, U16), ("dT", 512, F), ("y", 512, B16),
+    ("key", 1024, F), ("ki", 64, I32), ("ob", 32, U16), ("cn", 32, F), ("HL", 64, B16), ("crow", 512, B16),
+    ("sm", 512, I32), ("nx", 512, I32), ("dm", 512, F), ("left", 512, F),
+    ("agw", 32, F), ("h", 128, F), ("w1", 16, U16), ("w2", 16, U16), ("gC", 256, B16), ("oc32", 272, F), ("oa32", 272, F),
+]:
+    SCRATCH[_n] = ("sbuf", [128, _c], _d)
+for _k in range(8):
+    SCRATCH["P%d" % _k] = ("psum", [128, 512], F)
+NDMA = 24
+SEMAPHORES = ["qV", "qA", "qP", "qG", "arr0", "arr1", "sent"] + ["dma%d" % _k for _k in range(NDMA)]
+
+CY, PCY, LAT = 0.001, 0.0005, 0.08
+GATH, SCAT = 1.5, 3.5
+SEED, ROUNDS, TEMP = 1, 6000, 0.2
+
+
+def sends(T, topo, core):
+    others = [r for r in range(N) if T.cores[r] != core]
+    me = T.rank_of(core)
+    others.sort(key=lambda r: (r - me) % N)
+    near = [r for r in others if topo.chip(T.cores[r]) == topo.chip(core)]
+    far = [r for r in others if r not in near]
+    fe = topo.engines(core, T.cores[far[0]])
+    calls = [[], []]
+    a, b = len(fe) // 4, len(fe) // 2
+    for i, r in enumerate(far[:4]):
+        calls[0].append((r, sum(1 << e for e in fe[a * i:a * i + a])))
+    for i, r in enumerate(far[4:]):
+        calls[1].append((r, sum(1 << e for e in fe[b * i:b * i + b])))
+    for r in near:
+        calls[0].append((r, sum(1 << e for e in topo.engines(core, T.cores[r]) if e not in fe)))
+    return calls
+
+
+def bits(m):
+    return bin(m).count("1")
+
+
+def program(rank):
+    ops = []
+
+    def r_(b, a=0, e=None, st=1, p=None):
+        return (b, a, SCRATCH[b][1][1] if e is None else e, st, p, None)
+
+    def ind(b, a, e, ob, oa, oe):
+        return (b, a, e, 1, None, (ob, oa, oe))
+
+    def cnt(x):
+        return 16 * (x[5][2] - x[5][1]) if x[5] else (x[2] - x[1] + x[3] - 1) // x[3]
+
+    def two(x):
+        return SCRATCH[x[0]][2] in (B16, U16)
+
+    def add(q, name, args, kw, reads, writes, dur, **more):
+        rd, wr = [], []
+        for x in reads:
+            if isinstance(x, tuple):
+                rd.append(x[:3])
+                if x[5]: rd.append(x[5])
+        for x in writes:
+            wr.append(x[:3])
+            if x[5]: rd.append(x[5])
+        d = {"q": q, "calls": [(name, args, kw)], "rd": rd, "wr": wr, "dur": dur, "lat": 0.0}
+        d.update(more)
+        ops.append(d)
+        return d
+
+    def vdur(out, ins, base):
+        if out[5]: return 0.06 + cnt(out) * SCAT * CY
+        if ins[0][5]: return 0.06 + cnt(out) * GATH * CY
+        return 0.03 + max(64, cnt(ins[0]) * base) * CY
+
+    def half(*xs):
+        return 0.5 if all(two(x) for x in xs) else 1.0
+
+    def cp(out, a): return add("V", "tensor_copy", [out, a], {}, [a], [out], vdur(out, [a], half(out, a)))
+    def tt(out, a, b, op, **m):
+        ps = a[0][0] == "P" and a[0][1:].isdigit() or b[0][0] == "P" and b[0][1:].isdigit()
+        return add("V", "tensor_tensor", [out, a, b, op], {}, [a, b], [out], vdur(out, [a], 1.0 if ps else 2.0), **m)
+    def ts(out, a, s1, op0, s2=None, op1=None):
+        return add("V", "tensor_scalar", [out, a, s1, s2, op0] + ([op1] if op1 is not None else []), {}, [a, s1, s2], [out], vdur(out, [a], half(out, a)))
+    def scan(out, a, b, op0, op1): return add("V", "tensor_tensor_scan", [out, a, b, 0.0, op0, op1], {}, [a, b], [out], vdur(out, [a], 1.0))
+    def trans(out, a): return add("V", "transpose", [out, a], {}, [a], [out], vdur(out, [a], half(out, a)))
+    def mset(out, v): return add("V", "memset", [out, v], {}, [], [out], vdur(out, [out], half(out)))
+    def red(out, a, op): return add("V", "tensor_reduce", [out, a, AX.X, op], {}, [a], [out], vdur(out, [a], 1.0))
+    def act(out, a, f, bias=0.0, scale=1.0, acc=None):
+        kw = {"bias": bias, "scale": scale}
+        if acc: kw["accum_out"] = acc
+        return add("A", "activation", [out, a, f], kw, [a, bias, scale], [out] + ([acc] if acc else []), 0.1 + cnt(out) * (GATH if a[5] else 1.0) * CY)
+    def iota(out, pat, base, cm):
+        kw = {} if SCRATCH[out[0]][2] == I32 else {"allow_small_or_imprecise_dtypes": True}
+        return add("G", "iota", [out, pat, base, cm], kw, [], [out], 0.15 + 2 * cnt(out) * CY)
+    def mm(items, first=True, last=True):
+        d = None
+        for i, (o, l, x) in enumerate(items):
+            dur = 0.005 + max(64, cnt(x)) * PCY * (4 if SCRATCH[x[0]][2] == F else 1)
+            call = ("matmul", [o, l, x, first and i == 0, last and i == len(items) - 1], {})
+            if d is None:
+                d = add("P", call[0], call[1], {}, [l, x], [o], dur)
+            else:
+                d["calls"].append(call); d["rd"] += [l[:3], x[:3]]; d["dur"] += dur
+        return d
+    def mm2(x, y):
+        mm([x], True, False); mm([y], False, True)
+    nd = [0]
+    def dma(q, out, a, us):
+        rd = [a] if a[0] in SCRATCH else []
+        wr = [out] if out[0] in SCRATCH else []
+        add(q, "dma_start", [out, a], {}, rd, wr, 0.1, lat=us, sem="dma%d" % nd[0]); nd[0] += 1
+    def ext(b, a, e): return (b, a, e, 1, None, None)
+    def Z(name, r, base=0): return r_(name, base + 15 - r, base + 143 - r)
+    def PS(k, a=0, e=512, st=1): return r_("P%d" % k, a, e, st)
+    def row(k, n): return r_("rows", 512 * k, 512 * k + n, 1, (0, 1, 1))
+    def colv(k): return r_("col", 128 * k, 128 * k + 128, 1, (0, 1, 1))
+    def wrap(bank, c0, zname, buf, a, n):
+        return [(PS(bank, c0, c0 + n // 16), Z(zname, r), r_(buf, a + r, a + n, 16)) for r in range(16)]
+    def wrap_rot(bank, buf, lo, rot):
+        cut = W - rot
+        mm([(PS(bank, 0, 256), colv(0), row(0, 256))], True, False)
+        cb = cut // 16
+        edges = sorted(set([0, cb + 1, 256] + [c for c in range(64, 256, 64) if abs(c - cb - 1) >= 32]))
+        parts = sorted(zip(edges[:-1], edges[1:]), key=lambda x: (16 * x[1] - 1 + rot) % W if x[1] != cb + 1 else W)
+        for n, (c1, c2) in enumerate(parts):
+            it = []
+            for r in range(16):
+                c0 = (cut - r + 15) // 16
+                for u, v, sh in ((c1, min(c2, c0), rot), (max(c1, c0), c2, -cut)):
+                    if u < v:
+                        a = OFF + lo + 16 * u + r + sh
+                        it.append((PS(bank, u, v), Z("Z1", r), r_(buf, a, a + 16 * (v - u - 1) + 1, 16)))
+            mm(it, False, n == len(parts) - 1)
+    cG, cR, cCo, cLV = r_("pc", 0, 1), r_("pc", 1, 2), r_("pc", 2, 3), r_("pc", 3, 4)
+
+    dma("A", r_("cm"), ext("come", 0, 768), 2.2)
+    for k in range(4):
+        dma("S" if k % 2 == 0 else "A", r_("X", OFF + 1024 * k, OFF + 1024 * k + 1024), ext("x0", 1024 * k, 1024 * k + 1024), 2.5 + 0.9 * k)
+    dma("S", r_("cdi", 0, 256), ext("cd0", 0, W), 6.0)
+    dma("S", r_("cdi", 256, 288), ext("age", 0, 512), 6.2)
+    dma("S", r_("dli"), ext("dl0", 0, 2048), 10.0)
+    iota(r_("pi", 0, 1), [[0, 1]], 0, 1)
+    iota(r_("ia", 0, 144), [[1, 144]], -15, 0)
+    ts(r_("pi", 1, 2), r_("pi", 0, 1), 15, ALU.bitwise_and)
+    ts(r_("pi", 2, 3), r_("pi", 0, 1), 112, ALU.bitwise_and)
+    ts(r_("pi", 3, 4), r_("pi", 0, 1), 16, ALU.bitwise_and)
+    cp(cR, r_("pi", 1, 2)); cp(cG, r_("pi", 2, 3)); cp(r_("pc", 4, 5), r_("pi", 3, 4))
+    def fill(out, v): iota(out, [[0, cnt(out)]], int(v), 0)
+    def scaled(out, a, w, b=0.0): act(out, a, AF.Identity, b, w)
+    ts(r_("Z1"), r_("ia", 0, 144), cG, ALU.is_equal)
+    for nme, w in (("Z16", 16.0), ("Z128", 128.0), ("Z256", 256.0), ("ZW", WK), ("ZH", WK / 2)):
+        scaled(r_(nme), r_("Z1"), w)
+    iota(r_("ic", 0, 32), [[16, 32]], 0, 0)
+    scaled(r_("kw"), r_("ic", 0, 32), 1.0, cR)
+    fill(r_("zer"), 0)
+    iota(r_("pw"), [[0, 16], [512, 16]], 0, 0)
+    ts(r_("pc", 5, 6), cR, 32.0, ALU.mult)
+    scaled(r_("pw"), r_("pw"), 1.0, r_("pc", 5, 6))
+    iota(r_("ib"), [[16, 8], [0, 16]], 0, 0)
+    ts(r_("BO"), r_("ib"), cG, ALU.is_equal)
+    for nme, w in (("B512", -512.0), ("B256", -256.0), ("BOF", 1.0)):
+        scaled(r_(nme), r_("BO"), w)
+    iota(r_("M", 0, 128), [[1, 128]], 0, -1)
+    ts(r_("ID"), r_("M", 0, 128), 0.0, ALU.is_equal)
+    for nme, w in (("NID", -1.0), ("IDF", 1.0)) + ((("HID", 0.5),) if NX_ACT else ()):
+        scaled(r_(nme), r_("ID"), w)
+    ts(r_("M", 128, 256), r_("M", 0, 128), 0.0, ALU.is_lt, -1.0, ALU.mult)
+    tt(r_("SU"), r_("M", 128, 256), r_("BOF"), ALU.mult)
+    one = (0, 32, 1)
+    mset(r_("rows", 0, 512, 1, one), 1.0)
+    fill(r_("rows", 512, 1024, 1, one), 8 * WK)
+    for m in range(0, 16, 2):
+        fill(r_("rows", 1024 + 32 * m, 1024 + 32 * m + 64, 1, one), 8 * WK if m in J_ACT else 0)
+    for k, v in enumerate((0.0, 1.0, 5376.0, 1280.0)):
+        mset(r_("col", 128 * k, 128 * k + 128, 1, one), v)
+    if NX_ACT: mset(r_("col", 640, 768, 1, one), -0.25)
+    for m in range(16):
+        fill(r_("col", 512 + m, 640, 16, one), 1 if m in J_ACT else 0)
+    scaled(r_("cmh", 0, 256), r_("cm", 0, 256), 0.5, -0.25)
+    fill(r_("X", 0, OFF), 0); fill(r_("XA", 0, OFF), -1)
+    scaled(cCo, cR, 61.0, 7.0)
+    iota(r_("ic"), [[0, 16], [1, 16]], 0, 0)
+    act(r_("m0"), r_("ic"), AF.Sign)
+    ts(r_("md"), r_("ic"), cR, ALU.is_equal)
+    iota(r_("kf"), [[1, 512]], 0, 0)
+    cp(r_("ku"), r_("kf"))
+    tt(cLV, r_("pc", 5, 6), r_("pc", 4, 5), ALU.add)
+    iota(r_("LVf"), [[1, 16], [512, 2]], 0, 0)
+    ts(r_("LV"), r_("LVf"), cLV, ALU.add)
+    for r in range(16):
+        act(r_("ZM", 144 * r, 144 * r + 144), r_("Z1"), AF.Identity, 0.0, r_("md", r, r + 1))
+    fill(r_("E0", 256, 272), BIG); fill(r_("E1", 256, 272), BIG); fill(r_("V5"), 0)
+    for k in range(4):
+        mset(r_("C", OFF + 1024 * k, OFF + 1024 * k + 1024), 0.0)
+    mset(r_("C", TW, TW + 512), 0.0)
+    fill(r_("C", 0, OFF), 0)
+    for k in range(3):
+        fill(r_("D", 864 * k, 864 * k + 864), 0)
+    ts(r_("cdf", 0, 256), r_("cdi", 0, 256), float(OFF), ALU.add)
+    cp(r_("cdf", 256, 288), r_("cdi", 256, 288))
+    scaled(r_("cdh"), r_("cdf"), 1.0)
+    tt(r_("cdl"), r_("cdf"), r_("cdh"), ALU.subtract)
+    for f, b in ((0, "cdh"), (1, "cdl")):
+        dma("S", r_("C", OFF, OFF + W, 1, (f, 128, 16)), r_(b, 0, 256), 2.5)
+        dma("S", r_("C", TW, TW + 512, 1, (f, 128, 16)), r_(b, 256, 288), 2.5)
+    for k in range(4):
+        ts(r_("D", OFF + 2048 + 512 * k, OFF + 2560 + 512 * k), r_("dli", 512 * k, 512 * k + 512), KD + OFF, ALU.add)
+    scaled(r_("cmh", 256, 768), r_("cm", 256, 768), 0.5, -0.25)
+
+    def who(t, pieces):
+        n = W // pieces
+        for k in range(pieces):
+            c0, c1 = k * n // 16, (k + 1) * n // 16
+            bank = 4 + k % 2
+            mm(wrap(bank, c0, "Z1", "X", OFF + S * t + k * n, n))
+            act(PS(bank, 256 + c0, 256 + c1), PS(bank, c0, c1), AF.Square)
+            tt(r_("wi", c0, c1), PS(bank, 256 + c0, 256 + c1), r_("pw", c0, c1), ALU.add)
+            ts(r_("wj", c0, c1), r_("wi", c0, c1), 5, ALU.arith_shift_right, 255, ALU.bitwise_and)
+            cp(r_("who", c0, c1), r_("wj", c0, c1))
+
+    def hop(bank, w0, wout, wu, t, k):
+        thr = r_("agw", 16 * t, 16 * t + 16)
+        f, d, e = r_("h", 48 * k, 48 * k + 16), r_("h", 48 * k + 16, 48 * k + 32), r_("h", 48 * k + 32, 48 * k + 48)
+        tt(f, PS(bank, 0, 16), thr, ALU.is_lt)
+        tt(d, w0, PS(bank, 0, 16), ALU.subtract)
+        tt(e, f, d, ALU.mult)
+        tt(wout, e, PS(bank, 0, 16), ALU.add)
+        cp(wu, wout)
+
+    who(0, 4)
+    mm(wrap(6, 0, "Z1", "C", TW, 512))
+    for t in range(R - 1):
+        ts(r_("agw", 16 * t, 16 * t + 16), PS(6, 16 * t, 16 * t + 16), -1.0, ALU.mult, float(W + S * t + 255 + OFF), ALU.add)
+
+    for t in range(R):
+        lo, B, rot = S * t, W + S * t, ST * (t + 1)
+        cut = W - rot
+        xa, xb = OFF + B, OFF + B + S
+        last = t == R - 1
+        wrap_rot(7, "C", lo, rot)
+        cp(r_("cw"), PS(7, 0, 256))
+        if t == 0:
+            cp(r_("xi"), r_("cmh", 0, 256))
+        else:
+            tt(r_("xi"), r_("cmh", S * t, S * t + S), r_("z%d" % (t - 1)), ALU.add, arr=t - 1)
+        cp(r_("X", xa, xb), r_("xi"))
+        act(r_("XA", xa, xb), r_("X", xa, xb), AF.Identity)
+        src = "X" if t == 0 else "XA"
+        na = 0
+        for k in range(8):
+            a = OFF + lo + 512 * k
+            gx = ind("X", xa, xb, "who", 32 * k, 32 * k + 32)
+            ch = r_("cmp", 512 * k, 512 * k + 512)
+            bank = k % 2
+            if k in S3_ACT:
+                gb = r_("G", 512 * k, 512 * k + 512); sb = 2 + na % 2; na += 1
+                act(gb, gx, AF.Identity)
+                mm2((PS(sb), r_("NID"), r_(src, a, a + 512)), (PS(sb), r_("ID"), gb))
+                act(ch, PS(sb), AF.Sign, 0.5)
+                mm2((PS(bank), colv(3), row(0, 512)), (PS(bank), r_("B256"), ch))
+            else:
+                tt(ch, gx, r_(src, a, a + 512), ALU.is_ge)
+                mm2((PS(bank), colv(2), row(0, 512)), (PS(bank), r_("B512"), ch))
+            tt(r_("XA", a, a + 512), PS(bank), r_(src, a, a + 512), ALU.min)
+        mm([(PS(7, 0, 256), r_("BO"), r_("X", xa, xb))])
+        act(r_("sq4"), PS(7, 0, 256), AF.Square)
+        act(PS(7, 256, 512), PS(7, 0, 256), AF.Identity, 0.0 if t == 0 else r_("acc", 7 + t, 8 + t), cCo)
+        ts(r_("i4b"), r_("sq4"), 1.0 / 32, ALU.mult, -0.375, ALU.add)
+        tt(r_("i4a"), PS(7, 256, 512), r_("i4b"), ALU.add)
+        ts(r_("i4b"), r_("i4a"), W - 1, ALU.bitwise_and)
+        cp(r_("o4"), r_("i4b"))
+        ts(r_("c4"), r_("i4b"), KD + OFF + lo, ALU.add)
+        wrap_rot(5, "XA", lo, rot)
+        act(r_("thr"), PS(5, 0, 256), AF.Identity, 2048.0, -1.0)
+        if not last:
+            act(r_("junk"), PS(5, 0, 256), AF.Sign, 0.5, 1.0, r_("acc", t, t + 1))
+        for k in range(4):
+            gx = ind("XA", 0, xa, "cw", 64 * k, 64 * k + 64)
+            ch = r_("cmp", 1024 * k, 1024 * k + 1024)
+            if k in P_ACT: act(ch, gx, AF.Sign, -128.0, -1.0)
+            else: ts(ch, gx, -128.0, ALU.is_lt, -0.5, ALU.add)
+        order = [0, 1, 2, 3]
+        mm([(PS(6, 0, 256), colv(0), row(0, 256))], True, False)
+        for k in order:
+            mm(wrap(6, 64 * k, "Z128" if k in P_ACT else "Z256", "cmp", 1024 * k, 1024), False, k == order[-1])
+        for k in range(8):
+            act(r_("G4", 512 * k, 512 * k + 512), ind("XA", OFF + lo, xa, "o4", 32 * k, 32 * k + 32), AF.Identity)
+        tt(r_("O"), PS(6, 0, 256), r_("thr"), ALU.is_ge)
+        mm([(PS(4, 0, 256), r_("BO"), r_("O"))])
+        mm([(PS(7, 0, 256), r_("SU"), r_("O"))])
+        scan(r_("I"), PS(4, 0, 256), r_("zer"), ALU.add, ALU.add)
+        tt(r_("m2"), r_("I", 15, 256, 16), r_("md", 0, 16), ALU.mult)
+        red(r_("e2", 0, 1), r_("m2"), ALU.max)
+        ts(r_("L1"), r_("ku"), r_("e2", 0, 1), ALU.is_ge)
+        mm(wrap(0, 0, "Z16", "L1", 0, 512))
+        tt(r_("M"), r_("I"), r_("md"), ALU.mult)
+        scan(r_("E1", 0, 256), r_("M"), r_("M"), ALU.max, ALU.max)
+        ts(r_("of1"), PS(0, 0, 32), 15.0, ALU.add)
+        tt(r_("E0", 0, 256), PS(7, 0, 256), r_("I"), ALU.add)
+        mm(wrap(1, 0, "Z16", "L1", 0, 512), True, False)
+        tt(r_("L2"), ind("E1", 0, 272, "of1", 0, 32), r_("kf"), ALU.is_le)
+        mm(wrap(1, 0, "Z1", "L2", 0, 512), False, True)
+        cp(r_("of2"), PS(1, 0, 32))
+        cbk, r0 = cut // 16, cut % 16
+        X0 = float(OFF + lo + rot)
+        ts(r_("e2", 1, 2), cR, float(r0), ALU.is_lt)
+        ts(r_("oc", 0, 1), r_("O", cbk, cbk + 1), r_("e2", 1, 2), ALU.mult)
+        mm([(PS(5, 0, 1), r_("BO"), r_("oc", 0, 1))])
+        tt(r_("e2", 2, 3), PS(5, 0, 1), r_("I", cbk - 1, cbk), ALU.add)
+        ts(r_("ca"), r_("kw"), r_("e2", 2, 3), ALU.is_ge, -float(W), ALU.mult)
+        ts(r_("cb"), r_("kw"), r_("I", 255, 256), ALU.is_ge)
+        ts(r_("cc"), r_("kw"), 16.0 - X0, ALU.add)
+        tt(r_("cd"), r_("cb"), r_("cc"), ALU.mult)
+        tt(r_("corr"), r_("ca"), r_("cd"), ALU.add)
+        mm(wrap(4, 0, "Z256", "L1", 0, 512), True, False)
+        mm(wrap(4, 0, "Z16", "L2", 0, 512), False, False)
+        mm([(PS(4, 0, 32), r_("IDF"), r_("corr"))], False, False)
+        tt(r_("L3"), ind("E0", 0, 272, "of2", 0, 32), r_("kf"), ALU.is_le)
+        mm(wrap(4, 0, "Z1", "L3", 0, 512), False, True)
+        ts(r_("o2", 0, 64, 2), PS(4, 0, 32), X0, ALU.add)
+        ts(r_("o2", 1, 64, 2), PS(4, 0, 32), X0, ALU.add)
+        ts(r_("o"), PS(4, 0, 32), X0, ALU.add)
+        ts(r_("ofb"), PS(4, 0, 32), X0 + 10 * WK, ALU.add)
+        if D2_ACT: act(r_("d2", 0, 512), ind("D", 0, xa, "o2", 0, 32), AF.Identity)
+        else: cp(r_("d2", 0, 512), ind("D", 0, xa, "o2", 0, 32))
+        act(r_("d2", 512, 1024), ind("D", 0, xa, "o2", 32, 64), AF.Identity)
+        act(r_("y"), ind("XA", 0, xa, "o", 0, 32), AF.Identity)
+        trans(r_("V", 0, 512), r_("d2", 0, 512))
+        trans(r_("V", 512, 1024), r_("d2", 512, 1024))
+        ts(r_("oj"), ind("V", 0, 1024, "LV", 0, 32), -KD, ALU.add, 0.0, ALU.max)
+        mm([(PS(7, 0, 256), colv(1), row(1, 256))], True, False)
+        for k in range(8):
+            sb = 5 + k % 2
+            it = []
+            for j in range(2):
+                it.append((PS(sb, 256 * j, 256 * j + 256), r_("NID"), r_("X", xa, xb)))
+                it.append((PS(sb, 256 * j, 256 * j + 256), r_("ID"), r_("G4", 2 * k + j, W, 16)))
+            mm(it[:2]); mm(it[2:])
+            act(r_("S4", 512 * k, 512 * k + 512), PS(sb), AF.Sign, 0.5)
+            mm([(PS(7, 0, 256), Z("ZH", 2 * k + j), r_("S4", 512 * k + 256 * j, 512 * k + 256 * j + 256)) for j in range(2)], False, k == 7)
+        tt(r_("D", xa, xb), PS(7, 0, 256), r_("c4"), ALU.min)
+        trans(r_("V4"), r_("D", xa, xb))
+        scan(r_("V4s"), r_("m0"), r_("V4"), ALU.mult, ALU.max)
+        ts(r_("cn4"), r_("V4s", 15, 256, 16), -KD, ALU.add, OFF - 1.0, ALU.max)
+        ts(r_("V5", 0, 256, 16), r_("V4s", 15, 256, 16), -KD, ALU.add, OFF - 1.0, ALU.max)
+        tt(r_("V5", 1, 256, 16), r_("cn4"), r_("V5", 0, 256, 16), ALU.subtract)
+        trans(r_("C", xa, xb), r_("V5"))
+        if not last:
+            mm(wrap(5, 0, "Z1", "C", xa, S))
+            ts(r_("h", 96, 112), r_("kw", 0, 16), float(xa), ALU.add)
+            hop(5, r_("h", 96, 112), r_("h", 112, 128), r_("w1"), t, 0)
+        act(r_("dT"), ind("V", 0, 1024, "LV", 0, 32), AF.Identity)
+        na = 0
+        for m0 in range(0, 16, 2):
+            kb, k0 = (0, 0) if m0 < J_CUT else (4, J_CUT)
+            if m0 == k0:
+                k1 = J_CUT if k0 == 0 else 16
+                mm([(PS(kb, 32 * k0, 32 * k1), colv(1), r_("rows", 1024 + 32 * k0, 1024 + 32 * k1, 1, (0, 1, 1)))], True, False)
+            for m in (m0, m0 + 1):
+                gx = ind("XA", 0, xa, "oj", 32 * m, 32 * m + 32)
+                ch = r_("J", 512 * m, 512 * m + 512)
+                if m in J_ACT:
+                    gb = r_("G", 512 * (na % 8), 512 * (na % 8) + 512); sb = 2 + na % 2; na += 1
+                    act(gb, gx, AF.Identity)
+                    mm2((PS(sb), r_("NID"), r_("y")), (PS(sb), r_("ID"), gb))
+                    act(ch, PS(sb), AF.Sign, 0.5)
+                else:
+                    tt(ch, gx, r_("y"), ALU.is_ge)
+            mm(wrap(kb, 32 * m0, "ZH" if m0 in J_ACT else "ZW", "J", 512 * m0, 1024), False, m0 + 2 == k1)
+        n2 = 32 * (16 - J_CUT)
+        tt(r_("key", 0, 512 - n2), PS(0, 0, 512 - n2), r_("dT", 0, 512 - n2), ALU.min)
+        a, n, nxt = 0, 512 - n2, 512
+        while n > 32:
+            h = 32 * (n // 64)
+            tt(r_("key", a + n - h, a + n), r_("key", a, a + h), r_("key", a + n - h, a + n), ALU.max)
+            a += h; n -= h
+        tt(r_("key", 960, 992), r_("key", a, a + 32), r_("ofb"), ALU.max)
+        tt(r_("key", 512, 512 + n2), PS(4, 512 - n2, 512), r_("dT", 512 - n2, 512), ALU.min)
+        a, n = 512, n2
+        while n > 32:
+            h = 32 * (n // 64)
+            tt(r_("key", a + n - h, a + n), r_("key", a, a + h), r_("key", a + n - h, a + n), ALU.max)
+            a += h; n -= h
+        kk = r_("ki", 0, 32)
+        tt(kk, r_("key", a, a + 32), r_("key", 960, 992), ALU.max)
+        ts(r_("ki", 32, 64), r_("ki", 0, 32), 8191, ALU.bitwise_and)
+        cp(r_("ob"), r_("ki", 32, 64))
+        ts(r_("HL", 0, 32), kk, -KD, ALU.add, OFF - 1.0, ALU.max)
+        ts(r_("cn"), kk, -KD, ALU.add, OFF - 1.0, ALU.max)
+        tt(r_("HL", 32, 64), r_("cn"), r_("HL", 0, 32), ALU.subtract)
+        mm([(PS(1), colv(0), row(0, 512))], True, False)
+        mm([(PS(1, r, 512, 16), Z("ZM", f, 144 * r), r_("HL", 32 * f, 32 * f + 32)) for f in range(2) for r in range(16)], False, True)
+        act(r_("crow"), PS(1), AF.Identity)
+        if NX_ACT:
+            act(r_("xb"), ind("XA", 0, xa, "ob", 0, 32), AF.Identity)
+            mm([(PS(3), colv(5), row(0, 512)), (PS(3), r_("HID"), r_("y"))], True, False)
+            mm([(PS(3), r_("HID"), r_("xb"))], False, True)
+            cp(r_("nx"), PS(3))
+        else:
+            tt(r_("sm"), ind("XA", 0, xa, "ob", 0, 32), r_("y"), ALU.add)
+            ts(r_("nx"), r_("sm"), 1, ALU.arith_shift_right)
+        cp(ind("X", 0, xa, "o", 0, 32), r_("nx"))
+        cp(ind("C", 0, xa, "o", 0, 32), r_("crow"))
+        if last:
+            dma("S", ext("yx", 0, W), r_("X", OFF + lo, xa), 6.0)
+            dma("A", ext("yx", W, W + S), r_("X", xa, xb), 2.5)
+            for b, bank, out, name in (("XA", 2, "oa32", "ya"), ("C", 3, "oc32", "yc")):
+                it = [(PS(bank, 0, 272), Z("Z1", s), r_(b, OFF + lo + 272 * s, OFF + lo + 272 * s + 272)) for s in range(16)]
+                mm(it[:8], True, False); mm(it[8:], False, True)
+                if b == "XA": ts(r_(out), PS(bank, 0, 272), 0.0, ALU.is_ge)
+                else: act(r_(out), PS(bank, 0, 272), AF.Identity, -float(OFF))
+                dma("A", ext(name, 0, W + S), r_(out), 2.5)
+            break
+        if Q_ACT: act(r_("gC"), ind("C", 0, xb, "w1", 0, 16), AF.Identity)
+        else: cp(r_("gC"), ind("C", 0, xb, "w1", 0, 16))
+        mm(wrap(6, 0, "Z1", "gC", 0, S))
+        hop(6, r_("h", 112, 128), r_("h", 96, 112), r_("w2"), t, 1)
+        zs, z = "zs%d" % t, "z%d" % t
+        if Q_ACT > 1: act(r_(zs), ind("X", 0, xb, "w2", 0, 16), AF.Identity, 0.0, 0.5)
+        else: ts(r_(zs), ind("X", 0, xb, "w2", 0, 16), 0.5, ALU.mult)
+        add("G", "send", [t], {}, [r_(zs)], [("snd", t, t + 1, 1, None, None)], 1.0, lat=5.0, nosem=True)
+        cp(r_(z, 32 * rank, 32 * rank + 32), r_(zs, 32 * rank, 32 * rank + 32))
+        who(t + 1, 2)
+        cp(ind("XA", 0, xa, "o", 0, 32), r_("nx"))
+        act(r_("dm"), ind("D", 0, xa, "o", 0, 32), AF.Identity)
+        it = [(PS(2), colv(4), row(1, 512))] + [(PS(2), Z("ZH" if m in J_ACT else "ZW", m), r_("J", 512 * m, 512 * m + 512)) for m in range(16)]
+        for k in range(0, 17, 3):
+            mm(it[k:k + 3], k == 0, k + 3 >= 17)
+        tt(r_("left"), PS(2), r_("dm"), ALU.min)
+        cp(ind("D", 0, xa, "o", 0, 32), r_("left"))
+        mm([(PS(3, 0, 1), r_("BOF"), r_("acc", t, t + 1))])
+        if t == 0:
+            act(r_("junk"), r_("XA", OFF, OFF + S), AF.Sign, 0.5, 1.0, r_("acc", 2, 3))
+            ts(r_("acc", 8, 9), PS(3, 0, 1), -0.5, ALU.mult, 2048.0, ALU.add)
+            tt(r_("acc", 3, 4), PS(3, 0, 1), r_("acc", 2, 3), ALU.subtract)
+        else:
+            tt(r_("acc", 4, 5), r_("acc", 3, 4), PS(3, 0, 1), ALU.subtract)
+            ts(r_("acc", 9, 10), r_("acc", 4, 5), 0.5, ALU.mult, 128.0, ALU.add)
+        mset(r_("XA", OFF + lo, OFF + lo + S), -256.0)
+    return ops
+
+
+def is_psum(b):
+    return b in SCRATCH and SCRATCH[b][0] == "psum"
+
+
+def schedule(ops):
+    seen = {}
+    for i, o in enumerate(ops):
+        o["i"] = i
+        dep = {}
+        if "arr" in o:
+            for p in ops[:i]:
+                if p["calls"][0][0] == "send" and p["calls"][0][1][0] == o["arr"]: dep[p["i"]] = False
+        for acc, w in [(x, False) for x in o["rd"]] + [(x, True) for x in o["wr"]]:
+            b, a, e = acc
+            ps = is_psum(b)
+            for (a2, e2, j, w2) in seen.get(b, []):
+                if j == i: continue
+                p = ops[j]
+                dmaish = "sem" in p or "sem" in o
+                same = p["q"] == o["q"] and not dmaish
+                if ps:
+                    if same and not (w or w2): continue
+                elif a2 >= e or a >= e2 or not (w or w2): continue
+                need = (not same) or (o["q"] != "P" and ((w2 and not w) or SAME_QUEUE_WAW))
+                dep[j] = dep.get(j, False) or need
+        for acc, w in [(x, False) for x in o["rd"]] + [(x, True) for x in o["wr"]]:
+            b, a, e = acc
+            lst = seen.setdefault(b, [])
+            if w: lst[:] = [x for x in lst if not (is_psum(b) or (a <= x[0] and x[1] <= e)) or x[2] == i]
+            lst.append((a, e, i, w))
+        o["dep"] = dep
+    if "t0" not in KEPT:
+        KEPT["t0"] = best_times(ops)
+    for o in ops: o["t0"] = KEPT["t0"][o["i"]]
+    return sorted(ops, key=lambda o: (o["t0"], o["i"]))
+
+
+KEPT = {}
+
+
+def place(seq, before, q, dur):
+    t, busy = {}, {}
+    for i in seq:
+        t0 = 0.0
+        for j, gap in before[i]:
+            if t[j] + gap > t0: t0 = t[j] + gap
+        iv = busy.setdefault(q[i], [])
+        lo, hi = 0, len(iv)
+        while lo < hi:
+            mid = (lo + hi) // 2
+            if iv[mid][1] <= t0: lo = mid + 1
+            else: hi = mid
+        k = lo
+        while k < len(iv) and iv[k][0] < t0 + dur[i] - 1e-9:
+            t0 = max(t0, iv[k][1]); k += 1
+        iv.insert(k, (t0, t0 + dur[i]))
+        t[i] = t0
+    return t
+
+
+def best_times(ops):
+    n = len(ops)
+    q = [o["q"] for o in ops]; dur = [o["dur"] for o in ops]; lat = [o["lat"] for o in ops]
+    fw = [[] for _ in ops]; bw = [[] for _ in ops]
+    for o in ops:
+        for j, need in o["dep"].items():
+            extra = lat[j] + (LAT if need else 0.0)
+            fw[o["i"]].append((j, dur[j] + extra)); bw[j].append((o["i"], dur[o["i"]] + extra))
+    bw0 = [bw[i] + [(-1, lat[i])] for i in range(n)]
+    bl = [dur[i] + lat[i] for i in range(n)]
+    for i in reversed(range(n)):
+        for j, gap in fw[i]: bl[j] = max(bl[j], gap + bl[i])
+    rng = np.random.RandomState(SEED)
+    best, bt, key = 1e9, None, [-x for x in bl]
+    for it in range(ROUNDS):
+        k2 = list(key)
+        for i in range(n):
+            for j, gap in fw[i]:
+                if k2[j] + 1e-6 > k2[i]: k2[i] = k2[j] + 1e-6
+        t = place(sorted(range(n), key=lambda i: k2[i]), fw, q, dur)
+        span = max(t[i] + dur[i] + lat[i] for i in range(n))
+        if span < best: best, bt = span, t
+        if it == 0 or span < cur + TEMP * (1.0 - it / ROUNDS) * rng.rand():
+            cur, ct = span, t
+            tb = place([-1] + sorted(range(n), key=lambda i: (-(ct[i] + dur[i]), -i)), bw0 + [[]], q + ["-"], dur + [0.0])
+            late = [cur - (tb[i] + dur[i]) for i in range(n)]
+        a, w, amp, mix = rng.rand() * cur, 2.0 + 12.0 * rng.rand(), 4.0 * rng.rand(), float(rng.choice([0.0, 0.5, 1.0]))
+        noise = rng.rand(n) * amp
+        key = [(mix * late[i] + (1 - mix) * ct[i] + float(noise[i])) if a - w <= ct[i] <= a else ct[i] for i in range(n)]
+    return bt
+
+
+def plan(rank):
+    ops = program(rank)
+    order = schedule(ops)
+    pos, n = {}, {}
+    for o in order:
+        n[o["q"]] = n.get(o["q"], 0) + 1
+        o["pos"] = n[o["q"]]
+    clock = {q: {} for q in "VAPGS"}
+    for o in order:
+        ck = clock[o["q"]]
+        want = {}
+        for j, need in o["dep"].items():
+            if need:
+                p = ops[j]
+                key = p.get("sem", p["q"])
+                want[key] = max(want.get(key, (0, None)), (p["pos"], j))
+        o["waits"] = []
+        for key, (v, j) in sorted(want.items(), key=lambda x: -ops[x[1][1]]["t0"]):
+            if ck.get(key, 0) >= v: continue
+            o["waits"].append(j); ops[j]["inc"] = True
+            ck[key] = v
+            for k2, v2 in ops[j]["ck"].items(): ck[k2] = max(ck.get(k2, 0), v2)
+        o["ck"] = dict(ck)
+    tot = {}
+    for o in order:
+        if "sem" in o: o["val"] = 16
+        elif o.get("inc"):
+            tot[o["q"]] = tot.get(o["q"], 0) + 1
+            o["val"] = tot[o["q"]]
+    return ops, order, tot
+
+
+def rank_program(g, core, T, topo):
+    rank = T.rank_of(core)
+    if rank is None:
+        return
+    ops, order, tot = plan(rank)
+    eng = {"V": g.vector, "A": g.scalar, "P": g.tensor, "G": g, "S": g.sync}
+    calls = sends(T, topo, core)
+    coming = sum(bits(m) for r in range(N) if r != rank for c in sends(T, topo, T.cores[r]) for d, m in c if d == rank)
+    going = sum(bits(m) for c in calls for d, m in c)
+
+    def ap(x):
+        if not isinstance(x, tuple): return x
+        b, a, e, st, p, off = x
+        cols = slice(a, e, st) if st != 1 else slice(a, e)
+        if p is None: v = T[b][:, cols]
+        else: v = T[b][slice(p[0], p[1], p[2]) if p[2] != 1 else slice(p[0], p[1]), cols]
+        return v.indirect(T[off[0]][:, off[1]:off[2]]) if off else v
+
+    def sem_of(o):
+        return T.sem[o["sem"]] if "sem" in o else T.sem["q" + o["q"]]
+
+    for o in order:
+        e = eng[o["q"]]
+        for j in o["waits"]:
+            e.wait_ge(sem_of(ops[j]), ops[j]["val"])
+        if "arr" in o:
+            e.wait_ge(T.sem["arr%d" % o["arr"]], coming)
+        if o["calls"][0][0] == "send":
+            t = o["calls"][0][1][0]
+            for c in calls:
+                tr = []
+                for d, m in c:
+                    rid, pid = topo.addr(T.cores[d])[:2]
+                    tr.append(RemoteDMATransfer(dst_ids=[DstId(rid=rid, pnc=pid)], dma_engine_mask=m, remote_sem=T.sem["arr%d" % t],
+                                                src=T["zs%d" % t][:, 32 * d:32 * d + 32], dst=T["z%d" % t][:, 32 * rank:32 * rank + 32]))
+                g.remote_dma_fused(tr, local_sem=T.sem.sent)
+            continue
+        ins = None
+        for name, args, kw in o["calls"]:
+            a = [ap(x) for x in args]
+            k = {key: ap(x) for key, x in kw.items()}
+            if name == "tensor_copy": ins = e.tensor_copy(*a)
+            elif name == "tensor_tensor": ins = e.tensor_tensor(*a)
+            elif name == "tensor_scalar": ins = e.tensor_scalar(*a)
+            elif name == "tensor_tensor_scan": ins = e.tensor_tensor_scan(*a)
+            elif name == "tensor_reduce": ins = e.tensor_reduce(*a)
+            elif name == "transpose": ins = e.transpose(*a)
+            elif name == "memset": ins = e.memset(*a)
+            elif name == "activation": ins = e.activation(*a, **k)
+            elif name == "iota": ins = e.iota(*a, **k)
+            elif name == "matmul": ins = e.matmul(*a)
+            elif name == "dma_start": ins = e.dma_start(*a)
+        if "sem" in o: ins.then_inc(sem_of(o), 16)
+        elif o.get("inc"): ins.then_inc(sem_of(o), 1)
+    for q, v in tot.items():
+        g.wait_ge(T.sem["q" + q], v)
+    g.wait_ge(T.sem.sent, going * (R - 1))
+    for o in order:
+        if "sem" in o: g.wait_ge(sem_of(o), 16)

@@ -5,36 +5,36 @@ from concourse.mybir import AluOpType as ALU, AxisListType as AX, ActivationFunc
 W, S, R, CAP, ST, N = 4096, 256, 3, 512, 683, 8
 OFF = 544
 TW = OFF + W + R * S
-WK = 16384.0
-KD = 10 * WK + 8192.0
+NONE = OFF - 1.0
+MAGIC = 3 * 2 ** 22
 BIG = 100000.0
-S3_ACT = (1, 3, 5, 7)
-P_ACT = (1, 3)
-J_ACT = (4, 5, 10, 11)
-J_CUT = 12
-D2_ACT, NX_ACT, Q_ACT = False, True, 1
+NS = 544
+S3_ACT = (6,)
+UPD_V = (4, 6, 7)
+PAR_V = (5, 7)
+J_ACT = ((7,), (0, 3, 6))
+DW_ACT, DM_ACT, Q_ACT, HI_ACT = True, (False, True), 1, True
 SAME_QUEUE_WAW = True
 
 F, B16, I32, U16 = "float32", "bfloat16", "int32", "uint16"
 SCRATCH = {}
 for _n, _c, _d in [
-    ("X", TW, B16), ("XA", TW, B16), ("C", TW + 512, B16), ("D", TW, F),
-    ("cm", 768, B16), ("cmh", 768, F), ("xi", 256, I32), ("z0", 256, B16), ("z1", 256, B16), ("zs0", 256, B16), ("zs1", 256, B16),
-    ("dli", 2048, I32), ("cdi", 288, I32), ("cdf", 288, F), ("cdh", 288, B16), ("cdl", 288, B16),
-    ("pi", 8, I32), ("pc", 16, F), ("ia", 256, F), ("ib", 128, F), ("ic", 256, F), ("kf", 512, F), ("ku", 512, U16), ("kw", 32, F),
-    ("Z1", 144, B16), ("Z16", 144, B16), ("Z128", 144, B16), ("Z256", 144, B16), ("ZW", 144, B16), ("ZH", 144, B16), ("ZM", 16 * 144, B16),
-    ("BO", 128, B16), ("B512", 128, B16), ("B256", 128, B16), ("BOF", 128, F), ("ID", 128, B16), ("NID", 128, B16), ("IDF", 128, F), ("SU", 128, B16),
-    ("rows", 2048, B16), ("col", 768, B16), ("HID", 128, B16), ("xb", 512, B16), ("md", 256, F), ("m0", 256, F), ("pw", 256, F), ("zer", 256, F), ("LVf", 32, F), ("LV", 32, U16),
+    ("X", TW, B16), ("XA", TW, B16), ("C", TW + 512, B16), ("D", TW, F), ("DW", 304, B16),
+    ("cm", 768, B16), ("z0", 256, B16), ("z1", 256, B16), ("zs0", 256, B16), ("zs1", 256, B16),
+    ("dli", 2048, I32), ("cdi", 288, I32), ("cdf", 304, F), ("cdh", 304, B16), ("cdl", 304, B16),
+    ("pi", 16, I32), ("pc", 24, F), ("ia", 256, F), ("ib", 128, F), ("ic", 256, F), ("kf", NS, F), ("ku", NS, U16), ("kw", 48, F),
+    ("Z1", 144, B16), ("ZC", 144, B16), ("ZB", 144, B16), ("BH", 8, B16), ("N8K", 128, B16), ("HID", 128, B16), ("Rl", 768, B16), ("xb", 512, B16), ("nx", 512, B16), ("Ui", 2048, B16), ("U", 2048, B16),
+    ("BO", 128, B16), ("BOF", 128, F), ("ID", 128, B16), ("NID", 128, B16), ("ID32", 128, B16), ("IDF", 128, F), ("SU", 128, B16),
+    ("rows", 768, B16), ("col", 384, B16), ("mdB", 256, F), ("m0", 256, F), ("pw", 256, F), ("zer", 272, F), ("LVf", 16, F), ("LV", 32, U16),
     ("wi", 256, I32), ("wj", 256, I32), ("who", 256, U16),
-    ("cmp", 4096, B16), ("G", 4096, B16), ("G4", 4096, B16), ("S4", 4096, B16), ("J", 8192, B16),
+    ("cmp", 4096, B16), ("par", 4096, B16), ("G", 4096, B16), ("G4", 4096, B16), ("S4", 4096, B16), ("J", 8192, B16),
     ("sq4", 256, F), ("i4a", 256, I32), ("i4b", 256, I32), ("c4", 256, F), ("o4", 256, U16),
-    ("V4", 256, F), ("V4s", 256, F), ("cn4", 16, F), ("V5", 256, B16),
-    ("cw", 256, U16), ("thr", 256, F), ("junk", 256, B16), ("acc", 16, F), ("O", 256, B16), ("I", 256, F), ("M", 256, F),
-    ("E0", 272, F), ("E1", 272, F), ("m2", 16, F), ("e2", 8, F), ("oc", 16, B16), ("L1", 512, B16), ("L2", 512, B16), ("L3", 512, B16),
-    ("of1", 32, U16), ("of2", 32, U16), ("ca", 32, F), ("cb", 32, F), ("cc", 32, F), ("cd", 32, F), ("corr", 32, F),
-    ("o", 32, U16), ("o2", 64, U16), ("ofb", 32, F), ("d2", 1024, F), ("V", 1024, F), ("oj", 512, U16), ("dT", 512, F), ("y", 512, B16),
-    ("key", 1024, F), ("ki", 64, I32), ("ob", 32, U16), ("cn", 32, F), ("HL", 64, B16), ("crow", 512, B16),
-    ("sm", 512, I32), ("nx", 512, I32), ("dm", 512, F), ("left", 512, F),
+    ("V4s", 768, F), ("cn", 48, F), ("V5", 768, B16), ("crow", 512, B16),
+    ("cw", 256, U16), ("junk", 256, B16), ("acc", 16, F), ("O", 272, B16), ("I", 272, F), ("M", 256, F),
+    ("E0", 272, F), ("E1", 272, F), ("e2", 16, F), ("L1", NS, B16), ("L2", NS, B16), ("L3", NS, B16), ("lb", 96, B16),
+    ("of1", 48, U16), ("of2", 48, U16), ("ca", 48, F), ("cb", 48, F), ("cc", 48, F), ("cd", 48, F), ("corr", 48, F),
+    ("o", 48, U16), ("ofl", 48, F), ("dm", 560, F), ("V", 1024, F), ("oj", 512, U16), ("y", 1024, B16),
+    ("obf", 32, F), ("ob", 32, U16), ("left", 512, F),
     ("agw", 32, F), ("h", 128, F), ("w1", 16, U16), ("w2", 16, U16), ("gC", 256, B16), ("oc32", 272, F), ("oa32", 272, F),
 ]:
     SCRATCH[_n] = ("sbuf", [128, _c], _d)
@@ -43,8 +43,8 @@ for _k in range(8):
 NDMA = 24
 SEMAPHORES = ["qV", "qA", "qP", "qG", "arr0", "arr1", "sent"] + ["dma%d" % _k for _k in range(NDMA)]
 
-CY, PCY, LAT = 0.001, 0.0005, 0.08
-GATH, SCAT = 1.5, 3.5
+CY, PCY, LAT = 0.00083, 0.00042, 0.1
+GATH, SCAT = 1.56, 3.8
 SEED, ROUNDS, TEMP = 1, 6000, 0.2
 
 
@@ -89,155 +89,162 @@ def program(rank):
         rd, wr = [], []
         for x in reads:
             if isinstance(x, tuple):
-                rd.append(x[:3])
-                if x[5]: rd.append(x[5])
+                rd.append(x[:4])
+                if x[5]: rd.append(x[5] + (1,))
         for x in writes:
-            wr.append(x[:3])
-            if x[5]: rd.append(x[5])
+            wr.append(x[:4])
+            if x[5]: rd.append(x[5] + (1,))
         d = {"q": q, "calls": [(name, args, kw)], "rd": rd, "wr": wr, "dur": dur, "lat": 0.0}
         d.update(more)
         ops.append(d)
         return d
 
     def vdur(out, ins, base):
-        if out[5]: return 0.06 + cnt(out) * SCAT * CY
-        if ins[0][5]: return 0.06 + cnt(out) * GATH * CY
-        return 0.03 + max(64, cnt(ins[0]) * base) * CY
+        if out[5]: return 0.05 + cnt(out) * SCAT * CY
+        if ins[0][5]: return 0.05 + cnt(out) * GATH * CY
+        return 0.01 + max(64, cnt(ins[0]) * base) * CY
 
     def half(*xs):
         return 0.5 if all(two(x) for x in xs) else 1.0
 
     def cp(out, a): return add("V", "tensor_copy", [out, a], {}, [a], [out], vdur(out, [a], half(out, a)))
     def tt(out, a, b, op, **m):
-        ps = a[0][0] == "P" and a[0][1:].isdigit() or b[0][0] == "P" and b[0][1:].isdigit()
-        return add("V", "tensor_tensor", [out, a, b, op], {}, [a, b], [out], vdur(out, [a], 1.0 if ps else 2.0), **m)
+        return add("V", "tensor_tensor", [out, a, b, op], {}, [a, b], [out], vdur(out, [a], 1.0 if is_psum(a[0]) or is_psum(b[0]) else 2.0), **m)
     def ts(out, a, s1, op0, s2=None, op1=None):
         return add("V", "tensor_scalar", [out, a, s1, s2, op0] + ([op1] if op1 is not None else []), {}, [a, s1, s2], [out], vdur(out, [a], half(out, a)))
     def scan(out, a, b, op0, op1): return add("V", "tensor_tensor_scan", [out, a, b, 0.0, op0, op1], {}, [a, b], [out], vdur(out, [a], 1.0))
     def trans(out, a): return add("V", "transpose", [out, a], {}, [a], [out], vdur(out, [a], half(out, a)))
     def mset(out, v): return add("V", "memset", [out, v], {}, [], [out], vdur(out, [out], half(out)))
-    def red(out, a, op): return add("V", "tensor_reduce", [out, a, AX.X, op], {}, [a], [out], vdur(out, [a], 1.0))
     def act(out, a, f, bias=0.0, scale=1.0, acc=None):
         kw = {"bias": bias, "scale": scale}
         if acc: kw["accum_out"] = acc
-        return add("A", "activation", [out, a, f], kw, [a, bias, scale], [out] + ([acc] if acc else []), 0.1 + cnt(out) * (GATH if a[5] else 1.0) * CY)
+        dur = 0.065 + cnt(out) * GATH * CY if a[5] else 0.01 + max(64, cnt(out)) * CY
+        return add("A", "activation", [out, a, f], kw, [a, bias, scale], [out] + ([acc] if acc else []), dur)
     def iota(out, pat, base, cm):
         kw = {} if SCRATCH[out[0]][2] == I32 else {"allow_small_or_imprecise_dtypes": True}
-        return add("G", "iota", [out, pat, base, cm], kw, [], [out], 0.15 + 2 * cnt(out) * CY)
+        return add("G", "iota", [out, pat, base, cm], kw, [], [out], 0.13 + 2 * cnt(out) * CY)
     def mm(items, first=True, last=True):
         d = None
         for i, (o, l, x) in enumerate(items):
-            dur = 0.005 + max(64, cnt(x)) * PCY * (4 if SCRATCH[x[0]][2] == F else 1)
+            dur = max(64, cnt(x)) * PCY * (4 if SCRATCH[x[0]][2] == F else 1)
             call = ("matmul", [o, l, x, first and i == 0, last and i == len(items) - 1], {})
             if d is None:
                 d = add("P", call[0], call[1], {}, [l, x], [o], dur)
             else:
-                d["calls"].append(call); d["rd"] += [l[:3], x[:3]]; d["dur"] += dur
+                d["calls"].append(call); d["rd"] += [l[:4], x[:4]]; d["dur"] += dur
         return d
     def mm2(x, y):
-        mm([x], True, False); mm([y], False, True)
+        mm(x, True, False); mm(y, False, True)
     nd = [0]
     def dma(q, out, a, us):
         rd = [a] if a[0] in SCRATCH else []
         wr = [out] if out[0] in SCRATCH else []
         add(q, "dma_start", [out, a], {}, rd, wr, 0.1, lat=us, sem="dma%d" % nd[0]); nd[0] += 1
     def ext(b, a, e): return (b, a, e, 1, None, None)
-    def Z(name, r, base=0): return r_(name, base + 15 - r, base + 143 - r)
+    def Z(name, r): return r_(name, 15 - r, 143 - r)
     def PS(k, a=0, e=512, st=1): return r_("P%d" % k, a, e, st)
-    def row(k, n): return r_("rows", 512 * k, 512 * k + n, 1, (0, 1, 1))
+    def row(k): return r_("rows", 256 * k, 256 * k + 256, 1, (0, 1, 1))
     def colv(k): return r_("col", 128 * k, 128 * k + 128, 1, (0, 1, 1))
     def wrap(bank, c0, zname, buf, a, n):
         return [(PS(bank, c0, c0 + n // 16), Z(zname, r), r_(buf, a + r, a + n, 16)) for r in range(16)]
-    def wrap_rot(bank, buf, lo, rot):
-        cut = W - rot
-        mm([(PS(bank, 0, 256), colv(0), row(0, 256))], True, False)
-        cb = cut // 16
-        edges = sorted(set([0, cb + 1, 256] + [c for c in range(64, 256, 64) if abs(c - cb - 1) >= 32]))
-        parts = sorted(zip(edges[:-1], edges[1:]), key=lambda x: (16 * x[1] - 1 + rot) % W if x[1] != cb + 1 else W)
-        for n, (c1, c2) in enumerate(parts):
-            it = []
-            for r in range(16):
-                c0 = (cut - r + 15) // 16
-                for u, v, sh in ((c1, min(c2, c0), rot), (max(c1, c0), c2, -cut)):
-                    if u < v:
-                        a = OFF + lo + 16 * u + r + sh
-                        it.append((PS(bank, u, v), Z("Z1", r), r_(buf, a, a + 16 * (v - u - 1) + 1, 16)))
-            mm(it, False, n == len(parts) - 1)
-    cG, cR, cCo, cLV = r_("pc", 0, 1), r_("pc", 1, 2), r_("pc", 2, 3), r_("pc", 3, 4)
+    def pcol(k): return r_("pc", k, k + 1)
+    def icol(k): return r_("pi", k, k + 1)
+    cG, cR, cCo = pcol(0), pcol(1), pcol(2)
 
     dma("A", r_("cm"), ext("come", 0, 768), 2.2)
-    for k in range(4):
-        dma("S" if k % 2 == 0 else "A", r_("X", OFF + 1024 * k, OFF + 1024 * k + 1024), ext("x0", 1024 * k, 1024 * k + 1024), 2.5 + 0.9 * k)
-    dma("S", r_("cdi", 0, 256), ext("cd0", 0, W), 6.0)
+    dma("S", r_("X", OFF, OFF + 1024), ext("x0", 0, 1024), 2.5)
+    dma("S", r_("cdi", 0, 256), ext("cd0", 0, W), 3.0)
+    for k in range(1, 4):
+        dma("S" if k % 2 == 0 else "A", r_("X", OFF + 1024 * k, OFF + 1024 * k + 1024), ext("x0", 1024 * k, 1024 * k + 1024), 2.8 + 0.9 * k)
     dma("S", r_("cdi", 256, 288), ext("age", 0, 512), 6.2)
     dma("S", r_("dli"), ext("dl0", 0, 2048), 10.0)
-    iota(r_("pi", 0, 1), [[0, 1]], 0, 1)
-    iota(r_("ia", 0, 144), [[1, 144]], -15, 0)
-    ts(r_("pi", 1, 2), r_("pi", 0, 1), 15, ALU.bitwise_and)
-    ts(r_("pi", 2, 3), r_("pi", 0, 1), 112, ALU.bitwise_and)
-    ts(r_("pi", 3, 4), r_("pi", 0, 1), 16, ALU.bitwise_and)
-    cp(cR, r_("pi", 1, 2)); cp(cG, r_("pi", 2, 3)); cp(r_("pc", 4, 5), r_("pi", 3, 4))
     def fill(out, v): iota(out, [[0, cnt(out)]], int(v), 0)
     def scaled(out, a, w, b=0.0): act(out, a, AF.Identity, b, w)
+    iota(icol(0), [[0, 1]], 0, 1)
+    iota(r_("ia", 0, 144), [[1, 144]], -15, 0)
+    ts(icol(1), icol(0), 15, ALU.bitwise_and)
+    ts(icol(2), icol(0), 112, ALU.bitwise_and)
+    ts(icol(3), icol(0), 16, ALU.bitwise_and)
+    cp(cR, icol(1)); cp(cG, icol(2))
     ts(r_("Z1"), r_("ia", 0, 144), cG, ALU.is_equal)
-    for nme, w in (("Z16", 16.0), ("Z128", 128.0), ("Z256", 256.0), ("ZW", WK), ("ZH", WK / 2)):
-        scaled(r_(nme), r_("Z1"), w)
-    iota(r_("ic", 0, 32), [[16, 32]], 0, 0)
-    scaled(r_("kw"), r_("ic", 0, 32), 1.0, cR)
-    fill(r_("zer"), 0)
     iota(r_("pw"), [[0, 16], [512, 16]], 0, 0)
-    ts(r_("pc", 5, 6), cR, 32.0, ALU.mult)
-    scaled(r_("pw"), r_("pw"), 1.0, r_("pc", 5, 6))
-    iota(r_("ib"), [[16, 8], [0, 16]], 0, 0)
-    ts(r_("BO"), r_("ib"), cG, ALU.is_equal)
-    for nme, w in (("B512", -512.0), ("B256", -256.0), ("BOF", 1.0)):
-        scaled(r_(nme), r_("BO"), w)
+    ts(pcol(5), cR, 32.0, ALU.mult)
+    scaled(r_("pw"), r_("pw"), 1.0, pcol(5))
+    one = (0, 32, 1)
+    fill(r_("rows", 0, 256, 1, one), 1)
+    mset(r_("col", 128, 256, 1, one), -0.25)
+    fill(r_("col", 256, 384, 1, one), MAGIC)
+    for k in range(4):
+        iota(r_("Ui", 512 * k, 512 * k + 512), [[-1, 4], [-16, 8], [0, 16]], -4 * k, 1)
+        ts(r_("U", 512 * k, 512 * k + 512), r_("Ui", 512 * k, 512 * k + 512), 0.0, ALU.is_equal, -512.0, ALU.mult)
     iota(r_("M", 0, 128), [[1, 128]], 0, -1)
     ts(r_("ID"), r_("M", 0, 128), 0.0, ALU.is_equal)
-    for nme, w in (("NID", -1.0), ("IDF", 1.0)) + ((("HID", 0.5),) if NX_ACT else ()):
+    for nme, w in (("HID", 0.5), ("NID", -1.0), ("ID32", 32.0), ("IDF", 1.0), ("N8K", -8192.0)):
         scaled(r_(nme), r_("ID"), w)
+    iota(r_("ib"), [[16, 8], [0, 16]], 0, 0)
+    ts(r_("BO"), r_("ib"), cG, ALU.is_equal)
+    scaled(r_("BOF"), r_("BO"), 1.0)
     ts(r_("M", 128, 256), r_("M", 0, 128), 0.0, ALU.is_lt, -1.0, ALU.mult)
     tt(r_("SU"), r_("M", 128, 256), r_("BOF"), ALU.mult)
-    one = (0, 32, 1)
-    mset(r_("rows", 0, 512, 1, one), 1.0)
-    fill(r_("rows", 512, 1024, 1, one), 8 * WK)
-    for m in range(0, 16, 2):
-        fill(r_("rows", 1024 + 32 * m, 1024 + 32 * m + 64, 1, one), 8 * WK if m in J_ACT else 0)
-    for k, v in enumerate((0.0, 1.0, 5376.0, 1280.0)):
-        mset(r_("col", 128 * k, 128 * k + 128, 1, one), v)
-    if NX_ACT: mset(r_("col", 640, 768, 1, one), -0.25)
-    for m in range(16):
-        fill(r_("col", 512 + m, 640, 16, one), 1 if m in J_ACT else 0)
-    scaled(r_("cmh", 0, 256), r_("cm", 0, 256), 0.5, -0.25)
-    fill(r_("X", 0, OFF), 0); fill(r_("XA", 0, OFF), -1)
+    iota(icol(4), [[0, 1]], 256, 16)
+    tt(icol(5), icol(4), icol(3), ALU.subtract)
+    ts(icol(6), icol(5), 255, ALU.bitwise_and)
+    ts(icol(7), icol(5), 16, ALU.bitwise_and)
+    ts(icol(8), icol(7), 16.0, ALU.mult)
+    tt(icol(9), icol(8), icol(3), ALU.add)
+    iota(r_("LVf"), [[1, 16]], 0, 0)
+    for hf, op in ((0, ALU.subtract), (1, ALU.add)):
+        tt(icol(10 + hf), icol(6), icol(7), op)
+        ts(icol(12 + hf), icol(10 + hf), 255, ALU.bitwise_and)
+        tt(pcol(6 + hf), icol(12 + hf), icol(9), ALU.add)
+        ts(r_("LV", 16 * hf, 16 * hf + 16), r_("LVf"), pcol(6 + hf), ALU.add)
+    ts(r_("cdf", 0, 256), r_("cdi", 0, 256), 1.0, ALU.add)
+    ts(r_("cdf", 256, 272), r_("cdi", 0, 16), 1.0, ALU.add)
+    trans(r_("V", 0, 256), r_("cdf", 0, 256))
+    trans(r_("V", 256, 512), r_("cdf", 16, 272))
+    ts(r_("cw"), ind("V", 0, 512, "LV", 0, 16), NONE, ALU.add)
+    fill(r_("XA", 0, OFF), -1)
+    fill(r_("DW", 256, 304), 0)
     scaled(cCo, cR, 61.0, 7.0)
+    for t in range(R):
+        r0 = float(ST * (t + 1) % 16)
+        ts(pcol(8 + 2 * t), cR, r0, ALU.is_ge)
+        ts(pcol(9 + 2 * t), cR, r0, ALU.is_lt)
+    fill(r_("zer"), 0)
     iota(r_("ic"), [[0, 16], [1, 16]], 0, 0)
     act(r_("m0"), r_("ic"), AF.Sign)
-    ts(r_("md"), r_("ic"), cR, ALU.is_equal)
-    iota(r_("kf"), [[1, 512]], 0, 0)
+    ts(r_("mdB"), r_("ic"), cR, ALU.is_equal, BIG, ALU.mult)
+    for a, e, b in ((0, 256, 0), (256, 272, 0), (272, 288, 496), (288, NS, 256)):
+        iota(r_("kf", a, e), [[1, e - a]], b, 0)
+        iota(r_("ia", 144 + a // 16, 144 + e // 16), [[16, (e - a) // 16]], b, 0)
     cp(r_("ku"), r_("kf"))
-    tt(cLV, r_("pc", 5, 6), r_("pc", 4, 5), ALU.add)
-    iota(r_("LVf"), [[1, 16], [512, 2]], 0, 0)
-    ts(r_("LV"), r_("LVf"), cLV, ALU.add)
-    for r in range(16):
-        act(r_("ZM", 144 * r, 144 * r + 144), r_("Z1"), AF.Identity, 0.0, r_("md", r, r + 1))
-    fill(r_("E0", 256, 272), BIG); fill(r_("E1", 256, 272), BIG); fill(r_("V5"), 0)
+    scaled(r_("kw", 0, NS // 16), r_("ia", 144, 144 + NS // 16), 1.0, cR)
+    fill(r_("E1", 256, 272), BIG); fill(r_("V5"), 0)
+    scaled(r_("BH"), r_("BO", 0, 128, 16), 0.5)
+    ts(pcol(14), cR, 2.0, ALU.is_lt)
+    ts(pcol(15), cR, 3.0, ALU.is_lt)
+    scaled(r_("ZC"), r_("Z1"), pcol(14))
+    scaled(r_("ZB"), r_("Z1"), pcol(15))
+    fill(r_("col", 0, 128, 1, one), 1); fill(r_("rows", 256, 768, 1, one), 0)
+    for hf in range(2):
+        for j in J_ACT[hf]:
+            for m in (2 * j, 2 * j + 1):
+                fill(r_("rows", 256 * (hf + 1) + m, 256 * (hf + 2), 16, one), 8)
     for k in range(4):
-        mset(r_("C", OFF + 1024 * k, OFF + 1024 * k + 1024), 0.0)
-    mset(r_("C", TW, TW + 512), 0.0)
+        fill(r_("C", OFF + 1024 * k, OFF + 1024 * k + 1024), 0)
+    fill(r_("C", TW, TW + 512), 0)
     fill(r_("C", 0, OFF), 0)
+    fill(r_("X", 0, OFF), 0)
     for k in range(3):
         fill(r_("D", 864 * k, 864 * k + 864), 0)
-    ts(r_("cdf", 0, 256), r_("cdi", 0, 256), float(OFF), ALU.add)
-    cp(r_("cdf", 256, 288), r_("cdi", 256, 288))
+    cp(r_("cdf", 272, 304), r_("cdi", 256, 288))
     scaled(r_("cdh"), r_("cdf"), 1.0)
     tt(r_("cdl"), r_("cdf"), r_("cdh"), ALU.subtract)
     for f, b in ((0, "cdh"), (1, "cdl")):
         dma("S", r_("C", OFF, OFF + W, 1, (f, 128, 16)), r_(b, 0, 256), 2.5)
-        dma("S", r_("C", TW, TW + 512, 1, (f, 128, 16)), r_(b, 256, 288), 2.5)
+        dma("S", r_("C", TW, TW + 512, 1, (f, 128, 16)), r_(b, 272, 304), 2.5)
     for k in range(4):
-        ts(r_("D", OFF + 2048 + 512 * k, OFF + 2560 + 512 * k), r_("dli", 512 * k, 512 * k + 512), KD + OFF, ALU.add)
-    scaled(r_("cmh", 256, 768), r_("cm", 256, 768), 0.5, -0.25)
+        ts(r_("D", OFF + 2048 + 512 * k, OFF + 2560 + 512 * k), r_("dli", 512 * k, 512 * k + 512), float(OFF), ALU.add)
 
     def who(t, pieces):
         n = W // pieces
@@ -252,48 +259,59 @@ def program(rank):
 
     def hop(bank, w0, wout, wu, t, k):
         thr = r_("agw", 16 * t, 16 * t + 16)
-        f, d, e = r_("h", 48 * k, 48 * k + 16), r_("h", 48 * k + 16, 48 * k + 32), r_("h", 48 * k + 32, 48 * k + 48)
+        f, e = r_("h", 32 * k, 32 * k + 16), r_("h", 32 * k + 16, 32 * k + 32)
         tt(f, PS(bank, 0, 16), thr, ALU.is_lt)
-        tt(d, w0, PS(bank, 0, 16), ALU.subtract)
-        tt(e, f, d, ALU.mult)
-        tt(wout, e, PS(bank, 0, 16), ALU.add)
-        cp(wu, wout)
+        tt(e, f, w0, ALU.mult)
+        tt(wout, PS(bank, 0, 16), e, ALU.max)
+        ts(wu, wout, NONE, ALU.add)
+
+    def count(bank, buf, a, m, signs):
+        w = r_("BH") if signs else r_("BO", 0, 128, 16)
+        return [(PS(bank, 128 * b + m, 128 * b + 128, 16), r_(buf, a + 128 * b, a + 128 * b + 128), w) for b in range(2)]
+
+    def turned(bank, buf, a, ident):
+        return [(PS(bank, 128 * b, 128 * b + 128), r_(buf, a + 128 * b, a + 128 * b + 128), r_(ident)) for b in range(2)]
+
+    def youngest(k, cb, need, kb, lists, a0, out):
+        a = 256 * k
+        top, cn = r_("V4s", a + 15, a + 256, 16), r_("cn", 16 * k, 16 * k + 16)
+        if kb != cb: mm(turned(kb, lists, a0, "IDF"), True, False)
+        act(r_("Rl", a, a + 256), PS(cb, 0, 256), AF.Relu, need, -1.0)
+        if kb == cb: mm(turned(kb, lists, a0, "IDF"), True, False)
+        mm([(PS(kb, 0, 256), r_("N8K"), r_("Rl", a, a + 256))], False, True)
+        scan(r_("V4s", a, a + 256), r_("m0"), PS(kb, 0, 256), ALU.mult, ALU.max)
+        if HI_ACT: act(r_("V5", a, a + 256, 16), top, AF.Relu, -NONE)
+        else: ts(r_("V5", a, a + 256, 16), top, -NONE, ALU.add, 0.0, ALU.max)
+        ts(cn, top, -NONE, ALU.add, 0.0, ALU.max)
+        if k: act(r_("V5", a + 2, a + 256, 16), top, AF.Relu, 8192.0 * OFF, -8192.0)
+        tt(r_("V5", a + 1, a + 256, 16), cn, r_("V5", a, a + 256, 16), ALU.subtract)
+        mm(turned(cb, "V5", a, "ID"))
+        act(out, PS(cb, 0, 256), AF.Identity)
+
+    def left(k, bank, lists, a0, out):
+        mm([(PS(bank, 0, 256), r_("IDF"), r_(lists, a0, a0 + 256))], True, False)
+        mm(turned(bank, "Rl", 256 * k, "N8K"), False, True)
+        act(out, PS(bank, 0, 256), AF.Identity)
+
+    def halved(bank, a, b, out, **more):
+        o = PS(bank, 0, 256)
+        mm([(o, r_("HID"), a), (o, colv(1), row(0))], True, False)
+        mm(([(o, r_("HID"), b)] if b else []) + [(o, colv(2), row(0))], False, True).update(more)
+        act(out, o, AF.Identity, -float(MAGIC))
 
     who(0, 4)
-    mm(wrap(6, 0, "Z1", "C", TW, 512))
+    mm(wrap(6, 0, "ZC", "C", TW, 512))
     for t in range(R - 1):
-        ts(r_("agw", 16 * t, 16 * t + 16), PS(6, 16 * t, 16 * t + 16), -1.0, ALU.mult, float(W + S * t + 255 + OFF), ALU.add)
+        scaled(r_("agw", 16 * t, 16 * t + 16), PS(6, 16 * t, 16 * t + 16), -1.0, float(W + S * t + 256))
 
     for t in range(R):
         lo, B, rot = S * t, W + S * t, ST * (t + 1)
-        cut = W - rot
         xa, xb = OFF + B, OFF + B + S
+        c0, d0 = rot // 16, lo // 16
         last = t == R - 1
-        wrap_rot(7, "C", lo, rot)
-        cp(r_("cw"), PS(7, 0, 256))
-        if t == 0:
-            cp(r_("xi"), r_("cmh", 0, 256))
-        else:
-            tt(r_("xi"), r_("cmh", S * t, S * t + S), r_("z%d" % (t - 1)), ALU.add, arr=t - 1)
-        cp(r_("X", xa, xb), r_("xi"))
-        act(r_("XA", xa, xb), r_("X", xa, xb), AF.Identity)
-        src = "X" if t == 0 else "XA"
-        na = 0
-        for k in range(8):
-            a = OFF + lo + 512 * k
-            gx = ind("X", xa, xb, "who", 32 * k, 32 * k + 32)
-            ch = r_("cmp", 512 * k, 512 * k + 512)
-            bank = k % 2
-            if k in S3_ACT:
-                gb = r_("G", 512 * k, 512 * k + 512); sb = 2 + na % 2; na += 1
-                act(gb, gx, AF.Identity)
-                mm2((PS(sb), r_("NID"), r_(src, a, a + 512)), (PS(sb), r_("ID"), gb))
-                act(ch, PS(sb), AF.Sign, 0.5)
-                mm2((PS(bank), colv(3), row(0, 512)), (PS(bank), r_("B256"), ch))
-            else:
-                tt(ch, gx, r_(src, a, a + 512), ALU.is_ge)
-                mm2((PS(bank), colv(2), row(0, 512)), (PS(bank), r_("B512"), ch))
-            tt(r_("XA", a, a + 512), PS(bank), r_(src, a, a + 512), ALU.min)
+        if t == 0: halved(0, r_("cm", 0, S), None, r_("X", xa, xb))
+        else: halved(0, r_("cm", S * t, S * t + S), r_("z%d" % (t - 1)), r_("X", xa, xb), arr=t - 1)
+        if last: act(r_("XA", xa, xb), r_("X", xa, xb), AF.Identity)
         mm([(PS(7, 0, 256), r_("BO"), r_("X", xa, xb))])
         act(r_("sq4"), PS(7, 0, 256), AF.Square)
         act(PS(7, 256, 512), PS(7, 0, 256), AF.Identity, 0.0 if t == 0 else r_("acc", 7 + t, 8 + t), cCo)
@@ -301,179 +319,180 @@ def program(rank):
         tt(r_("i4a"), PS(7, 256, 512), r_("i4b"), ALU.add)
         ts(r_("i4b"), r_("i4a"), W - 1, ALU.bitwise_and)
         cp(r_("o4"), r_("i4b"))
-        ts(r_("c4"), r_("i4b"), KD + OFF + lo, ALU.add)
-        wrap_rot(5, "XA", lo, rot)
-        act(r_("thr"), PS(5, 0, 256), AF.Identity, 2048.0, -1.0)
-        if not last:
-            act(r_("junk"), PS(5, 0, 256), AF.Sign, 0.5, 1.0, r_("acc", t, t + 1))
+        ts(r_("c4"), r_("i4b"), float(OFF + lo), ALU.add)
+        for n, k in enumerate(S3_ACT):
+            a, sb = OFF + lo + 512 * k, 5 + n % 2
+            gb = r_("G", 512 * k, 512 * k + 512)
+            act(gb, ind("X", xa, xb, "who", 32 * k, 32 * k + 32), AF.Identity)
+            mm2([(PS(sb), r_("NID"), r_("X", a, a + 512))], [(PS(sb), r_("ID"), gb)])
+            act(r_("cmp", 512 * k, 512 * k + 512), PS(sb), AF.Sign, 0.5)
+        def runs(k, other):
+            x, y = 2 * k in other, 2 * k + 1 in other
+            return [(2 * k, 2 * k + 2, x)] if x == y else [(2 * k, 2 * k + 1, x), (2 * k + 1, 2 * k + 2, y)]
         for k in range(4):
-            gx = ind("XA", 0, xa, "cw", 64 * k, 64 * k + 64)
-            ch = r_("cmp", 1024 * k, 1024 * k + 1024)
-            if k in P_ACT: act(ch, gx, AF.Sign, -128.0, -1.0)
-            else: ts(ch, gx, -128.0, ALU.is_lt, -0.5, ALU.add)
-        order = [0, 1, 2, 3]
-        mm([(PS(6, 0, 256), colv(0), row(0, 256))], True, False)
-        for k in order:
-            mm(wrap(6, 64 * k, "Z128" if k in P_ACT else "Z256", "cmp", 1024 * k, 1024), False, k == order[-1])
-        for k in range(8):
-            act(r_("G4", 512 * k, 512 * k + 512), ind("XA", OFF + lo, xa, "o4", 32 * k, 32 * k + 32), AF.Identity)
-        tt(r_("O"), PS(6, 0, 256), r_("thr"), ALU.is_ge)
-        mm([(PS(4, 0, 256), r_("BO"), r_("O"))])
-        mm([(PS(7, 0, 256), r_("SU"), r_("O"))])
-        scan(r_("I"), PS(4, 0, 256), r_("zer"), ALU.add, ALU.add)
-        tt(r_("m2"), r_("I", 15, 256, 16), r_("md", 0, 16), ALU.mult)
-        red(r_("e2", 0, 1), r_("m2"), ALU.max)
-        ts(r_("L1"), r_("ku"), r_("e2", 0, 1), ALU.is_ge)
-        mm(wrap(0, 0, "Z16", "L1", 0, 512))
-        tt(r_("M"), r_("I"), r_("md"), ALU.mult)
-        scan(r_("E1", 0, 256), r_("M"), r_("M"), ALU.max, ALU.max)
-        ts(r_("of1"), PS(0, 0, 32), 15.0, ALU.add)
-        tt(r_("E0", 0, 256), PS(7, 0, 256), r_("I"), ALU.add)
-        mm(wrap(1, 0, "Z16", "L1", 0, 512), True, False)
-        tt(r_("L2"), ind("E1", 0, 272, "of1", 0, 32), r_("kf"), ALU.is_le)
-        mm(wrap(1, 0, "Z1", "L2", 0, 512), False, True)
-        cp(r_("of2"), PS(1, 0, 32))
-        cbk, r0 = cut // 16, cut % 16
-        X0 = float(OFF + lo + rot)
-        ts(r_("e2", 1, 2), cR, float(r0), ALU.is_lt)
-        ts(r_("oc", 0, 1), r_("O", cbk, cbk + 1), r_("e2", 1, 2), ALU.mult)
-        mm([(PS(5, 0, 1), r_("BO"), r_("oc", 0, 1))])
-        tt(r_("e2", 2, 3), PS(5, 0, 1), r_("I", cbk - 1, cbk), ALU.add)
-        ts(r_("ca"), r_("kw"), r_("e2", 2, 3), ALU.is_ge, -float(W), ALU.mult)
-        ts(r_("cb"), r_("kw"), r_("I", 255, 256), ALU.is_ge)
-        ts(r_("cc"), r_("kw"), 16.0 - X0, ALU.add)
-        tt(r_("cd"), r_("cb"), r_("cc"), ALU.mult)
-        tt(r_("corr"), r_("ca"), r_("cd"), ALU.add)
-        mm(wrap(4, 0, "Z256", "L1", 0, 512), True, False)
-        mm(wrap(4, 0, "Z16", "L2", 0, 512), False, False)
-        mm([(PS(4, 0, 32), r_("IDF"), r_("corr"))], False, False)
-        tt(r_("L3"), ind("E0", 0, 272, "of2", 0, 32), r_("kf"), ALU.is_le)
-        mm(wrap(4, 0, "Z1", "L3", 0, 512), False, True)
-        ts(r_("o2", 0, 64, 2), PS(4, 0, 32), X0, ALU.add)
-        ts(r_("o2", 1, 64, 2), PS(4, 0, 32), X0, ALU.add)
-        ts(r_("o"), PS(4, 0, 32), X0, ALU.add)
-        ts(r_("ofb"), PS(4, 0, 32), X0 + 10 * WK, ALU.add)
-        if D2_ACT: act(r_("d2", 0, 512), ind("D", 0, xa, "o2", 0, 32), AF.Identity)
-        else: cp(r_("d2", 0, 512), ind("D", 0, xa, "o2", 0, 32))
-        act(r_("d2", 512, 1024), ind("D", 0, xa, "o2", 32, 64), AF.Identity)
-        act(r_("y"), ind("XA", 0, xa, "o", 0, 32), AF.Identity)
-        trans(r_("V", 0, 512), r_("d2", 0, 512))
-        trans(r_("V", 512, 1024), r_("d2", 512, 1024))
-        ts(r_("oj"), ind("V", 0, 1024, "LV", 0, 32), -KD, ALU.add, 0.0, ALU.max)
-        mm([(PS(7, 0, 256), colv(1), row(1, 256))], True, False)
+            a = OFF + lo + 1024 * k
+            dw = r_("DW", d0 + 64 * k, d0 + 64 * k + 64)
+            for u, v, on in runs(k, S3_ACT):
+                if not on:
+                    tt(r_("cmp", 512 * u, 512 * v), ind("X", xa, xb, "who", 32 * u, 32 * v), r_("X", OFF + lo + 512 * u, OFF + lo + 512 * v), ALU.is_ge)
+            bank = k % 2
+            if t == 0: mm(wrap(bank, 0, "Z1", "cmp", 1024 * k, 1024))
+            else: mm2([(PS(bank, 0, 64), r_("ID32"), dw)], wrap(bank, 0, "Z1", "cmp", 1024 * k, 1024))
+            for u, v, on in runs(k, S3_ACT):
+                src, dst = PS(bank, 32 * (u - 2 * k), 32 * (v - 2 * k)), r_("DW", d0 + 32 * u, d0 + 32 * v)
+                if DW_ACT: act(dst, src, AF.Relu, -5.0 if on else -10.0)
+                else: ts(dst, src, -5.0 if on else -10.0, ALU.add, 0.0, ALU.max)
+            for p in range(2):
+                ub = 2 + (2 * k + p) % 3
+                it = [(PS(ub, r // 2, 512, 8), r_("U", 128 * r, 128 * r + 128), dw) for r in range(p, 16, 2)]
+                xs, xo = r_("X", a + p, a + 1024, 2), r_("XA", a + p, a + 1024, 2)
+                if 2 * k + p in UPD_V:
+                    d = mm(it)
+                    d["calls"] = [(n, x[:3] + [True, True], kw) for n, x, kw in d["calls"]]
+                    tt(xo, PS(ub), xs, ALU.add)
+                else:
+                    mm2([(PS(ub), r_("ID"), xs)], it)
+                    act(xo, PS(ub), AF.Identity)
+            for u, v, on in runs(k, PAR_V):
+                gx, ch = ind("XA", 0, a + 1024, "cw", 32 * u, 32 * v), r_("par", 512 * u, 512 * v)
+                if on: ts(ch, gx, -128.0, ALU.is_ge, -0.5, ALU.add)
+                else: act(ch, gx, AF.Sign, 128.0)
+            bank = 5 + k % 2
+            mm2([(PS(bank, 0, 64), r_("ID32"), dw)], wrap(bank, 0, "Z1", "par", 1024 * k, 1024))
+            c1, c2 = 64 * k, 64 * k + 64
+            for u, v, sh in ((c1, min(c2, c0), 256 - c0), (max(c1, c0 + 1), c2, -c0)):
+                if u < v: ts(r_("O", u + sh, v + sh), PS(bank, u - c1, v - c1), 0.0, ALU.is_lt)
+            if c1 <= c0 < c2:
+                for q, col in ((0, 8 + 2 * t), (256, 9 + 2 * t)):
+                    ts(r_("O", q, q + 1), PS(bank, c0 - c1, c0 - c1 + 1), 0.0, ALU.is_lt, pcol(col), ALU.mult)
+        for k in range(4):
+            act(r_("G4", 1024 * k, 1024 * k + 1024), ind("XA", OFF + lo, xa, "o4", 64 * k, 64 * k + 64), AF.Identity)
+        if not last:
+            act(r_("junk"), r_("DW", d0, d0 + 256), AF.Sign, -0.5, 1.0, r_("acc", t, t + 1))
+            if t == 0: act(r_("junk", 0, 240), r_("DW", 16, 256), AF.Sign, -0.5, 1.0, r_("acc", 2, 3))
+        nc = NS // 16
+        mm([(PS(0, 0, 257), r_("BO"), r_("O", 0, 257))])
+        mm([(PS(1, 0, 257), r_("SU"), r_("O", 0, 257))])
+        scan(r_("I", 0, 257), PS(0, 0, 257), r_("zer", 0, 257), ALU.add, ALU.add)
+        scan(r_("e2"), r_("mdB", 0, 16), r_("I", 15, 256, 16), ALU.max, ALU.min)
+        ts(r_("L1"), r_("ku"), r_("e2", 15, 16), ALU.is_ge)
+        mm(wrap(2, 0, "Z1", "L1", 0, NS))
+        scan(r_("E1", 0, 256), r_("mdB"), r_("I", 0, 256), ALU.max, ALU.min)
+        ts(r_("of1", 0, nc), PS(2, 0, nc), 16.0, ALU.mult, 15.0, ALU.add)
+        scaled(r_("lb", 0, nc), PS(2, 0, nc), 16.0)
+        tt(r_("E0", 0, 257), PS(1, 0, 257), r_("I", 0, 257), ALU.add)
+        tt(r_("L2"), ind("E1", 0, 272, "of1", 0, nc), r_("kf"), ALU.is_le)
+        mm2([(PS(3, 0, nc), r_("ID"), r_("lb", 0, nc))], wrap(3, 0, "Z1", "L2", 0, NS))
+        cp(r_("of2", 0, nc), PS(3, 0, nc))
+        scaled(r_("lb", 48, 48 + nc), PS(3, 0, nc), 16.0)
+        X0 = float(OFF + lo + 16 * c0)
+        ts(r_("ca", 0, nc), r_("kw", 0, nc), r_("I", 255 - c0, 256 - c0), ALU.is_ge, -float(W), ALU.mult)
+        ts(r_("cb", 0, nc), r_("kw", 0, nc), r_("I", 256, 257), ALU.is_ge)
+        scaled(r_("cc", 0, nc), r_("kw", 0, nc), 1.0, -X0)
+        tt(r_("cd", 0, nc), r_("cb", 0, nc), r_("cc", 0, nc), ALU.mult)
+        tt(r_("corr", 0, nc), r_("ca", 0, nc), r_("cd", 0, nc), ALU.add)
+        tt(r_("L3"), ind("E0", 0, 257, "of2", 0, nc), r_("kf"), ALU.is_le)
+        mm([(PS(4, 0, nc), r_("IDF"), r_("corr", 0, nc))], True, False)
+        mm([(PS(4, 0, nc), r_("ID"), r_("lb", 48, 48 + nc))], False, False)
+        mm(wrap(4, 0, "Z1", "L3", 0, NS), False, True)
+        ts(r_("o", 0, nc), PS(4, 0, nc), X0, ALU.add)
+        scaled(r_("ofl", 0, nc), PS(4, 0, nc), 1.0, X0 - NONE)
+        if last:
+            it = [(PS(1, 0, 272), Z("Z1", s), r_("XA", OFF + lo + 272 * s, OFF + lo + 272 * s + 272)) for s in range(16)]
+            mm2(it[:8], it[8:])
+            ts(r_("oa32"), PS(1, 0, 272), 0.0, ALU.is_ge)
+            dma("A", ext("ya", 0, W + S), r_("oa32"), 2.5)
+            dma("A", ext("yx", W, W + S), r_("X", xa, xb), 2.5)
+        HALF = ((0, 17, 0, 0, 16, 0), (16, 34, 272, 304, 288, 18))
+        for hf, (oa, oe, at, main, moved, om) in enumerate(HALF):
+            out, gx = r_("dm", at, at + 16 * (oe - oa)), ind("D", 0, xa, "o", oa, oe)
+            if DM_ACT[hf]: act(out, gx, AF.Identity)
+            else: cp(out, gx)
+            trans(r_("V", 512 * hf, 512 * hf + 256), r_("dm", main, main + 256))
+            trans(r_("V", 512 * hf + 256, 512 * hf + 512), r_("dm", moved, moved + 256))
+            ts(r_("oj", 256 * hf, 256 * hf + 256), ind("V", 512 * hf, 512 * hf + 512, "LV", 16 * hf, 16 * hf + 16), 0.0, ALU.max)
+            act(r_("y", 512 * hf, 512 * hf + 256), ind("XA", 0, xa, "o", om, om + 16), AF.Identity)
+            act(r_("y", 512 * hf + 256, 512 * hf + 512), r_("y", 512 * hf, 512 * hf + 256), AF.Identity)
         for k in range(8):
             sb = 5 + k % 2
-            it = []
             for j in range(2):
-                it.append((PS(sb, 256 * j, 256 * j + 256), r_("NID"), r_("X", xa, xb)))
-                it.append((PS(sb, 256 * j, 256 * j + 256), r_("ID"), r_("G4", 2 * k + j, W, 16)))
-            mm(it[:2]); mm(it[2:])
+                o2 = PS(sb, 256 * j, 256 * j + 256)
+                mm([(o2, r_("NID"), r_("X", xa, xb)), (o2, r_("ID"), r_("G4", 2 * k + j, W, 16))])
             act(r_("S4", 512 * k, 512 * k + 512), PS(sb), AF.Sign, 0.5)
-            mm([(PS(7, 0, 256), Z("ZH", 2 * k + j), r_("S4", 512 * k + 256 * j, 512 * k + 256 * j + 256)) for j in range(2)], False, k == 7)
-        tt(r_("D", xa, xb), PS(7, 0, 256), r_("c4"), ALU.min)
-        trans(r_("V4"), r_("D", xa, xb))
-        scan(r_("V4s"), r_("m0"), r_("V4"), ALU.mult, ALU.max)
-        ts(r_("cn4"), r_("V4s", 15, 256, 16), -KD, ALU.add, OFF - 1.0, ALU.max)
-        ts(r_("V5", 0, 256, 16), r_("V4s", 15, 256, 16), -KD, ALU.add, OFF - 1.0, ALU.max)
-        tt(r_("V5", 1, 256, 16), r_("cn4"), r_("V5", 0, 256, 16), ALU.subtract)
-        trans(r_("C", xa, xb), r_("V5"))
+            for j in range(2):
+                for it in count(7, "S4", 512 * k + 256 * j, 2 * k + j, True): mm([it])
+        youngest(0, 7, 3.0, 7, "c4", 0, r_("C", xa, xb))
         if not last:
-            mm(wrap(5, 0, "Z1", "C", xa, S))
-            ts(r_("h", 96, 112), r_("kw", 0, 16), float(xa), ALU.add)
-            hop(5, r_("h", 96, 112), r_("h", 112, 128), r_("w1"), t, 0)
-        act(r_("dT"), ind("V", 0, 1024, "LV", 0, 32), AF.Identity)
+            mm(wrap(7, 0, "ZC", "C", xa, S))
+            scaled(r_("h", 96, 112), r_("kw", 0, 16), 1.0, xa - NONE)
+            hop(7, r_("h", 96, 112), r_("h", 112, 128), r_("w1"), t, 0)
+            left(0, 7, "c4", 0, r_("D", xa, xb))
+            mm([(PS(7, 0, 1), r_("BOF"), r_("acc", t, t + 1))])
+            if t == 0:
+                ts(r_("acc", 8, 9), PS(7, 0, 1), 0.5, ALU.mult, 2048.0, ALU.add)
+            else:
+                mm([(PS(7, 1, 2), r_("BOF"), r_("acc", 2, 3))])
+                cp(r_("acc", 3, 4), PS(7, 1, 2))
+                tt(r_("acc", 4, 5), PS(7, 0, 1), r_("acc", 3, 4), ALU.subtract)
+                ts(r_("acc", 9, 10), r_("acc", 4, 5), 0.5, ALU.mult, 128.0, ALU.add)
         na = 0
-        for m0 in range(0, 16, 2):
-            kb, k0 = (0, 0) if m0 < J_CUT else (4, J_CUT)
-            if m0 == k0:
-                k1 = J_CUT if k0 == 0 else 16
-                mm([(PS(kb, 32 * k0, 32 * k1), colv(1), r_("rows", 1024 + 32 * k0, 1024 + 32 * k1, 1, (0, 1, 1)))], True, False)
-            for m in (m0, m0 + 1):
-                gx = ind("XA", 0, xa, "oj", 32 * m, 32 * m + 32)
-                ch = r_("J", 512 * m, 512 * m + 512)
-                if m in J_ACT:
+        for hf, (oa, oe, at, main, moved, om) in enumerate(HALF):
+            y2, s0 = r_("y", 512 * hf, 512 * hf + 512), 256 * hf
+            mm([(PS(hf, 0, 256), colv(0), row(1 + hf))], True, False)
+            order = sorted(range(8), key=lambda j: (J_ACT[hf].index(j) + 0.5) / len(J_ACT[hf]) if j in J_ACT[hf] else ([x for x in range(8) if x not in J_ACT[hf]].index(j) + 0.4) / (8 - len(J_ACT[hf])))
+            for n, j in enumerate(order):
+                gx = ind("XA", 0, xa, "oj", s0 + 32 * j, s0 + 32 * j + 32)
+                ja = 4096 * hf + 512 * j
+                if j in J_ACT[hf]:
                     gb = r_("G", 512 * (na % 8), 512 * (na % 8) + 512); sb = 2 + na % 2; na += 1
                     act(gb, gx, AF.Identity)
-                    mm2((PS(sb), r_("NID"), r_("y")), (PS(sb), r_("ID"), gb))
-                    act(ch, PS(sb), AF.Sign, 0.5)
+                    mm2([(PS(sb), r_("NID"), y2)], [(PS(sb), r_("ID"), gb)])
+                    act(r_("J", ja, ja + 512), PS(sb), AF.Sign, 0.5)
                 else:
-                    tt(ch, gx, r_("y"), ALU.is_ge)
-            mm(wrap(kb, 32 * m0, "ZH" if m0 in J_ACT else "ZW", "J", 512 * m0, 1024), False, m0 + 2 == k1)
-        n2 = 32 * (16 - J_CUT)
-        tt(r_("key", 0, 512 - n2), PS(0, 0, 512 - n2), r_("dT", 0, 512 - n2), ALU.min)
-        a, n, nxt = 0, 512 - n2, 512
-        while n > 32:
-            h = 32 * (n // 64)
-            tt(r_("key", a + n - h, a + n), r_("key", a, a + h), r_("key", a + n - h, a + n), ALU.max)
-            a += h; n -= h
-        tt(r_("key", 960, 992), r_("key", a, a + 32), r_("ofb"), ALU.max)
-        tt(r_("key", 512, 512 + n2), PS(4, 512 - n2, 512), r_("dT", 512 - n2, 512), ALU.min)
-        a, n = 512, n2
-        while n > 32:
-            h = 32 * (n // 64)
-            tt(r_("key", a + n - h, a + n), r_("key", a, a + h), r_("key", a + n - h, a + n), ALU.max)
-            a += h; n -= h
-        kk = r_("ki", 0, 32)
-        tt(kk, r_("key", a, a + 32), r_("key", 960, 992), ALU.max)
-        ts(r_("ki", 32, 64), r_("ki", 0, 32), 8191, ALU.bitwise_and)
-        cp(r_("ob"), r_("ki", 32, 64))
-        ts(r_("HL", 0, 32), kk, -KD, ALU.add, OFF - 1.0, ALU.max)
-        ts(r_("cn"), kk, -KD, ALU.add, OFF - 1.0, ALU.max)
-        tt(r_("HL", 32, 64), r_("cn"), r_("HL", 0, 32), ALU.subtract)
-        mm([(PS(1), colv(0), row(0, 512))], True, False)
-        mm([(PS(1, r, 512, 16), Z("ZM", f, 144 * r), r_("HL", 32 * f, 32 * f + 32)) for f in range(2) for r in range(16)], False, True)
-        act(r_("crow"), PS(1), AF.Identity)
-        if NX_ACT:
-            act(r_("xb"), ind("XA", 0, xa, "ob", 0, 32), AF.Identity)
-            mm([(PS(3), colv(5), row(0, 512)), (PS(3), r_("HID"), r_("y"))], True, False)
-            mm([(PS(3), r_("HID"), r_("xb"))], False, True)
-            cp(r_("nx"), PS(3))
-        else:
-            tt(r_("sm"), ind("XA", 0, xa, "ob", 0, 32), r_("y"), ALU.add)
-            ts(r_("nx"), r_("sm"), 1, ALU.arith_shift_right)
-        cp(ind("X", 0, xa, "o", 0, 32), r_("nx"))
-        cp(ind("C", 0, xa, "o", 0, 32), r_("crow"))
+                    tt(r_("J", ja, ja + 512), gx, y2, ALU.is_ge)
+                mm([it for i in range(2) for it in count(hf, "J", ja + 256 * i, 2 * j + i, j in J_ACT[hf])], False, n == 7)
+            youngest(1 + hf, hf, 11.0, 4, "dm", main, r_("crow", s0, s0 + 256))
+            cp(ind("C", 0, xa, "o", om, om + 16), r_("crow", s0, s0 + 256))
+            mm(wrap(hf, 0, "ZB", "crow", s0, 256))
+            tt(r_("obf", 16 * hf, 16 * hf + 16), PS(hf, 0, 16), r_("ofl", om, om + 16), ALU.min)
+            ts(r_("ob", 16 * hf, 16 * hf + 16), r_("obf", 16 * hf, 16 * hf + 16), NONE, ALU.add)
+            act(r_("xb", s0, s0 + 256), ind("XA", 0, xa, "ob", 16 * hf, 16 * hf + 16), AF.Identity)
+            halved(hf, r_("y", 512 * hf, 512 * hf + 256), r_("xb", s0, s0 + 256), r_("nx", s0, s0 + 256))
+            cp(ind("X", 0, xa, "o", om, om + 16), r_("nx", s0, s0 + 256))
         if last:
-            dma("S", ext("yx", 0, W), r_("X", OFF + lo, xa), 6.0)
-            dma("A", ext("yx", W, W + S), r_("X", xa, xb), 2.5)
-            for b, bank, out, name in (("XA", 2, "oa32", "ya"), ("C", 3, "oc32", "yc")):
-                it = [(PS(bank, 0, 272), Z("Z1", s), r_(b, OFF + lo + 272 * s, OFF + lo + 272 * s + 272)) for s in range(16)]
-                mm(it[:8], True, False); mm(it[8:], False, True)
-                if b == "XA": ts(r_(out), PS(bank, 0, 272), 0.0, ALU.is_ge)
-                else: act(r_(out), PS(bank, 0, 272), AF.Identity, -float(OFF))
-                dma("A", ext(name, 0, W + S), r_(out), 2.5)
+            dma("S", ext("yx", 0, W), r_("X", OFF + lo, xa), 5.0)
+            it = [(PS(7, 0, 272), Z("ZC", s), r_("C", OFF + lo + 272 * s, OFF + lo + 272 * s + 272)) for s in range(16)]
+            mm2(it[:8], it[8:])
+            act(r_("oc32"), PS(7, 0, 272), AF.Identity, -1.0)
+            dma("A", ext("yc", 0, W + S), r_("oc32"), 2.5)
             break
         if Q_ACT: act(r_("gC"), ind("C", 0, xb, "w1", 0, 16), AF.Identity)
         else: cp(r_("gC"), ind("C", 0, xb, "w1", 0, 16))
-        mm(wrap(6, 0, "Z1", "gC", 0, S))
-        hop(6, r_("h", 112, 128), r_("h", 96, 112), r_("w2"), t, 1)
+        mm(wrap(4, 0, "ZC", "gC", 0, S))
+        hop(4, r_("h", 112, 128), r_("h", 96, 112), r_("w2"), t, 1)
         zs, z = "zs%d" % t, "z%d" % t
-        if Q_ACT > 1: act(r_(zs), ind("X", 0, xb, "w2", 0, 16), AF.Identity, 0.0, 0.5)
-        else: ts(r_(zs), ind("X", 0, xb, "w2", 0, 16), 0.5, ALU.mult)
-        add("G", "send", [t], {}, [r_(zs)], [("snd", t, t + 1, 1, None, None)], 1.0, lat=5.0, nosem=True)
+        if Q_ACT > 1: act(r_(zs), ind("X", 0, xb, "w2", 0, 16), AF.Identity)
+        else: cp(r_(zs), ind("X", 0, xb, "w2", 0, 16))
+        add("G", "send", [t], {}, [r_(zs)], [("snd", t, t + 1, 1, None, None)], 1.0, lat=4.0, nosem=True)
         cp(r_(z, 32 * rank, 32 * rank + 32), r_(zs, 32 * rank, 32 * rank + 32))
         who(t + 1, 2)
-        cp(ind("XA", 0, xa, "o", 0, 32), r_("nx"))
-        act(r_("dm"), ind("D", 0, xa, "o", 0, 32), AF.Identity)
-        it = [(PS(2), colv(4), row(1, 512))] + [(PS(2), Z("ZH" if m in J_ACT else "ZW", m), r_("J", 512 * m, 512 * m + 512)) for m in range(16)]
-        for k in range(0, 17, 3):
-            mm(it[k:k + 3], k == 0, k + 3 >= 17)
-        tt(r_("left"), PS(2), r_("dm"), ALU.min)
-        cp(ind("D", 0, xa, "o", 0, 32), r_("left"))
-        mm([(PS(3, 0, 1), r_("BOF"), r_("acc", t, t + 1))])
-        if t == 0:
-            act(r_("junk"), r_("XA", OFF, OFF + S), AF.Sign, 0.5, 1.0, r_("acc", 2, 3))
-            ts(r_("acc", 8, 9), PS(3, 0, 1), -0.5, ALU.mult, 2048.0, ALU.add)
-            tt(r_("acc", 3, 4), PS(3, 0, 1), r_("acc", 2, 3), ALU.subtract)
-        else:
-            tt(r_("acc", 4, 5), r_("acc", 3, 4), PS(3, 0, 1), ALU.subtract)
-            ts(r_("acc", 9, 10), r_("acc", 4, 5), 0.5, ALU.mult, 128.0, ALU.add)
+        for k in range(2):
+            mm(wrap(2 + k, 0, "ZC", "C", OFF + lo + S + 2048 * k, 2048))
+            ts(r_("cw", 128 * k, 128 * k + 128), PS(2 + k, 0, 128), NONE, ALU.add)
+        for hf, (oa, oe, at, main, moved, om) in enumerate(HALF):
+            left(1 + hf, 6 + hf, "dm", main, r_("left", 256 * hf, 256 * hf + 256))
+            cp(ind("D", 0, xa, "o", om, om + 16), r_("left", 256 * hf, 256 * hf + 256))
         mset(r_("XA", OFF + lo, OFF + lo + S), -256.0)
     return ops
 
 
 def is_psum(b):
     return b in SCRATCH and SCRATCH[b][0] == "psum"
+
+
+def meet(x, y):
+    if x[0] >= y[1] or y[0] >= x[1]: return False
+    return x[2] != y[2] or (x[0] - y[0]) % x[2] == 0
 
 
 def schedule(ops):
@@ -485,23 +504,23 @@ def schedule(ops):
             for p in ops[:i]:
                 if p["calls"][0][0] == "send" and p["calls"][0][1][0] == o["arr"]: dep[p["i"]] = False
         for acc, w in [(x, False) for x in o["rd"]] + [(x, True) for x in o["wr"]]:
-            b, a, e = acc
+            b = acc[0]
             ps = is_psum(b)
-            for (a2, e2, j, w2) in seen.get(b, []):
+            for (run, j, w2) in seen.get(b, []):
                 if j == i: continue
                 p = ops[j]
                 dmaish = "sem" in p or "sem" in o
                 same = p["q"] == o["q"] and not dmaish
                 if ps:
                     if same and not (w or w2): continue
-                elif a2 >= e or a >= e2 or not (w or w2): continue
+                elif not (w or w2) or not meet(run, acc[1:]): continue
                 need = (not same) or (o["q"] != "P" and ((w2 and not w) or SAME_QUEUE_WAW))
                 dep[j] = dep.get(j, False) or need
         for acc, w in [(x, False) for x in o["rd"]] + [(x, True) for x in o["wr"]]:
-            b, a, e = acc
+            b, a, e, st = acc
             lst = seen.setdefault(b, [])
-            if w: lst[:] = [x for x in lst if not (is_psum(b) or (a <= x[0] and x[1] <= e)) or x[2] == i]
-            lst.append((a, e, i, w))
+            if w: lst[:] = [x for x in lst if not (is_psum(b) or (st == 1 and a <= x[0][0] and x[0][1] <= e)) or x[1] == i]
+            lst.append((acc[1:], i, w))
         o["dep"] = dep
     if "t0" not in KEPT:
         KEPT["t0"] = best_times(ops)
@@ -641,7 +660,6 @@ def rank_program(g, core, T, topo):
             elif name == "tensor_tensor": ins = e.tensor_tensor(*a)
             elif name == "tensor_scalar": ins = e.tensor_scalar(*a)
             elif name == "tensor_tensor_scan": ins = e.tensor_tensor_scan(*a)
-            elif name == "tensor_reduce": ins = e.tensor_reduce(*a)
             elif name == "transpose": ins = e.transpose(*a)
             elif name == "memset": ins = e.memset(*a)
             elif name == "activation": ins = e.activation(*a, **k)

@@ -5,15 +5,26 @@ from concourse.mybir import AluOpType as ALU, AxisListType as AX, ActivationFunc
 W, S, R, CAP, ST, N = 4096, 256, 3, 512, 683, 8
 OFF = 544
 TW = OFF + W + R * S
-NONE = OFF - 1.0
+BASE = OFF - 129.0
 MAGIC = 3 * 2 ** 22
 BIG = 100000.0
 NS = 544
-S3_ACT = (6,)
-UPD_V = (4, 6, 7)
-PAR_V = (5, 7)
-J_ACT = ((7,), (0, 3, 6))
-DW_ACT, DM_ACT, Q_ACT, HI_ACT = True, (False, True), 1, True
+S3_ACT = ((), (4,), (4,))
+UPD_V = ((4, 6, 7), (4, 6, 7), (4, 6, 7))
+PAR_V = ((5, 7), (3, 5, 7), (3, 5, 7))
+NA = 256
+J_ROWS = (2, 2)
+J_ACT = ((2, 2), (2, 2), (2, 3))
+S4_ACT = (4, 8)
+QUICK = (False, False)
+O_ACT = (0, 1, 2)
+S4_LATE = 0
+C_ACT, D_ACT, C32_PS = False, False, True
+S4_TT = True
+EARLY = 1
+J_BANK, K_BANK = (2, 3), ((4, 6), (4, 6), (4, 4))
+G4_CUT = (0, 2048, 3072, 4096)
+DW_ACT, DM_ACT, Q_ACT = True, (False, True), 1
 SAME_QUEUE_WAW = True
 
 F, B16, I32, U16 = "float32", "bfloat16", "int32", "uint16"
@@ -21,11 +32,11 @@ SCRATCH = {}
 for _n, _c, _d in [
     ("X", TW, B16), ("XA", TW, B16), ("C", TW + 512, B16), ("D", TW, F), ("DW", 304, B16),
     ("cm", 768, B16), ("z0", 256, B16), ("z1", 256, B16), ("zs0", 256, B16), ("zs1", 256, B16),
-    ("dli", 2048, I32), ("cdi", 288, I32), ("cdf", 304, F), ("cdh", 304, B16), ("cdl", 304, B16),
-    ("pi", 16, I32), ("pc", 24, F), ("ia", 256, F), ("ib", 128, F), ("ic", 256, F), ("kf", NS, F), ("ku", NS, U16), ("kw", 48, F),
-    ("Z1", 144, B16), ("ZC", 144, B16), ("ZB", 144, B16), ("BH", 8, B16), ("N8K", 128, B16), ("HID", 128, B16), ("Rl", 768, B16), ("xb", 512, B16), ("nx", 512, B16), ("Ui", 2048, B16), ("U", 2048, B16),
+    ("dli", 2048, I32), ("cdi", 288, I32), ("cdf", 304, F), ("cdh", 304, B16), ("cdl", 304, B16), ("cd32", 512, F), ("C32", TW, F), ("crow32", 512, F),
+    ("pi", 16, I32), ("pc", 24, F), ("ia", 256, F), ("ib", 128, F), ("ic", 384, F), ("kf", NS, F), ("ku", NS, U16), ("kw", 48, F),
+    ("Z1", 144, B16), ("ZC", 144, B16), ("ZB", 144, B16), ("BH", 8, B16), ("N8K", 128, B16), ("HID", 128, B16), ("Rl", 768, B16), ("xb", 512, B16), ("nx", 512, B16), ("mu", 16, F), ("zb", 1480, B16), ("U", 2048, B16),
     ("BO", 128, B16), ("BOF", 128, F), ("ID", 128, B16), ("NID", 128, B16), ("ID32", 128, B16), ("IDF", 128, F), ("SU", 128, B16),
-    ("rows", 768, B16), ("col", 384, B16), ("mdB", 256, F), ("m0", 256, F), ("pw", 256, F), ("zer", 272, F), ("LVf", 16, F), ("LV", 32, U16),
+    ("rows", 2816, B16), ("col", 384, B16), ("mdB", 256, F), ("m0", 384, F), ("P8K", 128, B16), ("ID2", 128, B16), ("sm", 1024, I32), ("pw", 256, F), ("zer", 864, F), ("LVf", 16, F), ("LV", 48, U16),
     ("wi", 256, I32), ("wj", 256, I32), ("who", 256, U16),
     ("cmp", 4096, B16), ("par", 4096, B16), ("G", 4096, B16), ("G4", 4096, B16), ("S4", 4096, B16), ("J", 8192, B16),
     ("sq4", 256, F), ("i4a", 256, I32), ("i4b", 256, I32), ("c4", 256, F), ("o4", 256, U16),
@@ -40,12 +51,13 @@ for _n, _c, _d in [
     SCRATCH[_n] = ("sbuf", [128, _c], _d)
 for _k in range(8):
     SCRATCH["P%d" % _k] = ("psum", [128, 512], F)
-NDMA = 24
+NDMA = 48
 SEMAPHORES = ["qV", "qA", "qP", "qG", "arr0", "arr1", "sent"] + ["dma%d" % _k for _k in range(NDMA)]
 
-CY, PCY, LAT = 0.00083, 0.00042, 0.1
+CY, PCY, LAT = 0.00083, 0.00042, 0.12
 GATH, SCAT = 1.56, 3.8
-SEED, ROUNDS, TEMP = 1, 6000, 0.2
+OTHERS = ((1.3, 1.15, 2.0), (1.3, 2.0, 5.5))
+SEED, ROUNDS, TEMP = 1, 7000, 0.3
 
 
 def sends(T, topo, core):
@@ -62,7 +74,7 @@ def sends(T, topo, core):
     for i, r in enumerate(far[4:]):
         calls[1].append((r, sum(1 << e for e in fe[b * i:b * i + b])))
     for r in near:
-        calls[0].append((r, sum(1 << e for e in topo.engines(core, T.cores[r]) if e not in fe)))
+        calls[0].append((r, sum(1 << e for e in [e for e in topo.engines(core, T.cores[r]) if e not in fe][:a])))
     return calls
 
 
@@ -71,7 +83,8 @@ def bits(m):
 
 
 def program(rank):
-    ops = []
+    ops, table = [], []
+    PARTS = ((NA, 0, 0, NA // 16 + 1, 0, 0, 16, 0), (CAP - NA, NA, NA // 16, NS // 16, NA + 16, NA + 48, NA + 32, NA // 16 + 2))
 
     def r_(b, a=0, e=None, st=1, p=None):
         return (b, a, SCRATCH[b][1][1] if e is None else e, st, p, None)
@@ -94,7 +107,8 @@ def program(rank):
         for x in writes:
             wr.append(x[:4])
             if x[5]: rd.append(x[5] + (1,))
-        d = {"q": q, "calls": [(name, args, kw)], "rd": rd, "wr": wr, "dur": dur, "lat": 0.0}
+        d = {"q": q, "calls": [(name, args, kw)], "rd": rd, "wr": wr, "dur": dur, "lat": 0.0,
+             "gathers": sum(cnt(x) for x in reads if isinstance(x, tuple) and x[5]), "scatters": sum(cnt(x) for x in writes if x[5])}
         d.update(more)
         ops.append(d)
         return d
@@ -116,13 +130,17 @@ def program(rank):
     def trans(out, a): return add("V", "transpose", [out, a], {}, [a], [out], vdur(out, [a], half(out, a)))
     def mset(out, v): return add("V", "memset", [out, v], {}, [], [out], vdur(out, [out], half(out)))
     def act(out, a, f, bias=0.0, scale=1.0, acc=None):
-        kw = {"bias": bias, "scale": scale}
+        kw = {} if out[5] else {"bias": bias, "scale": scale}
         if acc: kw["accum_out"] = acc
-        dur = 0.065 + cnt(out) * GATH * CY if a[5] else 0.01 + max(64, cnt(out)) * CY
+        dur = 0.065 + cnt(out) * (SCAT if out[5] else GATH if a[5] else 1.0) * CY
+        if f == AF.Silu and not table:
+            table.append(f); dur += 1.3
         return add("A", "activation", [out, a, f], kw, [a, bias, scale], [out] + ([acc] if acc else []), dur)
     def iota(out, pat, base, cm):
         kw = {} if SCRATCH[out[0]][2] == I32 else {"allow_small_or_imprecise_dtypes": True}
         return add("G", "iota", [out, pat, base, cm], kw, [], [out], 0.13 + 2 * cnt(out) * CY)
+    def select(out, a, pat, op, other, base, cm):
+        return add("G", "affine_select", [out, a, pat, op, other, base, cm], {}, [a], [out], 0.17 + 2 * cnt(out) * CY)
     def mm(items, first=True, last=True):
         d = None
         for i, (o, l, x) in enumerate(items):
@@ -133,17 +151,21 @@ def program(rank):
             else:
                 d["calls"].append(call); d["rd"] += [l[:4], x[:4]]; d["dur"] += dur
         return d
+    def apart(d):
+        d["calls"] = [(n, x[:3] + [True, True], kw) for n, x, kw in d["calls"]]
+        return d
     def mm2(x, y):
         mm(x, True, False); mm(y, False, True)
     nd = [0]
     def dma(q, out, a, us):
         rd = [a] if a[0] in SCRATCH else []
         wr = [out] if out[0] in SCRATCH else []
-        add(q, "dma_start", [out, a], {}, rd, wr, 0.1, lat=us, sem="dma%d" % nd[0]); nd[0] += 1
+        nd[0] += 1
+        return add(q, "dma_start", [out, a], {}, rd, wr, 0.1, lat=us, sem="dma%d" % nd[0])
     def ext(b, a, e): return (b, a, e, 1, None, None)
     def Z(name, r): return r_(name, 15 - r, 143 - r)
     def PS(k, a=0, e=512, st=1): return r_("P%d" % k, a, e, st)
-    def row(k): return r_("rows", 256 * k, 256 * k + 256, 1, (0, 1, 1))
+    def row(k, n): return r_("rows", 256 * k, 256 * k + n, 1, (0, 1, 1))
     def colv(k): return r_("col", 128 * k, 128 * k + 128, 1, (0, 1, 1))
     def wrap(bank, c0, zname, buf, a, n):
         return [(PS(bank, c0, c0 + n // 16), Z(zname, r), r_(buf, a + r, a + n, 16)) for r in range(16)]
@@ -151,13 +173,11 @@ def program(rank):
     def icol(k): return r_("pi", k, k + 1)
     cG, cR, cCo = pcol(0), pcol(1), pcol(2)
 
-    dma("A", r_("cm"), ext("come", 0, 768), 2.2)
-    dma("S", r_("X", OFF, OFF + 1024), ext("x0", 0, 1024), 2.5)
-    dma("S", r_("cdi", 0, 256), ext("cd0", 0, W), 3.0)
-    for k in range(1, 4):
-        dma("S" if k % 2 == 0 else "A", r_("X", OFF + 1024 * k, OFF + 1024 * k + 1024), ext("x0", 1024 * k, 1024 * k + 1024), 2.8 + 0.9 * k)
-    dma("S", r_("cdi", 256, 288), ext("age", 0, 512), 6.2)
-    dma("S", r_("dli"), ext("dl0", 0, 2048), 10.0)
+    def xload(k): return r_("X", OFF + 1024 * k, OFF + 1024 * k + 1024), ext("x0", 1024 * k, 1024 * k + 1024)
+    for q, loads in (("S", [xload(0) + (2.6,), (r_("cdi", 0, 256), ext("cd0", 0, W), 3.6), xload(2) + (4.5,), (r_("cdi", 256, 288), ext("age", 0, 512), 5.5), (r_("dli"), ext("dl0", 0, 2048), 9.5)]),
+                     ("A", [(r_("cm", 0, S), ext("come", 0, S), 2.3), xload(1) + (3.5,), xload(3) + (5.3,), (r_("cm", S, 768), ext("come", S, 768), 6.0)])):
+        for n, (out, a, us) in enumerate(loads):
+            dma(q, out, a, us).update(behind=n > 0)
     def fill(out, v): iota(out, [[0, cnt(out)]], int(v), 0)
     def scaled(out, a, w, b=0.0): act(out, a, AF.Identity, b, w)
     iota(icol(0), [[0, 1]], 0, 1)
@@ -174,47 +194,49 @@ def program(rank):
     fill(r_("rows", 0, 256, 1, one), 1)
     mset(r_("col", 128, 256, 1, one), -0.25)
     fill(r_("col", 256, 384, 1, one), MAGIC)
-    for k in range(4):
-        iota(r_("Ui", 512 * k, 512 * k + 512), [[-1, 4], [-16, 8], [0, 16]], -4 * k, 1)
-        ts(r_("U", 512 * k, 512 * k + 512), r_("Ui", 512 * k, 512 * k + 512), 0.0, ALU.is_equal, -512.0, ALU.mult)
     iota(r_("M", 0, 128), [[1, 128]], 0, -1)
     ts(r_("ID"), r_("M", 0, 128), 0.0, ALU.is_equal)
-    for nme, w in (("HID", 0.5), ("NID", -1.0), ("ID32", 32.0), ("IDF", 1.0), ("N8K", -8192.0)):
+    for nme, w in (("HID", 0.5), ("NID", -1.0), ("ID32", 32.0), ("IDF", 1.0), ("N8K", -8192.0), ("P8K", 8192.0), ("ID2", 2.0)):
         scaled(r_(nme), r_("ID"), w)
     iota(r_("ib"), [[16, 8], [0, 16]], 0, 0)
     ts(r_("BO"), r_("ib"), cG, ALU.is_equal)
     scaled(r_("BOF"), r_("BO"), 1.0)
-    ts(r_("M", 128, 256), r_("M", 0, 128), 0.0, ALU.is_lt, -1.0, ALU.mult)
-    tt(r_("SU"), r_("M", 128, 256), r_("BOF"), ALU.mult)
+    iota(r_("LVf"), [[1, 16]], 0, 0)
+    ts(r_("mu"), r_("LVf"), cR, ALU.is_equal, -512.0, ALU.mult)
+    for r in range(16):
+        if r % 2: ts(r_("U", 128 * r, 128 * r + 128), r_("BO"), r_("mu", r, r + 1), ALU.mult)
+        else: scaled(r_("U", 128 * r, 128 * r + 128), r_("BO"), r_("mu", r, r + 1))
+    select(r_("SU"), r_("BO"), [[-1, 128]], ALU.is_gt, 0.0, 0, 1)
     iota(icol(4), [[0, 1]], 256, 16)
     tt(icol(5), icol(4), icol(3), ALU.subtract)
     ts(icol(6), icol(5), 255, ALU.bitwise_and)
     ts(icol(7), icol(5), 16, ALU.bitwise_and)
     ts(icol(8), icol(7), 16.0, ALU.mult)
     tt(icol(9), icol(8), icol(3), ALU.add)
-    iota(r_("LVf"), [[1, 16]], 0, 0)
-    for hf, op in ((0, ALU.subtract), (1, ALU.add)):
-        tt(icol(10 + hf), icol(6), icol(7), op)
-        ts(icol(12 + hf), icol(10 + hf), 255, ALU.bitwise_and)
-        tt(pcol(6 + hf), icol(12 + hf), icol(9), ALU.add)
-        ts(r_("LV", 16 * hf, 16 * hf + 16), r_("LVf"), pcol(6 + hf), ALU.add)
-    ts(r_("cdf", 0, 256), r_("cdi", 0, 256), 1.0, ALU.add)
-    ts(r_("cdf", 256, 272), r_("cdi", 0, 16), 1.0, ALU.add)
+    tt(icol(10), icol(6), icol(7), ALU.subtract)
+    tt(pcol(6), icol(10), icol(9), ALU.add)
+    ts(r_("LV", 0, 16), r_("LVf"), pcol(6), ALU.add)
+    tt(icol(11), icol(6), icol(7), ALU.add)
+    ts(icol(12), icol(11), 255, ALU.bitwise_and)
+    tt(pcol(7), icol(12), icol(9), ALU.add)
+    ts(r_("LV", 16, 32), r_("LVf"), pcol(7), ALU.add)
+    ts(r_("cdf", 0, 256), r_("cdi", 0, 256), 65.0, ALU.add)
+    ts(r_("cdf", 256, 272), r_("cdi", 0, 16), 65.0, ALU.add)
     trans(r_("V", 0, 256), r_("cdf", 0, 256))
     trans(r_("V", 256, 512), r_("cdf", 16, 272))
-    ts(r_("cw"), ind("V", 0, 512, "LV", 0, 16), NONE, ALU.add)
+    ts(r_("cw"), ind("V", 0, 512, "LV", 0, 16), BASE + 64, ALU.add)
     fill(r_("XA", 0, OFF), -1)
     fill(r_("DW", 256, 304), 0)
     scaled(cCo, cR, 61.0, 7.0)
     for t in range(R):
-        r0 = float(ST * (t + 1) % 16)
-        ts(pcol(8 + 2 * t), cR, r0, ALU.is_ge)
-        ts(pcol(9 + 2 * t), cR, r0, ALU.is_lt)
-    fill(r_("zer"), 0)
-    iota(r_("ic"), [[0, 16], [1, 16]], 0, 0)
-    act(r_("m0"), r_("ic"), AF.Sign)
-    ts(r_("mdB"), r_("ic"), cR, ALU.is_equal, BIG, ALU.mult)
-    for a, e, b in ((0, 256, 0), (256, 272, 0), (272, 288, 496), (288, NS, 256)):
+        fill(pcol(16 + t), ST * (t + 1) % 16)
+    ts(r_("pc", 8, 14, 2), r_("pc", 16, 19), cR, ALU.is_le, -0.0625, ALU.mult)
+    ts(r_("pc", 9, 14, 2), r_("pc", 16, 19), cR, ALU.is_gt, -0.0625, ALU.mult)
+    fill(r_("zer"), 0); fill(r_("zb", 0, 740), 0); fill(r_("zb", 740, 1480), 0)
+    iota(r_("ic", 0, 256), [[0, 16], [1, 16]], 0, 0)
+    fill(r_("m0", 0, 256), 1); fill(r_("m0", 0, 256, 16), 0)
+    ts(r_("mdB"), r_("ic", 0, 256), cR, ALU.is_equal, BIG, ALU.mult)
+    for a, e, b in ((0, NA, 0), (NA, NA + 16, 0), (NA + 16, NA + 32, CAP - 16), (NA + 32, NS, NA)):
         iota(r_("kf", a, e), [[1, e - a]], b, 0)
         iota(r_("ia", 144 + a // 16, 144 + e // 16), [[16, (e - a) // 16]], b, 0)
     cp(r_("ku"), r_("kf"))
@@ -225,24 +247,28 @@ def program(rank):
     ts(pcol(15), cR, 3.0, ALU.is_lt)
     scaled(r_("ZC"), r_("Z1"), pcol(14))
     scaled(r_("ZB"), r_("Z1"), pcol(15))
-    fill(r_("col", 0, 128, 1, one), 1); fill(r_("rows", 256, 768, 1, one), 0)
-    for hf in range(2):
-        for j in J_ACT[hf]:
-            for m in (2 * j, 2 * j + 1):
-                fill(r_("rows", 256 * (hf + 1) + m, 256 * (hf + 2), 16, one), 8)
+    fill(r_("col", 0, 128, 1, one), 1)
+    fill(r_("rows", 256, 512, 1, one), 8)
+    for k in sorted(set(sum(J_ACT, ()) + S4_ACT)):
+        select(r_("rows", 512 + 256 * k, 768 + 256 * k, 1, one), r_("rows", 256, 512, 1, one), [[0, 16], [1, 16]], ALU.is_ge, 0.0, 2 * k - 16, 0)
     for k in range(4):
-        fill(r_("C", OFF + 1024 * k, OFF + 1024 * k + 1024), 0)
-    fill(r_("C", TW, TW + 512), 0)
-    fill(r_("C", 0, OFF), 0)
-    fill(r_("X", 0, OFF), 0)
+        dma("S", r_("C", 1480 * k, 1480 * k + 1480), r_("zb"), 4.0 + k)
+    dma("S", r_("X", 0, OFF), r_("zb", 0, OFF), 4.0)
     for k in range(3):
-        fill(r_("D", 864 * k, 864 * k + 864), 0)
+        dma("S", r_("D", 864 * k, 864 * k + 864), r_("zer"), 5.0 + k)
     cp(r_("cdf", 272, 304), r_("cdi", 256, 288))
     scaled(r_("cdh"), r_("cdf"), 1.0)
-    tt(r_("cdl"), r_("cdf"), r_("cdh"), ALU.subtract)
+    mm([(PS(7, 0, 304), r_("IDF"), r_("cdf")), (PS(7, 0, 304), r_("NID"), r_("cdh"))])
+    scaled(r_("cdl"), PS(7, 0, 304), 1.0, 64.0)
+    if C_ACT:
+        for k in range(7):
+            dma("S", r_("C32", 864 * k, min(TW, 864 * k + 864)), r_("zer", 0, min(864, TW - 864 * k)), 8.0 + k)
+        for f, b in ((0, "cdh"), (1, "cdl")):
+            scaled(r_("cd32", 256 * f, 256 * f + 256), r_(b, 0, 256), 1.0)
+            dma("S", r_("C32", OFF, OFF + W, 1, (f, 128, 16)), r_("cd32", 256 * f, 256 * f + 256), 3.0).update(any="C32")
     for f, b in ((0, "cdh"), (1, "cdl")):
-        dma("S", r_("C", OFF, OFF + W, 1, (f, 128, 16)), r_(b, 0, 256), 2.5)
-        dma("S", r_("C", TW, TW + 512, 1, (f, 128, 16)), r_(b, 272, 304), 2.5)
+        dma("S", r_("C", OFF, OFF + W, 1, (f, 128, 16)), r_(b, 0, 256), 2.5).update(any="C")
+        dma("S", r_("C", TW, TW + 512, 1, (f, 128, 16)), r_(b, 272, 304), 2.5).update(any="C")
     for k in range(4):
         ts(r_("D", OFF + 2048 + 512 * k, OFF + 2560 + 512 * k), r_("dli", 512 * k, 512 * k + 512), float(OFF), ALU.add)
 
@@ -263,46 +289,45 @@ def program(rank):
         tt(f, PS(bank, 0, 16), thr, ALU.is_lt)
         tt(e, f, w0, ALU.mult)
         tt(wout, PS(bank, 0, 16), e, ALU.max)
-        ts(wu, wout, NONE, ALU.add)
+        ts(wu, wout, BASE, ALU.add)
 
-    def count(bank, buf, a, m, signs):
+    def count(bank, buf, a, n, m, signs):
         w = r_("BH") if signs else r_("BO", 0, 128, 16)
-        return [(PS(bank, 128 * b + m, 128 * b + 128, 16), r_(buf, a + 128 * b, a + 128 * b + 128), w) for b in range(2)]
+        return [(PS(bank, b + m, b + 128, 16), r_(buf, a + b, a + b + 128), w) for b in range(0, n, 128)]
 
-    def turned(bank, buf, a, ident):
-        return [(PS(bank, 128 * b, 128 * b + 128), r_(buf, a + 128 * b, a + 128 * b + 128), r_(ident)) for b in range(2)]
+    def turned(bank, buf, a, n, ident):
+        return [(PS(bank, b, b + 128), r_(buf, a + b, a + b + 128), r_(ident)) for b in range(0, n, 128)]
 
-    def youngest(k, cb, need, kb, lists, a0, out):
-        a = 256 * k
-        top, cn = r_("V4s", a + 15, a + 256, 16), r_("cn", 16 * k, 16 * k + 16)
-        if kb != cb: mm(turned(kb, lists, a0, "IDF"), True, False)
-        act(r_("Rl", a, a + 256), PS(cb, 0, 256), AF.Relu, need, -1.0)
-        if kb == cb: mm(turned(kb, lists, a0, "IDF"), True, False)
-        mm([(PS(kb, 0, 256), r_("N8K"), r_("Rl", a, a + 256))], False, True)
-        scan(r_("V4s", a, a + 256), r_("m0"), PS(kb, 0, 256), ALU.mult, ALU.max)
-        if HI_ACT: act(r_("V5", a, a + 256, 16), top, AF.Relu, -NONE)
-        else: ts(r_("V5", a, a + 256, 16), top, -NONE, ALU.add, 0.0, ALU.max)
-        ts(cn, top, -NONE, ALU.add, 0.0, ALU.max)
-        if k: act(r_("V5", a + 2, a + 256, 16), top, AF.Relu, 8192.0 * OFF, -8192.0)
-        tt(r_("V5", a + 1, a + 256, 16), cn, r_("V5", a, a + 256, 16), ALU.subtract)
-        mm(turned(cb, "V5", a, "ID"))
-        act(out, PS(cb, 0, 256), AF.Identity)
+    def youngest(a, n, cb, need, kb, lists, a0, out, out32, quick=False):
+        top, cn = r_("V4s", a + 15, a + n, 16), r_("cn", a // 16, (a + n) // 16)
+        if kb != cb: mm(turned(kb, lists, a0, n, "IDF"), True, False)
+        if quick: ts(r_("Rl", a, a + n), PS(cb, 0, n), -need, ALU.add, 0.0, ALU.min)
+        else: act(r_("Rl", a, a + n), PS(cb, 0, n), AF.Relu, need, -1.0)
+        if kb == cb: mm(turned(kb, lists, a0, n, "IDF"), True, False)
+        mm([(PS(kb, 0, n), r_("P8K" if quick else "N8K"), r_("Rl", a, a + n))], False, True)
+        scan(r_("V4s", a, a + n), r_("m0", 0, n), PS(kb, 0, n), ALU.mult, ALU.max)
+        if quick: ts(r_("V5", a, a + n, 16), top, -BASE - 64, ALU.add, 0.0, ALU.max)
+        else: act(r_("V5", a, a + n, 16), top, AF.Relu, -BASE - 64)
+        ts(cn, top, -BASE, ALU.add, 64.0, ALU.max)
+        if a: act(r_("V5", a + 2, a + n, 16), top, AF.Relu, 16384.0 * (OFF - 0.5), -16384.0)
+        tt(r_("V5", a + 1, a + n, 16), cn, r_("V5", a, a + n, 16), ALU.subtract)
+        mm(turned(cb, "V5", a, n, "ID"))
+        if quick: cp(out, PS(cb, 0, n))
+        else: act(out, PS(cb, 0, n), AF.Identity)
+        if out32: act(out32, PS(cb, 0, n) if a == 0 or C32_PS else out, AF.Identity)
 
-    def left(k, bank, lists, a0, out):
-        mm([(PS(bank, 0, 256), r_("IDF"), r_(lists, a0, a0 + 256))], True, False)
-        mm(turned(bank, "Rl", 256 * k, "N8K"), False, True)
-        act(out, PS(bank, 0, 256), AF.Identity)
+    def left(a, n, bank, lists, a0, out, quick=False):
+        apart(mm(turned(bank, "Rl", a, n, "P8K" if quick else "N8K")))
+        tt(out, PS(bank, 0, n), r_(lists, a0, a0 + n), ALU.add)
 
     def halved(bank, a, b, out, **more):
-        o = PS(bank, 0, 256)
-        mm([(o, r_("HID"), a), (o, colv(1), row(0))], True, False)
-        mm(([(o, r_("HID"), b)] if b else []) + [(o, colv(2), row(0))], False, True).update(more)
+        n = cnt(a)
+        o = PS(bank, 0, n)
+        mm([(o, r_("HID"), a), (o, colv(1), row(0, n))], True, False)
+        mm(([(o, r_("HID"), b)] if b else []) + [(o, colv(2), row(0, n))], False, True).update(more)
         act(out, o, AF.Identity, -float(MAGIC))
 
     who(0, 4)
-    mm(wrap(6, 0, "ZC", "C", TW, 512))
-    for t in range(R - 1):
-        scaled(r_("agw", 16 * t, 16 * t + 16), PS(6, 16 * t, 16 * t + 16), -1.0, float(W + S * t + 256))
 
     for t in range(R):
         lo, B, rot = S * t, W + S * t, ST * (t + 1)
@@ -315,12 +340,18 @@ def program(rank):
         mm([(PS(7, 0, 256), r_("BO"), r_("X", xa, xb))])
         act(r_("sq4"), PS(7, 0, 256), AF.Square)
         act(PS(7, 256, 512), PS(7, 0, 256), AF.Identity, 0.0 if t == 0 else r_("acc", 7 + t, 8 + t), cCo)
-        ts(r_("i4b"), r_("sq4"), 1.0 / 32, ALU.mult, -0.375, ALU.add)
-        tt(r_("i4a"), PS(7, 256, 512), r_("i4b"), ALU.add)
-        ts(r_("i4b"), r_("i4a"), W - 1, ALU.bitwise_and)
-        cp(r_("o4"), r_("i4b"))
-        ts(r_("c4"), r_("i4b"), float(OFF + lo), ALU.add)
-        for n, k in enumerate(S3_ACT):
+        def offsets4():
+            d = ts(r_("i4b"), r_("sq4"), 1.0 / 32, ALU.mult, -0.375, ALU.add)
+            if S4_LATE: d["rd"].append(r_("par", 512 * S4_LATE - 1, 512 * S4_LATE)[:4])
+            tt(r_("i4a"), PS(7, 256, 512), r_("i4b"), ALU.add)
+            ts(r_("i4b"), r_("i4a"), W - 1, ALU.bitwise_and)
+            cp(r_("o4"), r_("i4b"))
+            ts(r_("c4"), r_("i4b"), float(OFF + lo), ALU.add)
+        if not S4_LATE: offsets4()
+        def mark(k, out, a, w):
+            if k in O_ACT: act(out, a, AF.Relu, 0.0, w)
+            else: ts(out, a, w, ALU.mult, 0.0, ALU.max)
+        for n, k in enumerate(S3_ACT[t]):
             a, sb = OFF + lo + 512 * k, 5 + n % 2
             gb = r_("G", 512 * k, 512 * k + 512)
             act(gb, ind("X", xa, xb, "who", 32 * k, 32 * k + 32), AF.Identity)
@@ -332,13 +363,15 @@ def program(rank):
         for k in range(4):
             a = OFF + lo + 1024 * k
             dw = r_("DW", d0 + 64 * k, d0 + 64 * k + 64)
-            for u, v, on in runs(k, S3_ACT):
-                if not on:
+            for u, v, on in runs(k, S3_ACT[t]):
+                if t and k < EARLY:
+                    tt(r_("cmp", 512 * u, 512 * v), ind("z%d" % (t - 1), 0, S, "who", 32 * u, 32 * v), r_("J", 512 * u, 512 * v), ALU.is_ge, arr=t - 1)
+                elif not on:
                     tt(r_("cmp", 512 * u, 512 * v), ind("X", xa, xb, "who", 32 * u, 32 * v), r_("X", OFF + lo + 512 * u, OFF + lo + 512 * v), ALU.is_ge)
             bank = k % 2
             if t == 0: mm(wrap(bank, 0, "Z1", "cmp", 1024 * k, 1024))
             else: mm2([(PS(bank, 0, 64), r_("ID32"), dw)], wrap(bank, 0, "Z1", "cmp", 1024 * k, 1024))
-            for u, v, on in runs(k, S3_ACT):
+            for u, v, on in runs(k, S3_ACT[t]):
                 src, dst = PS(bank, 32 * (u - 2 * k), 32 * (v - 2 * k)), r_("DW", d0 + 32 * u, d0 + 32 * v)
                 if DW_ACT: act(dst, src, AF.Relu, -5.0 if on else -10.0)
                 else: ts(dst, src, -5.0 if on else -10.0, ALU.add, 0.0, ALU.max)
@@ -346,27 +379,27 @@ def program(rank):
                 ub = 2 + (2 * k + p) % 3
                 it = [(PS(ub, r // 2, 512, 8), r_("U", 128 * r, 128 * r + 128), dw) for r in range(p, 16, 2)]
                 xs, xo = r_("X", a + p, a + 1024, 2), r_("XA", a + p, a + 1024, 2)
-                if 2 * k + p in UPD_V:
-                    d = mm(it)
-                    d["calls"] = [(n, x[:3] + [True, True], kw) for n, x, kw in d["calls"]]
+                if 2 * k + p in UPD_V[t]:
+                    apart(mm(it))
                     tt(xo, PS(ub), xs, ALU.add)
                 else:
                     mm2([(PS(ub), r_("ID"), xs)], it)
                     act(xo, PS(ub), AF.Identity)
-            for u, v, on in runs(k, PAR_V):
+            for u, v, on in runs(k, PAR_V[t]):
                 gx, ch = ind("XA", 0, a + 1024, "cw", 32 * u, 32 * v), r_("par", 512 * u, 512 * v)
-                if on: ts(ch, gx, -128.0, ALU.is_ge, -0.5, ALU.add)
+                if on: ts(ch, gx, -128.0, ALU.is_lt, -1.0, ALU.mult)
                 else: act(ch, gx, AF.Sign, 128.0)
             bank = 5 + k % 2
             mm2([(PS(bank, 0, 64), r_("ID32"), dw)], wrap(bank, 0, "Z1", "par", 1024 * k, 1024))
             c1, c2 = 64 * k, 64 * k + 64
             for u, v, sh in ((c1, min(c2, c0), 256 - c0), (max(c1, c0 + 1), c2, -c0)):
-                if u < v: ts(r_("O", u + sh, v + sh), PS(bank, u - c1, v - c1), 0.0, ALU.is_lt)
+                if u < v: mark(k, r_("O", u + sh, v + sh), PS(bank, u - c1, v - c1), -0.0625)
             if c1 <= c0 < c2:
                 for q, col in ((0, 8 + 2 * t), (256, 9 + 2 * t)):
-                    ts(r_("O", q, q + 1), PS(bank, c0 - c1, c0 - c1 + 1), 0.0, ALU.is_lt, pcol(col), ALU.mult)
-        for k in range(4):
-            act(r_("G4", 1024 * k, 1024 * k + 1024), ind("XA", OFF + lo, xa, "o4", 64 * k, 64 * k + 64), AF.Identity)
+                    mark(k, r_("O", q, q + 1), PS(bank, c0 - c1, c0 - c1 + 1), pcol(col))
+        if S4_LATE: offsets4()
+        for a, e in zip(G4_CUT[:-1], G4_CUT[1:]):
+            act(r_("G4", a, e), ind("XA", OFF + lo, xa, "o4", a // 16, e // 16), AF.Identity)
         if not last:
             act(r_("junk"), r_("DW", d0, d0 + 256), AF.Sign, -0.5, 1.0, r_("acc", t, t + 1))
             if t == 0: act(r_("junk", 0, 240), r_("DW", 16, 256), AF.Sign, -0.5, 1.0, r_("acc", 2, 3))
@@ -379,12 +412,12 @@ def program(rank):
         mm(wrap(2, 0, "Z1", "L1", 0, NS))
         scan(r_("E1", 0, 256), r_("mdB"), r_("I", 0, 256), ALU.max, ALU.min)
         ts(r_("of1", 0, nc), PS(2, 0, nc), 16.0, ALU.mult, 15.0, ALU.add)
-        scaled(r_("lb", 0, nc), PS(2, 0, nc), 16.0)
-        tt(r_("E0", 0, 257), PS(1, 0, 257), r_("I", 0, 257), ALU.add)
+        ts(r_("lb", 0, nc), PS(2, 0, nc), 16.0, ALU.mult)
+        tt(r_("E0", 0, 257), r_("I", 0, 257), PS(1, 0, 257), ALU.subtract)
         tt(r_("L2"), ind("E1", 0, 272, "of1", 0, nc), r_("kf"), ALU.is_le)
         mm2([(PS(3, 0, nc), r_("ID"), r_("lb", 0, nc))], wrap(3, 0, "Z1", "L2", 0, NS))
         cp(r_("of2", 0, nc), PS(3, 0, nc))
-        scaled(r_("lb", 48, 48 + nc), PS(3, 0, nc), 16.0)
+        ts(r_("lb", 48, 48 + nc), PS(3, 0, nc), 16.0, ALU.mult)
         X0 = float(OFF + lo + 16 * c0)
         ts(r_("ca", 0, nc), r_("kw", 0, nc), r_("I", 255 - c0, 256 - c0), ALU.is_ge, -float(W), ALU.mult)
         ts(r_("cb", 0, nc), r_("kw", 0, nc), r_("I", 256, 257), ALU.is_ge)
@@ -396,37 +429,49 @@ def program(rank):
         mm([(PS(4, 0, nc), r_("ID"), r_("lb", 48, 48 + nc))], False, False)
         mm(wrap(4, 0, "Z1", "L3", 0, NS), False, True)
         ts(r_("o", 0, nc), PS(4, 0, nc), X0, ALU.add)
-        scaled(r_("ofl", 0, nc), PS(4, 0, nc), 1.0, X0 - NONE)
+        scaled(r_("ofl", 0, nc), PS(4, 0, nc), 1.0, X0 - BASE)
         if last:
             it = [(PS(1, 0, 272), Z("Z1", s), r_("XA", OFF + lo + 272 * s, OFF + lo + 272 * s + 272)) for s in range(16)]
             mm2(it[:8], it[8:])
             ts(r_("oa32"), PS(1, 0, 272), 0.0, ALU.is_ge)
             dma("A", ext("ya", 0, W + S), r_("oa32"), 2.5)
             dma("A", ext("yx", W, W + S), r_("X", xa, xb), 2.5)
-        HALF = ((0, 17, 0, 0, 16, 0), (16, 34, 272, 304, 288, 18))
-        for hf, (oa, oe, at, main, moved, om) in enumerate(HALF):
+        for hf, (n, s0, oa, oe, at, main, moved, om) in enumerate(PARTS):
             out, gx = r_("dm", at, at + 16 * (oe - oa)), ind("D", 0, xa, "o", oa, oe)
             if DM_ACT[hf]: act(out, gx, AF.Identity)
             else: cp(out, gx)
-            trans(r_("V", 512 * hf, 512 * hf + 256), r_("dm", main, main + 256))
-            trans(r_("V", 512 * hf + 256, 512 * hf + 512), r_("dm", moved, moved + 256))
-            ts(r_("oj", 256 * hf, 256 * hf + 256), ind("V", 512 * hf, 512 * hf + 512, "LV", 16 * hf, 16 * hf + 16), 0.0, ALU.max)
-            act(r_("y", 512 * hf, 512 * hf + 256), ind("XA", 0, xa, "o", om, om + 16), AF.Identity)
-            act(r_("y", 512 * hf + 256, 512 * hf + 512), r_("y", 512 * hf, 512 * hf + 256), AF.Identity)
+            trans(r_("V", 2 * s0, 2 * s0 + n), r_("dm", main, main + n))
+            trans(r_("V", 2 * s0 + n, 2 * s0 + 2 * n), r_("dm", moved, moved + n))
+            ts(r_("oj", s0, s0 + n), ind("V", 2 * s0, 2 * s0 + 2 * n, "LV", s0 // 16, (s0 + n) // 16), 0.25, ALU.add, 0.0, ALU.max)
+            act(r_("y", 512 * hf, 512 * hf + n), ind("XA", 0, xa, "o", om, om + n // 16), AF.Identity)
+            k = n
+            while k < n * J_ROWS[hf]:
+                act(r_("y", 512 * hf + k, 512 * hf + 2 * k), r_("y", 512 * hf, 512 * hf + k), AF.Identity)
+                k *= 2
+        if not last:
+            mm(wrap(7, 0, "ZC", "C", TW + S * t, S))
+            scaled(r_("agw", 16 * t, 16 * t + 16), PS(7, 0, 16), -1.0, OFF + B + 255 + 64 - BASE)
+        mm([(PS(7, 128 * b, 128 * b + 128), colv(0), row(2 + S4_ACT[b], 128)) for b in range(2)], True, False)
         for k in range(8):
-            sb = 5 + k % 2
-            for j in range(2):
-                o2 = PS(sb, 256 * j, 256 * j + 256)
-                mm([(o2, r_("NID"), r_("X", xa, xb)), (o2, r_("ID"), r_("G4", 2 * k + j, W, 16))])
-            act(r_("S4", 512 * k, 512 * k + 512), PS(sb), AF.Sign, 0.5)
-            for j in range(2):
-                for it in count(7, "S4", 512 * k + 256 * j, 2 * k + j, True): mm([it])
-        youngest(0, 7, 3.0, 7, "c4", 0, r_("C", xa, xb))
+            sb, b, m0 = 5 + k % 2, k // 4, 4 * (k % 4)
+            on = m0 >= 16 - 2 * S4_ACT[b]
+            if not on and S4_TT:
+                if k == 0: mm([(PS(6, 0, S), r_("ID"), r_("X", xa, xb))])
+                for j in range(4):
+                    tt(r_("S4", 512 * k + 128 * j, 512 * k + 128 * j + 128), r_("G4", 2048 * b + m0 + j, 2048 * b + 2048, 16), PS(6, 128 * b, 128 * b + 128), ALU.is_ge)
+            else:
+                mm([(PS(sb, 128 * j, 128 * j + 128), r_("NID"), r_("X", xa + 128 * b, xa + 128 * b + 128)) for j in range(4)], True, False)
+                mm([(PS(sb, 128 * j, 128 * j + 128), r_("ID"), r_("G4", 2048 * b + m0 + j, 2048 * b + 2048, 16)) for j in range(4)], False, True)
+                if on: act(r_("S4", 512 * k, 512 * k + 512), PS(sb), AF.Sign, 0.5)
+                else: ts(r_("S4", 512 * k, 512 * k + 512), PS(sb), 0.0, ALU.is_ge)
+            w = r_("BH") if on else r_("BO", 0, 128, 16)
+            mm([(PS(7, 128 * b + m0 + j, 128 * b + 128, 16), r_("S4", 512 * k + 128 * j, 512 * k + 128 * j + 128), w) for j in range(4)], False, False).update(any=(t, 2), close=True)
+        youngest(0, S, 7, 11.0, 7, "c4", 0, r_("C", xa, xb), r_("C32", xa, xb) if C_ACT and not last else None)
         if not last:
             mm(wrap(7, 0, "ZC", "C", xa, S))
-            scaled(r_("h", 96, 112), r_("kw", 0, 16), 1.0, xa - NONE)
+            scaled(r_("h", 96, 112), r_("kw", 0, 16), 1.0, xa - BASE)
             hop(7, r_("h", 96, 112), r_("h", 112, 128), r_("w1"), t, 0)
-            left(0, 7, "c4", 0, r_("D", xa, xb))
+            left(0, S, 7, "c4", 0, r_("D", xa, xb))
             mm([(PS(7, 0, 1), r_("BOF"), r_("acc", t, t + 1))])
             if t == 0:
                 ts(r_("acc", 8, 9), PS(7, 0, 1), 0.5, ALU.mult, 2048.0, ALU.add)
@@ -436,52 +481,69 @@ def program(rank):
                 tt(r_("acc", 4, 5), PS(7, 0, 1), r_("acc", 3, 4), ALU.subtract)
                 ts(r_("acc", 9, 10), r_("acc", 4, 5), 0.5, ALU.mult, 128.0, ALU.add)
         na = 0
-        for hf, (oa, oe, at, main, moved, om) in enumerate(HALF):
-            y2, s0 = r_("y", 512 * hf, 512 * hf + 512), 256 * hf
-            mm([(PS(hf, 0, 256), colv(0), row(1 + hf))], True, False)
-            order = sorted(range(8), key=lambda j: (J_ACT[hf].index(j) + 0.5) / len(J_ACT[hf]) if j in J_ACT[hf] else ([x for x in range(8) if x not in J_ACT[hf]].index(j) + 0.4) / (8 - len(J_ACT[hf])))
-            for n, j in enumerate(order):
-                gx = ind("XA", 0, xa, "oj", s0 + 32 * j, s0 + 32 * j + 32)
-                ja = 4096 * hf + 512 * j
-                if j in J_ACT[hf]:
-                    gb = r_("G", 512 * (na % 8), 512 * (na % 8) + 512); sb = 2 + na % 2; na += 1
+        for hf, (n, s0, oa, oe, at, main, moved, om) in enumerate(PARTS):
+            rows, nc, c1 = J_ROWS[hf], n // 16, s0 // 16
+            wide, calls = rows * n, 16 // rows
+            y1, y2 = r_("y", 512 * hf, 512 * hf + n), r_("y", 512 * hf, 512 * hf + wide)
+            mm([(PS(hf, 0, n), colv(0), row(2 + J_ACT[t][hf], n))], True, False)
+            for j in range(calls):
+                gx = ind("XA", 0, xa, "oj", s0 + j * wide // 16, s0 + (j + 1) * wide // 16)
+                ja = 16 * s0 + wide * j
+                on = j >= calls - J_ACT[t][hf]
+                if on:
+                    gb = r_("G", 512 * (na % 8), 512 * (na % 8) + wide); sb = PS(J_BANK[na % len(J_BANK)], 0, wide); na += 1
                     act(gb, gx, AF.Identity)
-                    mm2([(PS(sb), r_("NID"), y2)], [(PS(sb), r_("ID"), gb)])
-                    act(r_("J", ja, ja + 512), PS(sb), AF.Sign, 0.5)
+                    mm2([(sb, r_("NID"), y2)], [(sb, r_("ID"), gb)])
+                    act(r_("J", ja, ja + wide), sb, AF.Sign, 0.5)
                 else:
-                    tt(r_("J", ja, ja + 512), gx, y2, ALU.is_ge)
-                mm([it for i in range(2) for it in count(hf, "J", ja + 256 * i, 2 * j + i, j in J_ACT[hf])], False, n == 7)
-            youngest(1 + hf, hf, 11.0, 4, "dm", main, r_("crow", s0, s0 + 256))
-            cp(ind("C", 0, xa, "o", om, om + 16), r_("crow", s0, s0 + 256))
-            mm(wrap(hf, 0, "ZB", "crow", s0, 256))
-            tt(r_("obf", 16 * hf, 16 * hf + 16), PS(hf, 0, 16), r_("ofl", om, om + 16), ALU.min)
-            ts(r_("ob", 16 * hf, 16 * hf + 16), r_("obf", 16 * hf, 16 * hf + 16), NONE, ALU.add)
-            act(r_("xb", s0, s0 + 256), ind("XA", 0, xa, "ob", 16 * hf, 16 * hf + 16), AF.Identity)
-            halved(hf, r_("y", 512 * hf, 512 * hf + 256), r_("xb", s0, s0 + 256), r_("nx", s0, s0 + 256))
-            cp(ind("X", 0, xa, "o", om, om + 16), r_("nx", s0, s0 + 256))
+                    tt(r_("J", ja, ja + wide), gx, y2, ALU.is_ge)
+                mm([it for i in range(rows) for it in count(hf, "J", ja + n * i, n, rows * j + i, on)], False, False).update(any=(t, hf), close=True)
+            youngest(S + s0, n, hf, 11.0, K_BANK[t][hf], "dm", main, r_("crow", s0, s0 + n), r_("crow32", s0, s0 + n) if C_ACT and not last else None, QUICK[hf])
+            if C_ACT and not last: act(ind("C32", 0, xa, "o", om, om + nc), r_("crow32", s0, s0 + n), AF.Silu)
+            else: cp(ind("C", 0, xa, "o", om, om + nc), r_("crow", s0, s0 + n))
+            mm(wrap(hf, 0, "ZB", "crow", s0, n))
+            tt(r_("obf", c1, c1 + nc), PS(hf, 0, nc), r_("ofl", om, om + nc), ALU.min)
+            ts(r_("ob", c1, c1 + nc), r_("obf", c1, c1 + nc), BASE, ALU.add)
+            gx = ind("XA", 0, xa, "ob", c1, c1 + nc)
+            if QUICK[hf]:
+                tt(r_("sm", 0, n), gx, y1, ALU.add)
+                ts(r_("sm", 512, 512 + n), r_("sm", 0, n), 1, ALU.arith_shift_right)
+                cp(ind("X", 0, xa, "o", om, om + nc), r_("sm", 512, 512 + n))
+            else:
+                act(r_("xb", s0, s0 + n), gx, AF.Identity)
+                halved(hf, y1, r_("xb", s0, s0 + n), r_("nx", s0, s0 + n))
+                cp(ind("X", 0, xa, "o", om, om + nc), r_("nx", s0, s0 + n))
         if last:
             dma("S", ext("yx", 0, W), r_("X", OFF + lo, xa), 5.0)
             it = [(PS(7, 0, 272), Z("ZC", s), r_("C", OFF + lo + 272 * s, OFF + lo + 272 * s + 272)) for s in range(16)]
-            mm2(it[:8], it[8:])
-            act(r_("oc32"), PS(7, 0, 272), AF.Identity, -1.0)
+            mm(it[:5], True, False); mm(it[5:10], False, False); mm(it[10:15], False, False); mm(it[15:], False, True)
+            ts(r_("oc32"), PS(7, 0, 272), BASE - OFF, ALU.add, -1.0, ALU.max)
             dma("A", ext("yc", 0, W + S), r_("oc32"), 2.5)
             break
-        if Q_ACT: act(r_("gC"), ind("C", 0, xb, "w1", 0, 16), AF.Identity)
-        else: cp(r_("gC"), ind("C", 0, xb, "w1", 0, 16))
+        act(r_("gC"), ind("C32" if C_ACT else "C", 0, xb, "w1", 0, 16), AF.Identity)
         mm(wrap(4, 0, "ZC", "gC", 0, S))
         hop(4, r_("h", 112, 128), r_("h", 96, 112), r_("w2"), t, 1)
         zs, z = "zs%d" % t, "z%d" % t
         if Q_ACT > 1: act(r_(zs), ind("X", 0, xb, "w2", 0, 16), AF.Identity)
         else: cp(r_(zs), ind("X", 0, xb, "w2", 0, 16))
-        add("G", "send", [t], {}, [r_(zs)], [("snd", t, t + 1, 1, None, None)], 1.0, lat=4.0, nosem=True)
+        add("G", "send", [t], {}, [r_(zs)], [("snd", t, t + 1, 1, None, None)], 1.0, lat=5.0, nosem=True)
         cp(r_(z, 32 * rank, 32 * rank + 32), r_(zs, 32 * rank, 32 * rank + 32))
-        who(t + 1, 2)
+        who(t + 1, 4)
+        for k in range(2 * EARLY):
+            a, gb = OFF + lo + S + 512 * k, r_("G", 512 * k, 512 * k + 512)
+            if k % 2 == 0: act(r_("G", 512 * k, 512 * k + 1024), ind("cm", S * t + S, S * t + 2 * S, "who", 32 * k, 32 * k + 64), AF.Identity)
+            mm2([(PS(1 - k % 2), r_("ID2"), r_("X", a, a + 512))], [(PS(1 - k % 2), r_("NID"), gb)])
+            act(r_("J", 512 * k, 512 * k + 512), PS(1 - k % 2), AF.Identity)
+        if C_ACT:
+            for n, s0, oa, oe, at, main, moved, om in PARTS:
+                cp(ind("C", 0, xa, "o", om, om + n // 16), r_("crow", s0, s0 + n))
         for k in range(2):
             mm(wrap(2 + k, 0, "ZC", "C", OFF + lo + S + 2048 * k, 2048))
-            ts(r_("cw", 128 * k, 128 * k + 128), PS(2 + k, 0, 128), NONE, ALU.add)
-        for hf, (oa, oe, at, main, moved, om) in enumerate(HALF):
-            left(1 + hf, 6 + hf, "dm", main, r_("left", 256 * hf, 256 * hf + 256))
-            cp(ind("D", 0, xa, "o", om, om + 16), r_("left", 256 * hf, 256 * hf + 256))
+            ts(r_("cw", 128 * k, 128 * k + 128), PS(2 + k, 0, 128), BASE, ALU.add)
+        for hf, (n, s0, oa, oe, at, main, moved, om) in enumerate(PARTS):
+            left(S + s0, n, 6 + hf, "dm", main, r_("left", s0, s0 + n), QUICK[hf])
+            if D_ACT: act(ind("D", 0, xa, "o", om, om + n // 16), r_("left", s0, s0 + n), AF.Silu)
+            else: cp(ind("D", 0, xa, "o", om, om + n // 16), r_("left", s0, s0 + n))
         mset(r_("XA", OFF + lo, OFF + lo + S), -256.0)
     return ops
 
@@ -503,6 +565,7 @@ def schedule(ops):
         if "arr" in o:
             for p in ops[:i]:
                 if p["calls"][0][0] == "send" and p["calls"][0][1][0] == o["arr"]: dep[p["i"]] = False
+        if o.get("behind"): dep[i - 1] = None
         for acc, w in [(x, False) for x in o["rd"]] + [(x, True) for x in o["wr"]]:
             b = acc[0]
             ps = is_psum(b)
@@ -511,6 +574,7 @@ def schedule(ops):
                 p = ops[j]
                 dmaish = "sem" in p or "sem" in o
                 same = p["q"] == o["q"] and not dmaish
+                if "any" in o and o["any"] == p.get("any"): continue
                 if ps:
                     if same and not (w or w2): continue
                 elif not (w or w2) or not meet(run, acc[1:]): continue
@@ -519,7 +583,7 @@ def schedule(ops):
         for acc, w in [(x, False) for x in o["rd"]] + [(x, True) for x in o["wr"]]:
             b, a, e, st = acc
             lst = seen.setdefault(b, [])
-            if w: lst[:] = [x for x in lst if not (is_psum(b) or (st == 1 and a <= x[0][0] and x[0][1] <= e)) or x[1] == i]
+            if w and "any" not in o: lst[:] = [x for x in lst if not (is_psum(b) or (st == 1 and a <= x[0][0] and x[0][1] <= e)) or x[1] == i]
             lst.append((acc[1:], i, w))
         o["dep"] = dep
     if "t0" not in KEPT:
@@ -531,10 +595,10 @@ def schedule(ops):
 KEPT = {}
 
 
-def place(seq, before, q, dur):
-    t, busy = {}, {}
+def place(seq, before, q, dur, free, held):
+    t, busy = {}, {k: list(v) for k, v in held.items()}
     for i in seq:
-        t0 = 0.0
+        t0 = free[i]
         for j, gap in before[i]:
             if t[j] + gap > t0: t0 = t[j] + gap
         iv = busy.setdefault(q[i], [])
@@ -554,39 +618,97 @@ def place(seq, before, q, dur):
 def best_times(ops):
     n = len(ops)
     q = [o["q"] for o in ops]; dur = [o["dur"] for o in ops]; lat = [o["lat"] for o in ops]
-    fw = [[] for _ in ops]; bw = [[] for _ in ops]
+    fw = [[] for _ in ops]
     for o in ops:
         for j, need in o["dep"].items():
-            extra = lat[j] + (LAT if need else 0.0)
-            fw[o["i"]].append((j, dur[j] + extra)); bw[j].append((o["i"], dur[o["i"]] + extra))
-    bw0 = [bw[i] + [(-1, lat[i])] for i in range(n)]
+            fw[o["i"]].append((j, dur[j] + (0.0 if need is None else lat[j]) + (LAT if need else 0.0)))
     bl = [dur[i] + lat[i] for i in range(n)]
     for i in reversed(range(n)):
         for j, gap in fw[i]: bl[j] = max(bl[j], gap + bl[i])
     rng = np.random.RandomState(SEED)
-    best, bt, key = 1e9, None, [-x for x in bl]
-    for it in range(ROUNDS):
-        k2 = list(key)
-        for i in range(n):
-            for j, gap in fw[i]:
-                if k2[j] + 1e-6 > k2[i]: k2[i] = k2[j] + 1e-6
-        t = place(sorted(range(n), key=lambda i: k2[i]), fw, q, dur)
-        span = max(t[i] + dur[i] + lat[i] for i in range(n))
-        if span < best: best, bt = span, t
-        if it == 0 or span < cur + TEMP * (1.0 - it / ROUNDS) * rng.rand():
-            cur, ct = span, t
-            tb = place([-1] + sorted(range(n), key=lambda i: (-(ct[i] + dur[i]), -i)), bw0 + [[]], q + ["-"], dur + [0.0])
-            late = [cur - (tb[i] + dur[i]) for i in range(n)]
-        a, w, amp, mix = rng.rand() * cur, 2.0 + 12.0 * rng.rand(), 4.0 * rng.rand(), float(rng.choice([0.0, 0.5, 1.0]))
-        noise = rng.rand(n) * amp
-        key = [(mix * late[i] + (1 - mix) * ct[i] + float(noise[i])) if a - w <= ct[i] <= a else ct[i] for i in range(n)]
-    return bt
+    part, sent = [R - 1] * n, 0
+    for i in reversed(range(n)):
+        if ops[i]["calls"][0][0] == "send": part[i] = ops[i]["calls"][0][1][0]
+        for j, gap in fw[i]: part[j] = min(part[j], part[i])
+    done, held, end = {}, {}, 0.0
+    durs = [[o["dur"] if o["calls"][0][0] in ("send", "dma_start") else f * (o["dur"] + CY * (o["gathers"] * (g - GATH) + o["scatters"] * (s - SCAT))) for o in ops] for f, g, s in OTHERS]
+    dones = [{} for _ in OTHERS]
+    for r in range(R):
+        ids = [i for i in range(n) if part[i] == r]
+        near = [i for i in done if done[i] + dur[i] > end]
+        both = set(ids + near)
+        deps = [{i: [(j, gap - dur[j] + d[j]) for j, gap in fw[i] if j in both] for i in both} for d in durs]
+        frees = [{i: max([x.get(i, 0.0)] + [x[j] + gap - dur[j] + d[j] for j, gap in fw[i] if j not in both]) for i in both} for d, x in zip(durs, dones)]
+        def replay(t):
+            seq = sorted(near + ids, key=lambda i: (t[i] if i in t else done[i], i))
+            out = []
+            for d, dep, fr in zip(durs, deps, frees):
+                x, at = {}, {}
+                for i in seq:
+                    t0 = max(fr[i], at.get(q[i], 0.0))
+                    for j, gap in dep[i]:
+                        if x[j] + gap > t0: t0 = x[j] + gap
+                    x[i] = t0; at[q[i]] = t0 + d[i]
+                out.append(x)
+            return out
+        free = {i: max([0.0] + [done[j] + gap for j, gap in fw[i] if j in done]) for i in ids}
+        inner = {i: [(j, gap) for j, gap in fw[i] if j not in done] for i in ids}
+        after = {i: [] for i in ids}
+        for i in ids:
+            for j, gap in inner[i]: after[j].append((i, gap - dur[j] + dur[i]))
+        zero = {i: lat[i] for i in ids}
+        first = min(free.values())
+        best, bt, key = 1e9, None, {i: -bl[i] for i in ids}
+        for it in range(ROUNDS):
+            for i in ids:
+                for j, gap in inner[i]:
+                    if key[j] + 1e-6 > key[i]: key[i] = key[j] + 1e-6
+            t = place(sorted(ids, key=key.get), inner, q, dur, free, held)
+            span = max(t[i] + dur[i] + lat[i] for i in ids)
+            score = 1e9
+            if it == 0 or span < cur + 1.5:
+                xs = replay(t)
+                score = (span + sum(max(x[i] + d[i] + lat[i] for i in ids) / f[0] for x, d, f in zip(xs, durs, OTHERS))) / (1 + len(OTHERS))
+            if score < best: best, bt, bx, bspan = score, t, xs, span
+            if it == 0 or score < held_score + TEMP * (1.0 - it / ROUNDS) * rng.rand():
+                cur, ct, held_score = span, t, score
+                tb = place(sorted(ids, key=lambda i: (-(ct[i] + dur[i]), -i)), after, q, dur, zero, {})
+                late = {i: cur - (tb[i] + dur[i]) for i in ids}
+                ends = {(q[i], round(ct[i] + dur[i], 6)): i for i in ids}
+                i, behind = max(ids, key=lambda i: ct[i] + dur[i] + lat[i]), []
+                while i is not None:
+                    j = next((j for j, gap in inner[i] if ct[j] + gap > ct[i] - 1e-7), None)
+                    if j is None:
+                        j = ends.get((q[i], round(ct[i], 6)))
+                        if j is not None: behind.append((j, i))
+                    i = j
+            if behind and rng.rand() < 0.5:
+                u, v = behind[rng.randint(len(behind))]
+                key, step = dict(ct), 0.01 + 3.0 * rng.rand() ** 3
+                if rng.rand() < 0.5: key[u] = ct[v] + step
+                else:
+                    key[v] = ct[u] - step
+                    for i in reversed(ids):
+                        for j, gap in inner[i]:
+                            if key[j] > key[i] - gap: key[j] = key[i] - gap
+                continue
+            a, w, amp, mix = first + rng.rand() * (cur - first), 1.0 + 12.0 * rng.rand(), 4.0 * rng.rand() ** 2, float(rng.choice([0.0, 0.5, 1.0]))
+            noise = (rng.rand(n) * amp).tolist()
+            key = {i: (mix * late[i] + (1 - mix) * ct[i] + noise[i]) if a - w <= ct[i] <= a else ct[i] for i in ids}
+        done.update(bt)
+        for x, y in zip(dones, bx): x.update(y)
+        for i in ids: held.setdefault(q[i], []).append((bt[i], bt[i] + dur[i]))
+        end = min(bt[i] for i in ids if lat[i] + bt[i] + dur[i] >= bspan - 1e-9) - 8.0
+        held = {k: [(0.0, end)] + sorted((max(u, end), v) for u, v in iv if v > end) for k, iv in held.items()}
+    return done
 
 
 def plan(rank):
     ops = program(rank)
     order = schedule(ops)
     pos, n = {}, {}
+    for o in {o["any"]: o for o in order if o.get("close")}.values():
+        o["calls"][-1][1][4] = True
     for o in order:
         n[o["q"]] = n.get(o["q"], 0) + 1
         o["pos"] = n[o["q"]]
@@ -664,6 +786,7 @@ def rank_program(g, core, T, topo):
             elif name == "memset": ins = e.memset(*a)
             elif name == "activation": ins = e.activation(*a, **k)
             elif name == "iota": ins = e.iota(*a, **k)
+            elif name == "affine_select": ins = e.affine_select(*a)
             elif name == "matmul": ins = e.matmul(*a)
             elif name == "dma_start": ins = e.dma_start(*a)
         if "sem" in o: ins.then_inc(sem_of(o), 16)

@@ -5,47 +5,59 @@ from concourse.mybir import AluOpType as ALU, AxisListType as AX, ActivationFunc
 W, S, R, CAP, ST, N = 4096, 256, 3, 512, 683, 8
 OFF = 544
 TW = OFF + W + R * S
-BASE = OFF - 129.0
+BASE = float(OFF)
+DZ = OFF + 2040
 MAGIC = 3 * 2 ** 22
 BIG = 100000.0
-NS = 544
+NS = 560
 S3_ACT = ((), (4,), (4,))
-UPD_V = ((4, 6, 7), (4, 6, 7), (4, 6, 7))
+UPD_V = ((3, 4, 5, 7),) * 3
 PAR_V = ((5, 7), (3, 5, 7), (3, 5, 7))
-NA = 256
-J_ROWS = (2, 2)
-J_ACT = ((2, 2), (2, 2), (2, 3))
-S4_ACT = (4, 8)
+PARTS = ((0, 256), (256, 256))
+OJ_CUT, G_ROWS, SPLIT = (0, 22, 32), 1, 2
+J_ACT = ((4, 6), (4, 6), (4, 6))
+S4_ACT = (8, 16)
 QUICK = (False, False)
-O_ACT = (0, 1, 2)
+O_ACT = (0,)
 S4_LATE = 0
 C_ACT, D_ACT, C32_PS = False, False, True
 S4_TT = True
+HI_V = False
+WHO0 = (0, 64, 128, 192, 256)
+PAR_BANK = (5, 6, 0, 1)
+H1, H2 = 0, 0
+S4_END = 3
+CUT2, CUT3 = ((0, 35),), ((0, 18), (18, 35))
+Y_V = True
+U_A = 8
+LEAD = (0.0, 0.0)
+NX_V = ()
 EARLY = 1
-J_BANK, K_BANK = (2, 3), ((4, 6), (4, 6), (4, 4))
-G4_CUT = (0, 2048, 3072, 4096)
-DW_ACT, DM_ACT, Q_ACT = True, (False, True), 1
+D_CUT = 16
+J_BANK, K_BANK = (2, 3), ((4, 4), (4, 4), (4, 5))
+G4_CUT = (0, 2048, 4096)
+DW_ACT, DM_ACT, Q_ACT = True, (False, False), 2
 SAME_QUEUE_WAW = True
 
 F, B16, I32, U16 = "float32", "bfloat16", "int32", "uint16"
 SCRATCH = {}
 for _n, _c, _d in [
-    ("X", TW, B16), ("XA", TW, B16), ("C", TW + 512, B16), ("D", TW, F), ("DW", 304, B16),
+    ("X", TW, B16), ("XA", TW, B16), ("C", TW + 512, B16), ("D", TW, I32), ("DW", 304, B16),
     ("cm", 768, B16), ("z0", 256, B16), ("z1", 256, B16), ("zs0", 256, B16), ("zs1", 256, B16),
-    ("dli", 2048, I32), ("cdi", 288, I32), ("cdf", 304, F), ("cdh", 304, B16), ("cdl", 304, B16), ("cd32", 512, F), ("C32", TW, F), ("crow32", 512, F),
+    ("cdi", 288, I32), ("cdf", 304, F), ("cdh", 304, B16), ("cdl", 304, B16),
     ("pi", 16, I32), ("pc", 24, F), ("ia", 256, F), ("ib", 128, F), ("ic", 384, F), ("kf", NS, F), ("ku", NS, U16), ("kw", 48, F),
-    ("Z1", 144, B16), ("ZC", 144, B16), ("ZB", 144, B16), ("BH", 8, B16), ("N8K", 128, B16), ("HID", 128, B16), ("Rl", 768, B16), ("xb", 512, B16), ("nx", 512, B16), ("mu", 16, F), ("zb", 1480, B16), ("U", 2048, B16),
+    ("Z1", 144, B16), ("ZC", 144, B16), ("ZB", 144, B16), ("BH", 8, B16), ("N8K", 128, B16), ("HID", 128, B16), ("Rl", 768, B16), ("xb", 512, B16), ("nx", 512, B16), ("mu", 16, F), ("od", 48, U16), ("U", 2048, B16),
     ("BO", 128, B16), ("BOF", 128, F), ("ID", 128, B16), ("NID", 128, B16), ("ID32", 128, B16), ("IDF", 128, F), ("SU", 128, B16),
-    ("rows", 2816, B16), ("col", 384, B16), ("mdB", 256, F), ("m0", 384, F), ("P8K", 128, B16), ("ID2", 128, B16), ("sm", 1024, I32), ("pw", 256, F), ("zer", 864, F), ("LVf", 16, F), ("LV", 48, U16),
+    ("rows", 4096, B16), ("col", 384, B16), ("mdB", 256, F), ("m0", 512, F), ("ID2", 128, B16), ("LVk", 32, F), ("pw", 256, F), ("zer", 272, F), ("LVf", 16, F), ("LV", 48, U16),
     ("wi", 256, I32), ("wj", 256, I32), ("who", 256, U16),
     ("cmp", 4096, B16), ("par", 4096, B16), ("G", 4096, B16), ("G4", 4096, B16), ("S4", 4096, B16), ("J", 8192, B16),
     ("sq4", 256, F), ("i4a", 256, I32), ("i4b", 256, I32), ("c4", 256, F), ("o4", 256, U16),
     ("V4s", 768, F), ("cn", 48, F), ("V5", 768, B16), ("crow", 512, B16),
     ("cw", 256, U16), ("junk", 256, B16), ("acc", 16, F), ("O", 272, B16), ("I", 272, F), ("M", 256, F),
     ("E0", 272, F), ("E1", 272, F), ("e2", 16, F), ("L1", NS, B16), ("L2", NS, B16), ("L3", NS, B16), ("lb", 96, B16),
-    ("of1", 48, U16), ("of2", 48, U16), ("ca", 48, F), ("cb", 48, F), ("cc", 48, F), ("cd", 48, F), ("corr", 48, F),
-    ("o", 48, U16), ("ofl", 48, F), ("dm", 560, F), ("V", 1024, F), ("oj", 512, U16), ("y", 1024, B16),
-    ("obf", 32, F), ("ob", 32, U16), ("left", 512, F),
+    ("of1", 48, U16), ("of2", 48, U16), ("ca", 48, B16), ("cb", 48, F), ("cc", 48, F), ("cd", 48, F), ("hz", 32, F),
+    ("o", 48, U16), ("ofl", 48, F), ("dm", NS, F), ("V", 1024, F), ("oj", 512, U16), ("y", 1024, B16),
+    ("obf", 32, F), ("ob", 32, U16), ("left", 512, I32),
     ("agw", 32, F), ("h", 128, F), ("w1", 16, U16), ("w2", 16, U16), ("gC", 256, B16), ("oc32", 272, F), ("oa32", 272, F),
 ]:
     SCRATCH[_n] = ("sbuf", [128, _c], _d)
@@ -54,10 +66,11 @@ for _k in range(8):
 NDMA = 48
 SEMAPHORES = ["qV", "qA", "qP", "qG", "arr0", "arr1", "sent"] + ["dma%d" % _k for _k in range(NDMA)]
 
-CY, PCY, LAT = 0.00083, 0.00042, 0.12
+CY, PCY, LAT = 0.00083, 0.0005, 0.13
 GATH, SCAT = 1.56, 3.8
-OTHERS = ((1.3, 1.15, 2.0), (1.3, 2.0, 5.5))
-SEED, ROUNDS, TEMP = 1, 7000, 0.3
+SEND, DMA, FIXA = 3.2, 0.75, 0.1
+OTHERS = ((1.2, 1.15, 2.0, 2.0), (1.35, 2.0, 5.5, 5.0), (1.3, 1.7, 4.5, 4.0))
+SEED, ROUNDS, TEMP = 1, 21000, 0.4
 
 
 def sends(T, topo, core):
@@ -84,7 +97,8 @@ def bits(m):
 
 def program(rank):
     ops, table = [], []
-    PARTS = ((NA, 0, 0, NA // 16 + 1, 0, 0, 16, 0), (CAP - NA, NA, NA // 16, NS // 16, NA + 16, NA + 48, NA + 32, NA // 16 + 2))
+    RW = max(n for s0, n in PARTS + ((0, S),))
+    signed = sorted(set(sum(J_ACT, ()) + S4_ACT))
 
     def r_(b, a=0, e=None, st=1, p=None):
         return (b, a, SCRATCH[b][1][1] if e is None else e, st, p, None)
@@ -116,7 +130,7 @@ def program(rank):
     def vdur(out, ins, base):
         if out[5]: return 0.05 + cnt(out) * SCAT * CY
         if ins[0][5]: return 0.05 + cnt(out) * GATH * CY
-        return 0.01 + max(64, cnt(ins[0]) * base) * CY
+        return 0.015 + max(64, cnt(ins[0]) * base) * CY
 
     def half(*xs):
         return 0.5 if all(two(x) for x in xs) else 1.0
@@ -132,7 +146,7 @@ def program(rank):
     def act(out, a, f, bias=0.0, scale=1.0, acc=None):
         kw = {} if out[5] else {"bias": bias, "scale": scale}
         if acc: kw["accum_out"] = acc
-        dur = 0.065 + cnt(out) * (SCAT if out[5] else GATH if a[5] else 1.0) * CY
+        dur = (0.065 if a[5] else FIXA) + cnt(out) * (GATH if a[5] else 1.0) * CY
         if f == AF.Silu and not table:
             table.append(f); dur += 1.3
         return add("A", "activation", [out, a, f], kw, [a, bias, scale], [out] + ([acc] if acc else []), dur)
@@ -161,11 +175,11 @@ def program(rank):
         rd = [a] if a[0] in SCRATCH else []
         wr = [out] if out[0] in SCRATCH else []
         nd[0] += 1
-        return add(q, "dma_start", [out, a], {}, rd, wr, 0.1, lat=us, sem="dma%d" % nd[0])
+        return add(q, "dma_start", [out, a], {}, rd, wr, 0.1, lat=us * DMA, sem="dma%d" % nd[0])
     def ext(b, a, e): return (b, a, e, 1, None, None)
     def Z(name, r): return r_(name, 15 - r, 143 - r)
     def PS(k, a=0, e=512, st=1): return r_("P%d" % k, a, e, st)
-    def row(k, n): return r_("rows", 256 * k, 256 * k + n, 1, (0, 1, 1))
+    def row(k, n): return r_("rows", 512 * k, 512 * k + n, 1, (0, 1, 1))
     def colv(k): return r_("col", 128 * k, 128 * k + 128, 1, (0, 1, 1))
     def wrap(bank, c0, zname, buf, a, n):
         return [(PS(bank, c0, c0 + n // 16), Z(zname, r), r_(buf, a + r, a + n, 16)) for r in range(16)]
@@ -174,7 +188,7 @@ def program(rank):
     cG, cR, cCo = pcol(0), pcol(1), pcol(2)
 
     def xload(k): return r_("X", OFF + 1024 * k, OFF + 1024 * k + 1024), ext("x0", 1024 * k, 1024 * k + 1024)
-    for q, loads in (("S", [xload(0) + (2.6,), (r_("cdi", 0, 256), ext("cd0", 0, W), 3.6), xload(2) + (4.5,), (r_("cdi", 256, 288), ext("age", 0, 512), 5.5), (r_("dli"), ext("dl0", 0, 2048), 9.5)]),
+    for q, loads in (("S", [xload(0) + (2.6,), (r_("cdi", 0, 256), ext("cd0", 0, W), 3.6), xload(2) + (4.5,), (r_("cdi", 256, 288), ext("age", 0, 512), 5.5), (r_("D", OFF + 2048, OFF + W), ext("dl0", 0, 2048), 9.5)]),
                      ("A", [(r_("cm", 0, S), ext("come", 0, S), 2.3), xload(1) + (3.5,), xload(3) + (5.3,), (r_("cm", S, 768), ext("come", S, 768), 6.0)])):
         for n, (out, a, us) in enumerate(loads):
             dma(q, out, a, us).update(behind=n > 0)
@@ -192,19 +206,20 @@ def program(rank):
     scaled(r_("pw"), r_("pw"), 1.0, pcol(5))
     one = (0, 32, 1)
     fill(r_("rows", 0, 256, 1, one), 1)
+    if RW > 256: fill(r_("rows", 256, RW, 1, one), 1)
     mset(r_("col", 128, 256, 1, one), -0.25)
     fill(r_("col", 256, 384, 1, one), MAGIC)
     iota(r_("M", 0, 128), [[1, 128]], 0, -1)
     ts(r_("ID"), r_("M", 0, 128), 0.0, ALU.is_equal)
-    for nme, w in (("HID", 0.5), ("NID", -1.0), ("ID32", 32.0), ("IDF", 1.0), ("N8K", -8192.0), ("P8K", 8192.0), ("ID2", 2.0)):
-        scaled(r_(nme), r_("ID"), w)
+    for nme, w in (("HID", 0.5), ("NID", -1.0), ("ID32", 32.0), ("IDF", 1.0), ("N8K", -8192.0), ("ID2", 2.0)):
+        ts(r_(nme), r_("ID"), w, ALU.mult)
     iota(r_("ib"), [[16, 8], [0, 16]], 0, 0)
     ts(r_("BO"), r_("ib"), cG, ALU.is_equal)
     scaled(r_("BOF"), r_("BO"), 1.0)
     iota(r_("LVf"), [[1, 16]], 0, 0)
     ts(r_("mu"), r_("LVf"), cR, ALU.is_equal, -512.0, ALU.mult)
     for r in range(16):
-        if r % 2: ts(r_("U", 128 * r, 128 * r + 128), r_("BO"), r_("mu", r, r + 1), ALU.mult)
+        if r % U_A: ts(r_("U", 128 * r, 128 * r + 128), r_("BO"), r_("mu", r, r + 1), ALU.mult)
         else: scaled(r_("U", 128 * r, 128 * r + 128), r_("BO"), r_("mu", r, r + 1))
     select(r_("SU"), r_("BO"), [[-1, 128]], ALU.is_gt, 0.0, 0, 1)
     iota(icol(4), [[0, 1]], 256, 16)
@@ -216,15 +231,11 @@ def program(rank):
     tt(icol(10), icol(6), icol(7), ALU.subtract)
     tt(pcol(6), icol(10), icol(9), ALU.add)
     ts(r_("LV", 0, 16), r_("LVf"), pcol(6), ALU.add)
-    tt(icol(11), icol(6), icol(7), ALU.add)
-    ts(icol(12), icol(11), 255, ALU.bitwise_and)
-    tt(pcol(7), icol(12), icol(9), ALU.add)
-    ts(r_("LV", 16, 32), r_("LVf"), pcol(7), ALU.add)
-    ts(r_("cdf", 0, 256), r_("cdi", 0, 256), 65.0, ALU.add)
-    ts(r_("cdf", 256, 272), r_("cdi", 0, 16), 65.0, ALU.add)
+    cp(r_("cdf", 0, 256), r_("cdi", 0, 256))
+    cp(r_("cdf", 256, 272), r_("cdi", 0, 16))
     trans(r_("V", 0, 256), r_("cdf", 0, 256))
     trans(r_("V", 256, 512), r_("cdf", 16, 272))
-    ts(r_("cw"), ind("V", 0, 512, "LV", 0, 16), BASE + 64, ALU.add)
+    ts(r_("cw"), ind("V", 0, 512, "LV", 0, 16), BASE, ALU.add)
     fill(r_("XA", 0, OFF), -1)
     fill(r_("DW", 256, 304), 0)
     scaled(cCo, cR, 61.0, 7.0)
@@ -232,11 +243,11 @@ def program(rank):
         fill(pcol(16 + t), ST * (t + 1) % 16)
     ts(r_("pc", 8, 14, 2), r_("pc", 16, 19), cR, ALU.is_le, -0.0625, ALU.mult)
     ts(r_("pc", 9, 14, 2), r_("pc", 16, 19), cR, ALU.is_gt, -0.0625, ALU.mult)
-    fill(r_("zer"), 0); fill(r_("zb", 0, 740), 0); fill(r_("zb", 740, 1480), 0)
+    fill(r_("zer"), 0); fill(r_("hz"), 0); fill(r_("D", DZ, DZ + 8), -1)
     iota(r_("ic", 0, 256), [[0, 16], [1, 16]], 0, 0)
-    fill(r_("m0", 0, 256), 1); fill(r_("m0", 0, 256, 16), 0)
+    fill(r_("m0", 0, RW), BIG); fill(r_("m0", 0, RW, 16), -1)
     ts(r_("mdB"), r_("ic", 0, 256), cR, ALU.is_equal, BIG, ALU.mult)
-    for a, e, b in ((0, NA, 0), (NA, NA + 16, 0), (NA + 16, NA + 32, CAP - 16), (NA + 32, NS, NA)):
+    for a, e, b in ((0, 256, 0), (256, 288, 0), (288, 544, 256), (544, NS, 256)):
         iota(r_("kf", a, e), [[1, e - a]], b, 0)
         iota(r_("ia", 144 + a // 16, 144 + e // 16), [[16, (e - a) // 16]], b, 0)
     cp(r_("ku"), r_("kf"))
@@ -245,51 +256,39 @@ def program(rank):
     scaled(r_("BH"), r_("BO", 0, 128, 16), 0.5)
     ts(pcol(14), cR, 2.0, ALU.is_lt)
     ts(pcol(15), cR, 3.0, ALU.is_lt)
-    scaled(r_("ZC"), r_("Z1"), pcol(14))
-    scaled(r_("ZB"), r_("Z1"), pcol(15))
+    ts(r_("ZC"), r_("Z1"), pcol(14), ALU.mult)
+    ts(r_("ZB"), r_("Z1"), pcol(15), ALU.mult)
     fill(r_("col", 0, 128, 1, one), 1)
-    fill(r_("rows", 256, 512, 1, one), 8)
-    for k in sorted(set(sum(J_ACT, ()) + S4_ACT)):
-        select(r_("rows", 512 + 256 * k, 768 + 256 * k, 1, one), r_("rows", 256, 512, 1, one), [[0, 16], [1, 16]], ALU.is_ge, 0.0, 2 * k - 16, 0)
-    for k in range(4):
-        dma("S", r_("C", 1480 * k, 1480 * k + 1480), r_("zb"), 4.0 + k)
-    dma("S", r_("X", 0, OFF), r_("zb", 0, OFF), 4.0)
-    for k in range(3):
-        dma("S", r_("D", 864 * k, 864 * k + 864), r_("zer"), 5.0 + k)
+    fill(r_("rows", 512, 512 + RW, 1, one), 8)
+    for j, k in enumerate(signed):
+        n = RW if k in sum(J_ACT, ()) else 128
+        select(r_("rows", 1024 + 512 * j, 1024 + 512 * j + n, 1, one), r_("rows", 512, 512 + n, 1, one), [[0, n // 16], [1, 16]], ALU.is_ge, 0.0, k - 16, 0)
+    for a in range(0, OFF + W, 580):
+        fill(r_("C", a, a + 580), 0)
+    fill(r_("C", TW, TW + 512), 0); fill(r_("X", 0, OFF), 0)
     cp(r_("cdf", 272, 304), r_("cdi", 256, 288))
     scaled(r_("cdh"), r_("cdf"), 1.0)
     mm([(PS(7, 0, 304), r_("IDF"), r_("cdf")), (PS(7, 0, 304), r_("NID"), r_("cdh"))])
-    scaled(r_("cdl"), PS(7, 0, 304), 1.0, 64.0)
-    if C_ACT:
-        for k in range(7):
-            dma("S", r_("C32", 864 * k, min(TW, 864 * k + 864)), r_("zer", 0, min(864, TW - 864 * k)), 8.0 + k)
-        for f, b in ((0, "cdh"), (1, "cdl")):
-            scaled(r_("cd32", 256 * f, 256 * f + 256), r_(b, 0, 256), 1.0)
-            dma("S", r_("C32", OFF, OFF + W, 1, (f, 128, 16)), r_("cd32", 256 * f, 256 * f + 256), 3.0).update(any="C32")
+    scaled(r_("cdl"), PS(7, 0, 304), 1.0)
     for f, b in ((0, "cdh"), (1, "cdl")):
         dma("S", r_("C", OFF, OFF + W, 1, (f, 128, 16)), r_(b, 0, 256), 2.5).update(any="C")
         dma("S", r_("C", TW, TW + 512, 1, (f, 128, 16)), r_(b, 272, 304), 2.5).update(any="C")
-    for k in range(4):
-        ts(r_("D", OFF + 2048 + 512 * k, OFF + 2560 + 512 * k), r_("dli", 512 * k, 512 * k + 512), float(OFF), ALU.add)
 
-    def who(t, pieces):
-        n = W // pieces
-        for k in range(pieces):
-            c0, c1 = k * n // 16, (k + 1) * n // 16
+    def who(t, cuts):
+        for k, (c0, c1) in enumerate(zip(cuts[:-1], cuts[1:])):
             bank = 4 + k % 2
-            mm(wrap(bank, c0, "Z1", "X", OFF + S * t + k * n, n))
+            mm(wrap(bank, c0, "Z1", "X", OFF + S * t + 16 * c0, 16 * (c1 - c0)))
             act(PS(bank, 256 + c0, 256 + c1), PS(bank, c0, c1), AF.Square)
             tt(r_("wi", c0, c1), PS(bank, 256 + c0, 256 + c1), r_("pw", c0, c1), ALU.add)
             ts(r_("wj", c0, c1), r_("wi", c0, c1), 5, ALU.arith_shift_right, 255, ALU.bitwise_and)
             cp(r_("who", c0, c1), r_("wj", c0, c1))
 
-    def hop(bank, w0, wout, wu, t, k):
-        thr = r_("agw", 16 * t, 16 * t + 16)
-        f, e = r_("h", 32 * k, 32 * k + 16), r_("h", 32 * k + 16, 32 * k + 32)
-        tt(f, PS(bank, 0, 16), thr, ALU.is_lt)
-        tt(e, f, w0, ALU.mult)
-        tt(wout, PS(bank, 0, 16), e, ALU.max)
-        ts(wu, wout, BASE, ALU.add)
+    def hop(bank, w0, buf, a, k, wu, t):
+        mm([(PS(bank, 0, 32, 2), r_("IDF"), w0)], True, False)
+        mm([(PS(bank, 1, 32, 2), l, x) for o, l, x in wrap(bank, 0, "ZC", buf, a, S)], False, True)
+        tt(r_("hz", 1, 32, 2), PS(bank, 1, 32, 2), r_("agw", 16 * t, 16 * t + 16), ALU.is_lt)
+        scan(r_("h", 32 * k, 32 * k + 32), r_("hz"), PS(bank, 0, 32), ALU.mult, ALU.max)
+        ts(wu, r_("h", 32 * k + 1, 32 * k + 32, 2), BASE, ALU.add)
 
     def count(bank, buf, a, n, m, signs):
         w = r_("BH") if signs else r_("BO", 0, 128, 16)
@@ -298,26 +297,22 @@ def program(rank):
     def turned(bank, buf, a, n, ident):
         return [(PS(bank, b, b + 128), r_(buf, a + b, a + b + 128), r_(ident)) for b in range(0, n, 128)]
 
-    def youngest(a, n, cb, need, kb, lists, a0, out, out32, quick=False):
-        top, cn = r_("V4s", a + 15, a + n, 16), r_("cn", a // 16, (a + n) // 16)
+    def youngest(a, n, cb, need, kb, lists, a0, out):
+        top = r_("V4s", a + 15, a + n, 16)
         if kb != cb: mm(turned(kb, lists, a0, n, "IDF"), True, False)
-        if quick: ts(r_("Rl", a, a + n), PS(cb, 0, n), -need, ALU.add, 0.0, ALU.min)
-        else: act(r_("Rl", a, a + n), PS(cb, 0, n), AF.Relu, need, -1.0)
+        act(r_("Rl", a, a + n), PS(cb, 0, n), AF.Relu, need, -1.0)
         if kb == cb: mm(turned(kb, lists, a0, n, "IDF"), True, False)
-        mm([(PS(kb, 0, n), r_("P8K" if quick else "N8K"), r_("Rl", a, a + n))], False, True)
-        scan(r_("V4s", a, a + n), r_("m0", 0, n), PS(kb, 0, n), ALU.mult, ALU.max)
-        if quick: ts(r_("V5", a, a + n, 16), top, -BASE - 64, ALU.add, 0.0, ALU.max)
-        else: act(r_("V5", a, a + n, 16), top, AF.Relu, -BASE - 64)
-        ts(cn, top, -BASE, ALU.add, 64.0, ALU.max)
-        if a: act(r_("V5", a + 2, a + n, 16), top, AF.Relu, 16384.0 * (OFF - 0.5), -16384.0)
-        tt(r_("V5", a + 1, a + n, 16), cn, r_("V5", a, a + n, 16), ALU.subtract)
+        mm([(PS(kb, 0, n), r_("N8K"), r_("Rl", a, a + n))], False, True)
+        scan(r_("V4s", a, a + n), r_("m0", 0, n), PS(kb, 0, n), ALU.min, ALU.max)
+        if HI_V: cp(r_("V5", a, a + n, 16), top)
+        else: act(r_("V5", a, a + n, 16), top, AF.Identity)
+        if a: act(r_("V5", a + 2, a + n, 16), top, AF.Relu, 0.0, -8192.0)
+        tt(r_("V5", a + 1, a + n, 16), top, r_("V5", a, a + n, 16), ALU.subtract)
         mm(turned(cb, "V5", a, n, "ID"))
-        if quick: cp(out, PS(cb, 0, n))
-        else: act(out, PS(cb, 0, n), AF.Identity)
-        if out32: act(out32, PS(cb, 0, n) if a == 0 or C32_PS else out, AF.Identity)
+        act(out, PS(cb, 0, n), AF.Identity)
 
-    def left(a, n, bank, lists, a0, out, quick=False):
-        apart(mm(turned(bank, "Rl", a, n, "P8K" if quick else "N8K")))
+    def left(a, n, bank, lists, a0, out):
+        apart(mm(turned(bank, "Rl", a, n, "N8K")))
         tt(out, PS(bank, 0, n), r_(lists, a0, a0 + n), ALU.add)
 
     def halved(bank, a, b, out, **more):
@@ -327,7 +322,7 @@ def program(rank):
         mm(([(o, r_("HID"), b)] if b else []) + [(o, colv(2), row(0, n))], False, True).update(more)
         act(out, o, AF.Identity, -float(MAGIC))
 
-    who(0, 4)
+    who(0, WHO0)
 
     for t in range(R):
         lo, B, rot = S * t, W + S * t, ST * (t + 1)
@@ -346,7 +341,7 @@ def program(rank):
             tt(r_("i4a"), PS(7, 256, 512), r_("i4b"), ALU.add)
             ts(r_("i4b"), r_("i4a"), W - 1, ALU.bitwise_and)
             cp(r_("o4"), r_("i4b"))
-            ts(r_("c4"), r_("i4b"), float(OFF + lo), ALU.add)
+            ts(r_("c4"), r_("i4b"), float(lo), ALU.add)
         if not S4_LATE: offsets4()
         def mark(k, out, a, w):
             if k in O_ACT: act(out, a, AF.Relu, 0.0, w)
@@ -360,14 +355,17 @@ def program(rank):
         def runs(k, other):
             x, y = 2 * k in other, 2 * k + 1 in other
             return [(2 * k, 2 * k + 2, x)] if x == y else [(2 * k, 2 * k + 1, x), (2 * k + 1, 2 * k + 2, y)]
+        later = []
         for k in range(4):
             a = OFF + lo + 1024 * k
             dw = r_("DW", d0 + 64 * k, d0 + 64 * k + 64)
             for u, v, on in runs(k, S3_ACT[t]):
-                if t and k < EARLY:
-                    tt(r_("cmp", 512 * u, 512 * v), ind("z%d" % (t - 1), 0, S, "who", 32 * u, 32 * v), r_("J", 512 * u, 512 * v), ALU.is_ge, arr=t - 1)
-                elif not on:
+                if t and u == 0 and EARLY:
+                    tt(r_("cmp", 0, 512), ind("z%d" % (t - 1), 0, S, "who", 0, 32), r_("J", 0, 512), ALU.is_ge, arr=t - 1)
+                    u = 1
+                if not on:
                     tt(r_("cmp", 512 * u, 512 * v), ind("X", xa, xb, "who", 32 * u, 32 * v), r_("X", OFF + lo + 512 * u, OFF + lo + 512 * v), ALU.is_ge)
+            if k == 0: lead = [(ops[-1], LEAD[1])] if t == 0 else []
             bank = k % 2
             if t == 0: mm(wrap(bank, 0, "Z1", "cmp", 1024 * k, 1024))
             else: mm2([(PS(bank, 0, 64), r_("ID32"), dw)], wrap(bank, 0, "Z1", "cmp", 1024 * k, 1024))
@@ -389,7 +387,9 @@ def program(rank):
                 gx, ch = ind("XA", 0, a + 1024, "cw", 32 * u, 32 * v), r_("par", 512 * u, 512 * v)
                 if on: ts(ch, gx, -128.0, ALU.is_lt, -1.0, ALU.mult)
                 else: act(ch, gx, AF.Sign, 128.0)
-            bank = 5 + k % 2
+            bank = PAR_BANK[k]
+            later.append((k, bank, dw))
+        for k, bank, dw in later:
             mm2([(PS(bank, 0, 64), r_("ID32"), dw)], wrap(bank, 0, "Z1", "par", 1024 * k, 1024))
             c1, c2 = 64 * k, 64 * k + 64
             for u, v, sh in ((c1, min(c2, c0), 256 - c0), (max(c1, c0 + 1), c2, -c0)):
@@ -402,7 +402,7 @@ def program(rank):
             act(r_("G4", a, e), ind("XA", OFF + lo, xa, "o4", a // 16, e // 16), AF.Identity)
         if not last:
             act(r_("junk"), r_("DW", d0, d0 + 256), AF.Sign, -0.5, 1.0, r_("acc", t, t + 1))
-            if t == 0: act(r_("junk", 0, 240), r_("DW", 16, 256), AF.Sign, -0.5, 1.0, r_("acc", 2, 3))
+            if t == 0: act(r_("junk", 0, 240), r_("DW", 16, 256), AF.Sign, 0.5, -1.0, r_("acc", 2, 3))
         nc = NS // 16
         mm([(PS(0, 0, 257), r_("BO"), r_("O", 0, 257))])
         mm([(PS(1, 0, 257), r_("SU"), r_("O", 0, 257))])
@@ -414,47 +414,51 @@ def program(rank):
         ts(r_("of1", 0, nc), PS(2, 0, nc), 16.0, ALU.mult, 15.0, ALU.add)
         ts(r_("lb", 0, nc), PS(2, 0, nc), 16.0, ALU.mult)
         tt(r_("E0", 0, 257), r_("I", 0, 257), PS(1, 0, 257), ALU.subtract)
-        tt(r_("L2"), ind("E1", 0, 272, "of1", 0, nc), r_("kf"), ALU.is_le)
-        mm2([(PS(3, 0, nc), r_("ID"), r_("lb", 0, nc))], wrap(3, 0, "Z1", "L2", 0, NS))
-        cp(r_("of2", 0, nc), PS(3, 0, nc))
-        ts(r_("lb", 48, 48 + nc), PS(3, 0, nc), 16.0, ALU.mult)
+        for (u, v), bank in zip(CUT2, (3, 0)):
+            tt(r_("L2", 16 * u, 16 * v), ind("E1", 0, 272, "of1", u, v), r_("kf", 16 * u, 16 * v), ALU.is_le)
+            mm2([(PS(bank, 0, v - u), r_("ID"), r_("lb", u, v))], wrap(bank, 0, "Z1", "L2", 16 * u, 16 * (v - u)))
+            cp(r_("of2", u, v), PS(bank, 0, v - u))
+            ts(r_("lb", 48 + u, 48 + v), PS(bank, 0, v - u), 16.0, ALU.mult)
         X0 = float(OFF + lo + 16 * c0)
         ts(r_("ca", 0, nc), r_("kw", 0, nc), r_("I", 255 - c0, 256 - c0), ALU.is_ge, -float(W), ALU.mult)
         ts(r_("cb", 0, nc), r_("kw", 0, nc), r_("I", 256, 257), ALU.is_ge)
         scaled(r_("cc", 0, nc), r_("kw", 0, nc), 1.0, -X0)
         tt(r_("cd", 0, nc), r_("cb", 0, nc), r_("cc", 0, nc), ALU.mult)
-        tt(r_("corr", 0, nc), r_("ca", 0, nc), r_("cd", 0, nc), ALU.add)
-        tt(r_("L3"), ind("E0", 0, 257, "of2", 0, nc), r_("kf"), ALU.is_le)
-        mm([(PS(4, 0, nc), r_("IDF"), r_("corr", 0, nc))], True, False)
-        mm([(PS(4, 0, nc), r_("ID"), r_("lb", 48, 48 + nc))], False, False)
-        mm(wrap(4, 0, "Z1", "L3", 0, NS), False, True)
-        ts(r_("o", 0, nc), PS(4, 0, nc), X0, ALU.add)
-        scaled(r_("ofl", 0, nc), PS(4, 0, nc), 1.0, X0 - BASE)
+        for (u, v), bank in zip(CUT3, (4, 2)):
+            o3 = PS(bank, 0, v - u)
+            tt(r_("L3", 16 * u, 16 * v), ind("E0", 0, 257, "of2", u, v), r_("kf", 16 * u, 16 * v), ALU.is_le)
+            mm([(o3, r_("IDF"), r_("cd", u, v)), (o3, r_("ID"), r_("ca", u, v))], True, False)
+            mm([(o3, r_("ID"), r_("lb", 48 + u, 48 + v))], False, False)
+            mm(wrap(bank, 0, "Z1", "L3", 16 * u, 16 * (v - u)), False, True)
+            ts(r_("od", u, v), o3, X0 - DZ, ALU.add, 0.0, ALU.max)
+            ts(r_("o", u, v), o3, X0, ALU.add)
+            scaled(r_("ofl", u, v), o3, 1.0, X0 - BASE)
         if last:
             it = [(PS(1, 0, 272), Z("Z1", s), r_("XA", OFF + lo + 272 * s, OFF + lo + 272 * s + 272)) for s in range(16)]
             mm2(it[:8], it[8:])
             ts(r_("oa32"), PS(1, 0, 272), 0.0, ALU.is_ge)
             dma("A", ext("ya", 0, W + S), r_("oa32"), 2.5)
             dma("A", ext("yx", W, W + S), r_("X", xa, xb), 2.5)
-        for hf, (n, s0, oa, oe, at, main, moved, om) in enumerate(PARTS):
-            out, gx = r_("dm", at, at + 16 * (oe - oa)), ind("D", 0, xa, "o", oa, oe)
-            if DM_ACT[hf]: act(out, gx, AF.Identity)
-            else: cp(out, gx)
-            trans(r_("V", 2 * s0, 2 * s0 + n), r_("dm", main, main + n))
-            trans(r_("V", 2 * s0 + n, 2 * s0 + 2 * n), r_("dm", moved, moved + n))
-            ts(r_("oj", s0, s0 + n), ind("V", 2 * s0, 2 * s0 + 2 * n, "LV", s0 // 16, (s0 + n) // 16), 0.25, ALU.add, 0.0, ALU.max)
-            act(r_("y", 512 * hf, 512 * hf + n), ind("XA", 0, xa, "o", om, om + n // 16), AF.Identity)
-            k = n
-            while k < n * J_ROWS[hf]:
-                act(r_("y", 512 * hf + k, 512 * hf + 2 * k), r_("y", 512 * hf, 512 * hf + k), AF.Identity)
-                k *= 2
-        if not last:
-            mm(wrap(7, 0, "ZC", "C", TW + S * t, S))
-            scaled(r_("agw", 16 * t, 16 * t + 16), PS(7, 0, 16), -1.0, OFF + B + 255 + 64 - BASE)
-        mm([(PS(7, 128 * b, 128 * b + 128), colv(0), row(2 + S4_ACT[b], 128)) for b in range(2)], True, False)
+        for hf in range(2):
+            om, a = 18 * hf, 512 * hf
+            cp(r_("dm", 16 * om, 16 * om + 272), ind("D", DZ, xa, "od", om, om + 17))
+            trans(r_("V", a, a + 256), r_("dm", 16 * om, 16 * om + 256))
+            trans(r_("V", a + 256, a + 512), r_("dm", 16 * om + 16, 16 * om + 272))
+            ts(r_("oj", 256 * hf, 256 * hf + 256), ind("V", a, a + 512, "LV", 0, 16), BASE, ALU.add, 0.0, ALU.max)
+            act(r_("y", a, a + 256), ind("XA", 0, xa, "o", om, om + 16), AF.Identity)
+            if Y_V: cp(r_("y", a + 256, a + 512), r_("y", a, a + 256))
+            else: act(r_("y", a + 256, a + 512), r_("y", a, a + 256), AF.Identity)
+        signs4 = []
+        if t == 0:
+            mm(wrap(7, 0, "ZC", "C", TW, 2 * S))
+            scaled(r_("agw"), PS(7, 0, 32), -1.0, B + 255.0)
+        elif not last:
+            scaled(r_("agw", 16, 32), r_("agw", 16, 32), 1.0, float(S))
+        first4 = len(ops)
+        mm([(PS(7, 128 * b, 128 * b + 128), colv(0), row(2 + signed.index(S4_ACT[b]), 128)) for b in range(2)], True, False)
         for k in range(8):
-            sb, b, m0 = 5 + k % 2, k // 4, 4 * (k % 4)
-            on = m0 >= 16 - 2 * S4_ACT[b]
+            sb, b, m0 = 6 if last else 5 + k % 2, k // 4, 4 * (k % 4)
+            on = m0 >= 16 - S4_ACT[b]
             if not on and S4_TT:
                 if k == 0: mm([(PS(6, 0, S), r_("ID"), r_("X", xa, xb))])
                 for j in range(4):
@@ -462,88 +466,82 @@ def program(rank):
             else:
                 mm([(PS(sb, 128 * j, 128 * j + 128), r_("NID"), r_("X", xa + 128 * b, xa + 128 * b + 128)) for j in range(4)], True, False)
                 mm([(PS(sb, 128 * j, 128 * j + 128), r_("ID"), r_("G4", 2048 * b + m0 + j, 2048 * b + 2048, 16)) for j in range(4)], False, True)
-                if on: act(r_("S4", 512 * k, 512 * k + 512), PS(sb), AF.Sign, 0.5)
+                if on: signs4.append(act(r_("S4", 512 * k, 512 * k + 512), PS(sb), AF.Sign, 0.5))
                 else: ts(r_("S4", 512 * k, 512 * k + 512), PS(sb), 0.0, ALU.is_ge)
             w = r_("BH") if on else r_("BO", 0, 128, 16)
             mm([(PS(7, 128 * b + m0 + j, 128 * b + 128, 16), r_("S4", 512 * k + 128 * j, 512 * k + 128 * j + 128), w) for j in range(4)], False, False).update(any=(t, 2), close=True)
-        youngest(0, S, 7, 11.0, 7, "c4", 0, r_("C", xa, xb), r_("C32", xa, xb) if C_ACT and not last else None)
+        youngest(0, S, 7, 11.0, 7, "c4", 0, r_("C", xa, xb))
+        if last:
+            step4 = ops[first4:]
+            del ops[first4:]
+        signs5 = []
         if not last:
-            mm(wrap(7, 0, "ZC", "C", xa, S))
             scaled(r_("h", 96, 112), r_("kw", 0, 16), 1.0, xa - BASE)
-            hop(7, r_("h", 96, 112), r_("h", 112, 128), r_("w1"), t, 0)
+            hop(7, r_("h", 96, 112), "C", xa, 0, r_("w1"), t)
+            lead.append((ops[-1], LEAD[0]))
             left(0, S, 7, "c4", 0, r_("D", xa, xb))
-            mm([(PS(7, 0, 1), r_("BOF"), r_("acc", t, t + 1))])
-            if t == 0:
-                ts(r_("acc", 8, 9), PS(7, 0, 1), 0.5, ALU.mult, 2048.0, ALU.add)
-            else:
-                mm([(PS(7, 1, 2), r_("BOF"), r_("acc", 2, 3))])
-                cp(r_("acc", 3, 4), PS(7, 1, 2))
-                tt(r_("acc", 4, 5), PS(7, 0, 1), r_("acc", 3, 4), ALU.subtract)
-                ts(r_("acc", 9, 10), r_("acc", 4, 5), 0.5, ALU.mult, 128.0, ALU.add)
+            mm([(PS(7, 0, 1), r_("BOF"), r_("acc", k, k + 1)) for k in ((0,), (1, 2))[t]])
+            scaled(r_("acc", 8 + t, 9 + t), PS(7, 0, 1), 0.5, (2048.0, 128.0)[t])
         na = 0
-        for hf, (n, s0, oa, oe, at, main, moved, om) in enumerate(PARTS):
-            rows, nc, c1 = J_ROWS[hf], n // 16, s0 // 16
-            wide, calls = rows * n, 16 // rows
-            y1, y2 = r_("y", 512 * hf, 512 * hf + n), r_("y", 512 * hf, 512 * hf + wide)
-            mm([(PS(hf, 0, n), colv(0), row(2 + J_ACT[t][hf], n))], True, False)
-            for j in range(calls):
-                gx = ind("XA", 0, xa, "oj", s0 + j * wide // 16, s0 + (j + 1) * wide // 16)
-                ja = 16 * s0 + wide * j
-                on = j >= calls - J_ACT[t][hf]
+        for hf in range(2):
+            s0, n, om, c1, c2 = 256 * hf, 256, 18 * hf, 16 * hf, 16 * hf + 16
+            y2 = r_("y", 2 * s0, 2 * s0 + 512)
+            mm([(PS(hf, 0, n), colv(0), row(2 + signed.index(J_ACT[t][hf]), n))], True, False)
+            for m in range(0, 16, 2):
+                on, ja = m >= 16 - J_ACT[t][hf], 16 * s0 + n * m
+                gx, out = ind("XA", 0, xa, "oj", s0 + 16 * m, s0 + 16 * m + 32), r_("J", ja, ja + 512)
                 if on:
-                    gb = r_("G", 512 * (na % 8), 512 * (na % 8) + wide); sb = PS(J_BANK[na % len(J_BANK)], 0, wide); na += 1
+                    gb, sb = r_("G", 512 * na, 512 * na + 512), PS(2 + na % 2)
+                    na += 1
                     act(gb, gx, AF.Identity)
                     mm2([(sb, r_("NID"), y2)], [(sb, r_("ID"), gb)])
-                    act(r_("J", ja, ja + wide), sb, AF.Sign, 0.5)
+                    signs5.append(act(out, sb, AF.Sign, 0.5))
                 else:
-                    tt(r_("J", ja, ja + wide), gx, y2, ALU.is_ge)
-                mm([it for i in range(rows) for it in count(hf, "J", ja + n * i, n, rows * j + i, on)], False, False).update(any=(t, hf), close=True)
-            youngest(S + s0, n, hf, 11.0, K_BANK[t][hf], "dm", main, r_("crow", s0, s0 + n), r_("crow32", s0, s0 + n) if C_ACT and not last else None, QUICK[hf])
-            if C_ACT and not last: act(ind("C32", 0, xa, "o", om, om + nc), r_("crow32", s0, s0 + n), AF.Silu)
-            else: cp(ind("C", 0, xa, "o", om, om + nc), r_("crow", s0, s0 + n))
+                    tt(out, gx, y2, ALU.is_ge)
+                mm(count(hf, "J", ja, n, m, on) + count(hf, "J", ja + n, n, m + 1, on), False, False).update(any=(t, hf), close=True)
+            youngest(S + s0, n, hf, 11.0, K_BANK[t][hf], "dm", 16 * om, r_("crow", s0, s0 + n))
+            if not last: cp(ind("C", 0, xa, "o", om, om + 16), r_("crow", s0, s0 + n))
             mm(wrap(hf, 0, "ZB", "crow", s0, n))
-            tt(r_("obf", c1, c1 + nc), PS(hf, 0, nc), r_("ofl", om, om + nc), ALU.min)
-            ts(r_("ob", c1, c1 + nc), r_("obf", c1, c1 + nc), BASE, ALU.add)
-            gx = ind("XA", 0, xa, "ob", c1, c1 + nc)
-            if QUICK[hf]:
-                tt(r_("sm", 0, n), gx, y1, ALU.add)
-                ts(r_("sm", 512, 512 + n), r_("sm", 0, n), 1, ALU.arith_shift_right)
-                cp(ind("X", 0, xa, "o", om, om + nc), r_("sm", 512, 512 + n))
-            else:
-                act(r_("xb", s0, s0 + n), gx, AF.Identity)
-                halved(hf, y1, r_("xb", s0, s0 + n), r_("nx", s0, s0 + n))
-                cp(ind("X", 0, xa, "o", om, om + nc), r_("nx", s0, s0 + n))
+            tt(r_("obf", c1, c2), PS(hf, 0, 16), r_("ofl", om, om + 16), ALU.min)
+            ts(r_("ob", c1, c2), r_("obf", c1, c2), BASE, ALU.add)
+            if hf in NX_V:
+                tt(r_("wi"), ind("XA", 0, xa, "ob", c1, c2), r_("y", 2 * s0, 2 * s0 + n), ALU.add)
+                ts(r_("wj"), r_("wi"), 1, ALU.arith_shift_right)
+                cp(ind("X", 0, xa, "o", om, om + 16), r_("wj"))
+                continue
+            act(r_("xb", s0, s0 + n), ind("XA", 0, xa, "ob", c1, c2), AF.Identity)
+            halved(hf, r_("y", 2 * s0, 2 * s0 + n), r_("xb", s0, s0 + n), r_("nx", s0, s0 + n))
+            cp(ind("X", 0, xa, "o", om, om + 16), r_("nx", s0, s0 + n))
         if last:
+            for hf, d in enumerate(([], [ops[-1]])):
+                cp(ind("C", 0, xa, "o", 18 * hf, 18 * hf + 16), r_("crow", 256 * hf, 256 * hf + 256)).update(after=d)
+            ops.extend(step4)
+            for d in signs4[len(signs4) - S4_END:]: d["after"] = signs5
             dma("S", ext("yx", 0, W), r_("X", OFF + lo, xa), 5.0)
-            it = [(PS(7, 0, 272), Z("ZC", s), r_("C", OFF + lo + 272 * s, OFF + lo + 272 * s + 272)) for s in range(16)]
-            mm(it[:5], True, False); mm(it[5:10], False, False); mm(it[10:15], False, False); mm(it[15:], False, True)
-            ts(r_("oc32"), PS(7, 0, 272), BASE - OFF, ALU.add, -1.0, ALU.max)
-            dma("A", ext("yc", 0, W + S), r_("oc32"), 2.5)
+            for k in range(2):
+                it = [(PS(2 + k, 0, 136), Z("ZC", s), r_("C", OFF + lo + 2176 * k + 136 * s, OFF + lo + 2176 * k + 136 * s + 136)) for s in range(16)]
+                mm2(it[:14], it[14:])
+                scaled(r_("oc32", 136 * k, 136 * k + 136), PS(2 + k, 0, 136), 1.0)
+                dma("A", ext("yc", 2176 * k, 2176 * k + 2176), r_("oc32", 136 * k, 136 * k + 136), 2.5)
             break
-        act(r_("gC"), ind("C32" if C_ACT else "C", 0, xb, "w1", 0, 16), AF.Identity)
-        mm(wrap(4, 0, "ZC", "gC", 0, S))
-        hop(4, r_("h", 112, 128), r_("h", 96, 112), r_("w2"), t, 1)
+        act(r_("gC"), ind("C", 0, xb, "w1", 0, 16), AF.Identity)
+        hop(4, r_("h", 1, 32, 2), "gC", 0, 1, r_("w2"), t)
         zs, z = "zs%d" % t, "z%d" % t
         if Q_ACT > 1: act(r_(zs), ind("X", 0, xb, "w2", 0, 16), AF.Identity)
         else: cp(r_(zs), ind("X", 0, xb, "w2", 0, 16))
-        add("G", "send", [t], {}, [r_(zs)], [("snd", t, t + 1, 1, None, None)], 1.0, lat=5.0, nosem=True)
+        add("G", "send", [t], {}, [r_(zs)], [("snd", t, t + 1, 1, None, None)], 0.6, lat=SEND, nosem=True, lead=lead)
         cp(r_(z, 32 * rank, 32 * rank + 32), r_(zs, 32 * rank, 32 * rank + 32))
-        who(t + 1, 4)
-        for k in range(2 * EARLY):
-            a, gb = OFF + lo + S + 512 * k, r_("G", 512 * k, 512 * k + 512)
-            if k % 2 == 0: act(r_("G", 512 * k, 512 * k + 1024), ind("cm", S * t + S, S * t + 2 * S, "who", 32 * k, 32 * k + 64), AF.Identity)
-            mm2([(PS(1 - k % 2), r_("ID2"), r_("X", a, a + 512))], [(PS(1 - k % 2), r_("NID"), gb)])
-            act(r_("J", 512 * k, 512 * k + 512), PS(1 - k % 2), AF.Identity)
-        if C_ACT:
-            for n, s0, oa, oe, at, main, moved, om in PARTS:
-                cp(ind("C", 0, xa, "o", om, om + n // 16), r_("crow", s0, s0 + n))
+        who(t + 1, (0, 64, 256))
+        if EARLY:
+            act(r_("G", 0, 512), ind("cm", S * t + S, S * t + 2 * S, "who", 0, 32), AF.Identity)
+            mm2([(PS(1), r_("ID2"), r_("X", OFF + lo + S, OFF + lo + S + 512))], [(PS(1), r_("NID"), r_("G", 0, 512))])
+            act(r_("J", 0, 512), PS(1), AF.Identity)
         for k in range(2):
             mm(wrap(2 + k, 0, "ZC", "C", OFF + lo + S + 2048 * k, 2048))
             ts(r_("cw", 128 * k, 128 * k + 128), PS(2 + k, 0, 128), BASE, ALU.add)
-        for hf, (n, s0, oa, oe, at, main, moved, om) in enumerate(PARTS):
-            left(S + s0, n, 6 + hf, "dm", main, r_("left", s0, s0 + n), QUICK[hf])
-            if D_ACT: act(ind("D", 0, xa, "o", om, om + n // 16), r_("left", s0, s0 + n), AF.Silu)
-            else: cp(ind("D", 0, xa, "o", om, om + n // 16), r_("left", s0, s0 + n))
+        for hf in range(2):
+            left(S + 256 * hf, 256, 6 + hf, "dm", 288 * hf, r_("left", 256 * hf, 256 * hf + 256))
+            cp(ind("D", 0, xa, "o", 18 * hf, 18 * hf + 16), r_("left", 256 * hf, 256 * hf + 256))
         mset(r_("XA", OFF + lo, OFF + lo + S), -256.0)
     return ops
 
@@ -566,6 +564,7 @@ def schedule(ops):
             for p in ops[:i]:
                 if p["calls"][0][0] == "send" and p["calls"][0][1][0] == o["arr"]: dep[p["i"]] = False
         if o.get("behind"): dep[i - 1] = None
+        for p in o.get("after", []): dep[p["i"]] = None
         for acc, w in [(x, False) for x in o["rd"]] + [(x, True) for x in o["wr"]]:
             b = acc[0]
             ps = is_psum(b)
@@ -622,6 +621,7 @@ def best_times(ops):
     for o in ops:
         for j, need in o["dep"].items():
             fw[o["i"]].append((j, dur[j] + (0.0 if need is None else lat[j]) + (LAT if need else 0.0)))
+        for p, us in o.get("lead", []): fw[o["i"]].append((p["i"], p["dur"] + us))
     bl = [dur[i] + lat[i] for i in range(n)]
     for i in reversed(range(n)):
         for j, gap in fw[i]: bl[j] = max(bl[j], gap + bl[i])
@@ -631,7 +631,10 @@ def best_times(ops):
         if ops[i]["calls"][0][0] == "send": part[i] = ops[i]["calls"][0][1][0]
         for j, gap in fw[i]: part[j] = min(part[j], part[i])
     done, held, end = {}, {}, 0.0
-    durs = [[o["dur"] if o["calls"][0][0] in ("send", "dma_start") else f * (o["dur"] + CY * (o["gathers"] * (g - GATH) + o["scatters"] * (s - SCAT))) for o in ops] for f, g, s in OTHERS]
+    durs = [[o["dur"] if o["calls"][0][0] in ("send", "dma_start") else f * (o["dur"] + CY * (o["gathers"] * (g - GATH) + o["scatters"] * (s - SCAT))) for o in ops] for f, g, s, x in OTHERS]
+    for d, other in zip(durs, OTHERS):
+        for o in ops:
+            if o["calls"][0][0] == "send": d[o["i"]] += other[3] - SEND
     dones = [{} for _ in OTHERS]
     for r in range(R):
         ids = [i for i in range(n) if part[i] == r]
@@ -666,7 +669,7 @@ def best_times(ops):
             t = place(sorted(ids, key=key.get), inner, q, dur, free, held)
             span = max(t[i] + dur[i] + lat[i] for i in ids)
             score = 1e9
-            if it == 0 or span < cur + 1.5:
+            if it == 0 or span < cur + 0.8:
                 xs = replay(t)
                 score = (span + sum(max(x[i] + d[i] + lat[i] for i in ids) / f[0] for x, d, f in zip(xs, durs, OTHERS))) / (1 + len(OTHERS))
             if score < best: best, bt, bx, bspan = score, t, xs, span

import numpy as np
from concourse.bass import DstId, RemoteDMATransfer
from concourse.mybir import AluOpType as ALU, AxisListType as AX, ActivationFunctionType as AF

W, S, R, CAP, ST, N = 4096, 256, 3, 512, 683, 8
OFF = 544
TW = OFF + W + R * S
BASE = float(OFF)
DZ = OFF + 2040
MAGIC = 3 * 2 ** 22
BIG = 100000.0
NS = 560
S3_ACT = ((), (4,), (4,))
UPD_V = ((3, 4, 5, 7),) * 3
PAR_V = ((5, 7), (3, 5, 7), (3, 5, 7))
PARTS = ((0, 256), (256, 256))
OJ_CUT, G_ROWS, SPLIT = (0, 22, 32), 1, 2
J_ACT = ((4, 6), (4, 6), (4, 6))
S4_ACT = (8, 16)
QUICK = (False, False)
O_ACT = (0,)
S4_LATE = 0
C_ACT, D_ACT, C32_PS = False, False, True
S4_TT = True
HI_V = False
WHO0 = (0, 64, 128, 192, 256)
PAR_BANK = (5, 6, 0, 1)
H1, H2 = 0, 0
S4_END = 3
CUT2, CUT3 = ((0, 35),), ((0, 18), (18, 35))
Y_V = True
U_A = 8
LEAD = (0.0, 0.0)
NX_V = ()
EARLY = 1
D_CUT = 16
J_BANK, K_BANK = (2, 3), ((4, 4), (4, 4), (4, 5))
G4_CUT = (0, 2048, 4096)
DW_ACT, DM_ACT, Q_ACT = True, (False, False), 2
SAME_QUEUE_WAW = True

F, B16, I32, U16 = "float32", "bfloat16", "int32", "uint16"
SCRATCH = {}
for _n, _c, _d in [
    ("X", TW, B16), ("XA", TW, B16), ("C", TW + 512, B16), ("D", TW, I32), ("DW", 304, B16),
    ("cm", 768, B16), ("z0", 256, B16), ("z1", 256, B16), ("zs0", 256, B16), ("zs1", 256, B16),
    ("cdi", 288, I32), ("cdf", 304, F), ("cdh", 304, B16), ("cdl", 304, B16),
    ("pi", 16, I32), ("pc", 24, F), ("ia", 256, F), ("ib", 128, F), ("ic", 384, F), ("kf", NS, F), ("ku", NS, U16), ("kw", 48, F),
    ("Z1", 144, B16), ("ZC", 144, B16), ("ZB", 144, B16), ("BH", 8, B16), ("N8K", 128, B16), ("HID", 128, B16), ("Rl", 768, B16), ("xb", 512, B16), ("nx", 512, B16), ("mu", 16, F), ("od", 48, U16), ("U", 2048, B16),
    ("BO", 128, B16), ("BOF", 128, F), ("ID", 128, B16), ("NID", 128, B16), ("ID32", 128, B16), ("IDF", 128, F), ("SU", 128, B16),
    ("rows", 4096, B16), ("col", 384, B16), ("mdB", 256, F), ("m0", 512, F), ("ID2", 128, B16), ("LVk", 32, F), ("pw", 256, F), ("zer", 272, F), ("LVf", 16, F), ("LV", 48, U16),
    ("wi", 256, I32), ("wj", 256, I32), ("who", 256, U16),
    ("cmp", 4096, B16), ("par", 4096, B16), ("G", 4096, B16), ("G4", 4096, B16), ("S4", 4096, B16), ("J", 8192, B16),
    ("sq4", 256, F), ("i4a", 256, I32), ("i4b", 256, I32), ("c4", 256, F), ("o4", 256, U16),
    ("V4s", 768, F), ("cn", 48, F), ("V5", 768, B16), ("crow", 512, B16),
    ("cw", 256, U16), ("junk", 256, B16), ("acc", 16, F), ("O", 272, B16), ("I", 272, F), ("M", 256, F),
    ("E0", 272, F), ("E1", 272, F), ("e2", 16, F), ("L1", NS, B16), ("L2", NS, B16), ("L3", NS, B16), ("lb", 96, B16),
    ("of1", 48, U16), ("of2", 48, U16), ("ca", 48, B16), ("cb", 48, F), ("cc", 48, F), ("cd", 48, F), ("hz", 32, F),
    ("o", 48, U16), ("ofl", 48, F), ("dm", NS, F), ("V", 1024, F), ("oj", 512, U16), ("y", 1024, B16),
    ("obf", 32, F), ("ob", 32, U16), ("left", 512, I32),
    ("agw", 32, F), ("h", 128, F), ("w1", 16, U16), ("w2", 16, U16), ("gC", 256, B16), ("oc32", 272, F), ("oa32", 272, F),
]:
    SCRATCH[_n] = ("sbuf", [128, _c], _d)
for _k in range(8):
    SCRATCH["P%d" % _k] = ("psum", [128, 512], F)
NDMA = 48
SEMAPHORES = ["qV", "qA", "qP", "qG", "arr0", "arr1", "sent"] + ["dma%d" % _k for _k in range(NDMA)]

CY, PCY, LAT = 0.00083, 0.0005, 0.13
GATH, SCAT = 1.56, 3.8
SEND, DMA, FIXA = 3.2, 0.75, 0.1
OTHERS = ((1.2, 1.15, 2.0, 2.0), (1.35, 2.0, 5.5, 5.0), (1.3, 1.7, 4.5, 4.0))
SEED, ROUNDS, TEMP = 1, 21000, 0.4


def sends(T, topo, core):
    others = [r for r in range(N) if T.cores[r] != core]
    me = T.rank_of(core)
    others.sort(key=lambda r: (r - me) % N)
    near = [r for r in others if topo.chip(T.cores[r]) == topo.chip(core)]
    far = [r for r in others if r not in near]
    fe = topo.engines(core, T.cores[far[0]])
    calls = [[], []]
    a, b = len(fe) // 4, len(fe) // 2
    for i, r in enumerate(far[:4]):
        calls[0].append((r, sum(1 << e for e in fe[a * i:a * i + a])))
    for i, r in enumerate(far[4:]):
        calls[1].append((r, sum(1 << e for e in fe[b * i:b * i + b])))
    for r in near:
        calls[0].append((r, sum(1 << e for e in [e for e in topo.engines(core, T.cores[r]) if e not in fe][:a])))
    return calls


def bits(m):
    return bin(m).count("1")


def program(rank):
    ops, table = [], []
    RW = max(n for s0, n in PARTS + ((0, S),))
    signed = sorted(set(sum(J_ACT, ()) + S4_ACT))

    def r_(b, a=0, e=None, st=1, p=None):
        return (b, a, SCRATCH[b][1][1] if e is None else e, st, p, None)

    def ind(b, a, e, ob, oa, oe):
        return (b, a, e, 1, None, (ob, oa, oe))

    def cnt(x):
        return 16 * (x[5][2] - x[5][1]) if x[5] else (x[2] - x[1] + x[3] - 1) // x[3]

    def two(x):
        return SCRATCH[x[0]][2] in (B16, U16)

    def add(q, name, args, kw, reads, writes, dur, **more):
        rd, wr = [], []
        for x in reads:
            if isinstance(x, tuple):
                rd.append(x[:4])
                if x[5]: rd.append(x[5] + (1,))
        for x in writes:
            wr.append(x[:4])
            if x[5]: rd.append(x[5] + (1,))
        d = {"q": q, "calls": [(name, args, kw)], "rd": rd, "wr": wr, "dur": dur, "lat": 0.0,
             "gathers": sum(cnt(x) for x in reads if isinstance(x, tuple) and x[5]), "scatters": sum(cnt(x) for x in writes if x[5])}
        d.update(more)
        ops.append(d)
        return d

    def vdur(out, ins, base):
        if out[5]: return 0.05 + cnt(out) * SCAT * CY
        if ins[0][5]: return 0.05 + cnt(out) * GATH * CY
        return 0.015 + max(64, cnt(ins[0]) * base) * CY

    def half(*xs):
        return 0.5 if all(two(x) for x in xs) else 1.0

    def cp(out, a): return add("V", "tensor_copy", [out, a], {}, [a], [out], vdur(out, [a], half(out, a)))
    def tt(out, a, b, op, **m):
        return add("V", "tensor_tensor", [out, a, b, op], {}, [a, b], [out], vdur(out, [a], 1.0 if is_psum(a[0]) or is_psum(b[0]) else 2.0), **m)
    def ts(out, a, s1, op0, s2=None, op1=None):
        return add("V", "tensor_scalar", [out, a, s1, s2, op0] + ([op1] if op1 is not None else []), {}, [a, s1, s2], [out], vdur(out, [a], half(out, a)))
    def scan(out, a, b, op0, op1): return add("V", "tensor_tensor_scan", [out, a, b, 0.0, op0, op1], {}, [a, b], [out], vdur(out, [a], 1.0))
    def trans(out, a): return add("V", "transpose", [out, a], {}, [a], [out], vdur(out, [a], half(out, a)))
    def mset(out, v): return add("V", "memset", [out, v], {}, [], [out], vdur(out, [out], half(out)))
    def act(out, a, f, bias=0.0, scale=1.0, acc=None):
        kw = {} if out[5] else {"bias": bias, "scale": scale}
        if acc: kw["accum_out"] = acc
        dur = (0.065 if a[5] else FIXA) + cnt(out) * (GATH if a[5] else 1.0) * CY
        if f == AF.Silu and not table:
            table.append(f); dur += 1.3
        return add("A", "activation", [out, a, f], kw, [a, bias, scale], [out] + ([acc] if acc else []), dur)
    def iota(out, pat, base, cm):
        kw = {} if SCRATCH[out[0]][2] == I32 else {"allow_small_or_imprecise_dtypes": True}
        return add("G", "iota", [out, pat, base, cm], kw, [], [out], 0.13 + 2 * cnt(out) * CY)
    def select(out, a, pat, op, other, base, cm):
        return add("G", "affine_select", [out, a, pat, op, other, base, cm], {}, [a], [out], 0.17 + 2 * cnt(out) * CY)
    def mm(items, first=True, last=True):
        d = None
        for i, (o, l, x) in enumerate(items):
            dur = max(64, cnt(x)) * PCY * (4 if SCRATCH[x[0]][2] == F else 1)
            call = ("matmul", [o, l, x, first and i == 0, last and i == len(items) - 1], {})
            if d is None:
                d = add("P", call[0], call[1], {}, [l, x], [o], dur)
            else:
                d["calls"].append(call); d["rd"] += [l[:4], x[:4]]; d["dur"] += dur
        return d
    def apart(d):
        d["calls"] = [(n, x[:3] + [True, True], kw) for n, x, kw in d["calls"]]
        return d
    def mm2(x, y):
        mm(x, True, False); mm(y, False, True)
    nd = [0]
    def dma(q, out, a, us):
        rd = [a] if a[0] in SCRATCH else []
        wr = [out] if out[0] in SCRATCH else []
        nd[0] += 1
        return add(q, "dma_start", [out, a], {}, rd, wr, 0.1, lat=us * DMA, sem="dma%d" % nd[0])
    def ext(b, a, e): return (b, a, e, 1, None, None)
    def Z(name, r): return r_(name, 15 - r, 143 - r)
    def PS(k, a=0, e=512, st=1): return r_("P%d" % k, a, e, st)
    def row(k, n): return r_("rows", 512 * k, 512 * k + n, 1, (0, 1, 1))
    def colv(k): return r_("col", 128 * k, 128 * k + 128, 1, (0, 1, 1))
    def wrap(bank, c0, zname, buf, a, n):
        return [(PS(bank, c0, c0 + n // 16), Z(zname, r), r_(buf, a + r, a + n, 16)) for r in range(16)]
    def pcol(k): return r_("pc", k, k + 1)
    def icol(k): return r_("pi", k, k + 1)
    cG, cR, cCo = pcol(0), pcol(1), pcol(2)

    def xload(k): return r_("X", OFF + 1024 * k, OFF + 1024 * k + 1024), ext("x0", 1024 * k, 1024 * k + 1024)
    for q, loads in (("S", [xload(0) + (2.6,), (r_("cdi", 0, 256), ext("cd0", 0, W), 3.6), xload(2) + (4.5,), (r_("cdi", 256, 288), ext("age", 0, 512), 5.5), (r_("D", OFF + 2048, OFF + W), ext("dl0", 0, 2048), 9.5)]),
                     ("A", [(r_("cm", 0, S), ext("come", 0, S), 2.3), xload(1) + (3.5,), xload(3) + (5.3,), (r_("cm", S, 768), ext("come", S, 768), 6.0)])):
        for n, (out, a, us) in enumerate(loads):
            dma(q, out, a, us).update(behind=n > 0)
    def fill(out, v): iota(out, [[0, cnt(out)]], int(v), 0)
    def scaled(out, a, w, b=0.0): act(out, a, AF.Identity, b, w)
    iota(icol(0), [[0, 1]], 0, 1)
    iota(r_("ia", 0, 144), [[1, 144]], -15, 0)
    ts(icol(1), icol(0), 15, ALU.bitwise_and)
    ts(icol(2), icol(0), 112, ALU.bitwise_and)
    ts(icol(3), icol(0), 16, ALU.bitwise_and)
    cp(cR, icol(1)); cp(cG, icol(2))
    ts(r_("Z1"), r_("ia", 0, 144), cG, ALU.is_equal)
    iota(r_("pw"), [[0, 16], [512, 16]], 0, 0)
    ts(pcol(5), cR, 32.0, ALU.mult)
    scaled(r_("pw"), r_("pw"), 1.0, pcol(5))
    one = (0, 32, 1)
    fill(r_("rows", 0, 256, 1, one), 1)
    if RW > 256: fill(r_("rows", 256, RW, 1, one), 1)
    mset(r_("col", 128, 256, 1, one), -0.25)
    fill(r_("col", 256, 384, 1, one), MAGIC)
    iota(r_("M", 0, 128), [[1, 128]], 0, -1)
    ts(r_("ID"), r_("M", 0, 128), 0.0, ALU.is_equal)
    for nme, w in (("HID", 0.5), ("NID", -1.0), ("ID32", 32.0), ("IDF", 1.0), ("N8K", -8192.0), ("ID2", 2.0)):
        ts(r_(nme), r_("ID"), w, ALU.mult)
    iota(r_("ib"), [[16, 8], [0, 16]], 0, 0)
    ts(r_("BO"), r_("ib"), cG, ALU.is_equal)
    scaled(r_("BOF"), r_("BO"), 1.0)
    iota(r_("LVf"), [[1, 16]], 0, 0)
    ts(r_("mu"), r_("LVf"), cR, ALU.is_equal, -512.0, ALU.mult)
    for r in range(16):
        if r % U_A: ts(r_("U", 128 * r, 128 * r + 128), r_("BO"), r_("mu", r, r + 1), ALU.mult)
        else: scaled(r_("U", 128 * r, 128 * r + 128), r_("BO"), r_("mu", r, r + 1))
    select(r_("SU"), r_("BO"), [[-1, 128]], ALU.is_gt, 0.0, 0, 1)
    iota(icol(4), [[0, 1]], 256, 16)
    tt(icol(5), icol(4), icol(3), ALU.subtract)
    ts(icol(6), icol(5), 255, ALU.bitwise_and)
    ts(icol(7), icol(5), 16, ALU.bitwise_and)
    ts(icol(8), icol(7), 16.0, ALU.mult)
    tt(icol(9), icol(8), icol(3), ALU.add)
    tt(icol(10), icol(6), icol(7), ALU.subtract)
    tt(pcol(6), icol(10), icol(9), ALU.add)
    ts(r_("LV", 0, 16), r_("LVf"), pcol(6), ALU.add)
    cp(r_("cdf", 0, 256), r_("cdi", 0, 256))
    cp(r_("cdf", 256, 272), r_("cdi", 0, 16))
    trans(r_("V", 0, 256), r_("cdf", 0, 256))
    trans(r_("V", 256, 512), r_("cdf", 16, 272))
    ts(r_("cw"), ind("V", 0, 512, "LV", 0, 16), BASE, ALU.add)
    fill(r_("XA", 0, OFF), -1)
    fill(r_("DW", 256, 304), 0)
    scaled(cCo, cR, 61.0, 7.0)
    for t in range(R):
        fill(pcol(16 + t), ST * (t + 1) % 16)
    ts(r_("pc", 8, 14, 2), r_("pc", 16, 19), cR, ALU.is_le, -0.0625, ALU.mult)
    ts(r_("pc", 9, 14, 2), r_("pc", 16, 19), cR, ALU.is_gt, -0.0625, ALU.mult)
    fill(r_("zer"), 0); fill(r_("hz"), 0); fill(r_("D", DZ, DZ + 8), -1)
    iota(r_("ic", 0, 256), [[0, 16], [1, 16]], 0, 0)
    fill(r_("m0", 0, RW), BIG); fill(r_("m0", 0, RW, 16), -1)
    ts(r_("mdB"), r_("ic", 0, 256), cR, ALU.is_equal, BIG, ALU.mult)
    for a, e, b in ((0, 256, 0), (256, 288, 0), (288, 544, 256), (544, NS, 256)):
        iota(r_("kf", a, e), [[1, e - a]], b, 0)
        iota(r_("ia", 144 + a // 16, 144 + e // 16), [[16, (e - a) // 16]], b, 0)
    cp(r_("ku"), r_("kf"))
    scaled(r_("kw", 0, NS // 16), r_("ia", 144, 144 + NS // 16), 1.0, cR)
    fill(r_("E1", 256, 272), BIG); fill(r_("V5"), 0)
    scaled(r_("BH"), r_("BO", 0, 128, 16), 0.5)
    ts(pcol(14), cR, 2.0, ALU.is_lt)
    ts(pcol(15), cR, 3.0, ALU.is_lt)
    ts(r_("ZC"), r_("Z1"), pcol(14), ALU.mult)
    ts(r_("ZB"), r_("Z1"), pcol(15), ALU.mult)
    fill(r_("col", 0, 128, 1, one), 1)
    fill(r_("rows", 512, 512 + RW, 1, one), 8)
    for j, k in enumerate(signed):
        n = RW if k in sum(J_ACT, ()) else 128
        select(r_("rows", 1024 + 512 * j, 1024 + 512 * j + n, 1, one), r_("rows", 512, 512 + n, 1, one), [[0, n // 16], [1, 16]], ALU.is_ge, 0.0, k - 16, 0)
    for a in range(0, OFF + W, 580):
        fill(r_("C", a, a + 580), 0)
    fill(r_("C", TW, TW + 512), 0); fill(r_("X", 0, OFF), 0)
    cp(r_("cdf", 272, 304), r_("cdi", 256, 288))
    scaled(r_("cdh"), r_("cdf"), 1.0)
    mm([(PS(7, 0, 304), r_("IDF"), r_("cdf")), (PS(7, 0, 304), r_("NID"), r_("cdh"))])
    scaled(r_("cdl"), PS(7, 0, 304), 1.0)
    for f, b in ((0, "cdh"), (1, "cdl")):
        dma("S", r_("C", OFF, OFF + W, 1, (f, 128, 16)), r_(b, 0, 256), 2.5).update(any="C")
        dma("S", r_("C", TW, TW + 512, 1, (f, 128, 16)), r_(b, 272, 304), 2.5).update(any="C")

    def who(t, cuts):
        for k, (c0, c1) in enumerate(zip(cuts[:-1], cuts[1:])):
            bank = 4 + k % 2
            mm(wrap(bank, c0, "Z1", "X", OFF + S * t + 16 * c0, 16 * (c1 - c0)))
            act(PS(bank, 256 + c0, 256 + c1), PS(bank, c0, c1), AF.Square)
            tt(r_("wi", c0, c1), PS(bank, 256 + c0, 256 + c1), r_("pw", c0, c1), ALU.add)
            ts(r_("wj", c0, c1), r_("wi", c0, c1), 5, ALU.arith_shift_right, 255, ALU.bitwise_and)
            cp(r_("who", c0, c1), r_("wj", c0, c1))

    def hop(bank, w0, buf, a, k, wu, t):
        mm([(PS(bank, 0, 32, 2), r_("IDF"), w0)], True, False)
        mm([(PS(bank, 1, 32, 2), l, x) for o, l, x in wrap(bank, 0, "ZC", buf, a, S)], False, True)
        tt(r_("hz", 1, 32, 2), PS(bank, 1, 32, 2), r_("agw", 16 * t, 16 * t + 16), ALU.is_lt)
        scan(r_("h", 32 * k, 32 * k + 32), r_("hz"), PS(bank, 0, 32), ALU.mult, ALU.max)
        ts(wu, r_("h", 32 * k + 1, 32 * k + 32, 2), BASE, ALU.add)

    def count(bank, buf, a, n, m, signs):
        w = r_("BH") if signs else r_("BO", 0, 128, 16)
        return [(PS(bank, b + m, b + 128, 16), r_(buf, a + b, a + b + 128), w) for b in range(0, n, 128)]

    def turned(bank, buf, a, n, ident):
        return [(PS(bank, b, b + 128), r_(buf, a + b, a + b + 128), r_(ident)) for b in range(0, n, 128)]

    def youngest(a, n, cb, need, kb, lists, a0, out):
        top = r_("V4s", a + 15, a + n, 16)
        if kb != cb: mm(turned(kb, lists, a0, n, "IDF"), True, False)
        act(r_("Rl", a, a + n), PS(cb, 0, n), AF.Relu, need, -1.0)
        if kb == cb: mm(turned(kb, lists, a0, n, "IDF"), True, False)
        mm([(PS(kb, 0, n), r_("N8K"), r_("Rl", a, a + n))], False, True)
        scan(r_("V4s", a, a + n), r_("m0", 0, n), PS(kb, 0, n), ALU.min, ALU.max)
        if HI_V: cp(r_("V5", a, a + n, 16), top)
        else: act(r_("V5", a, a + n, 16), top, AF.Identity)
        if a: act(r_("V5", a + 2, a + n, 16), top, AF.Relu, 0.0, -8192.0)
        tt(r_("V5", a + 1, a + n, 16), top, r_("V5", a, a + n, 16), ALU.subtract)
        mm(turned(cb, "V5", a, n, "ID"))
        act(out, PS(cb, 0, n), AF.Identity)

    def left(a, n, bank, lists, a0, out):
        apart(mm(turned(bank, "Rl", a, n, "N8K")))
        tt(out, PS(bank, 0, n), r_(lists, a0, a0 + n), ALU.add)

    def halved(bank, a, b, out, **more):
        n = cnt(a)
        o = PS(bank, 0, n)
        mm([(o, r_("HID"), a), (o, colv(1), row(0, n))], True, False)
        mm(([(o, r_("HID"), b)] if b else []) + [(o, colv(2), row(0, n))], False, True).update(more)
        act(out, o, AF.Identity, -float(MAGIC))

    who(0, WHO0)

    for t in range(R):
        lo, B, rot = S * t, W + S * t, ST * (t + 1)
        xa, xb = OFF + B, OFF + B + S
        c0, d0 = rot // 16, lo // 16
        last = t == R - 1
        if t == 0: halved(0, r_("cm", 0, S), None, r_("X", xa, xb))
        else: halved(0, r_("cm", S * t, S * t + S), r_("z%d" % (t - 1)), r_("X", xa, xb), arr=t - 1)
        if last: act(r_("XA", xa, xb), r_("X", xa, xb), AF.Identity)
        mm([(PS(7, 0, 256), r_("BO"), r_("X", xa, xb))])
        act(r_("sq4"), PS(7, 0, 256), AF.Square)
        act(PS(7, 256, 512), PS(7, 0, 256), AF.Identity, 0.0 if t == 0 else r_("acc", 7 + t, 8 + t), cCo)
        def offsets4():
            d = ts(r_("i4b"), r_("sq4"), 1.0 / 32, ALU.mult, -0.375, ALU.add)
            if S4_LATE: d["rd"].append(r_("par", 512 * S4_LATE - 1, 512 * S4_LATE)[:4])
            tt(r_("i4a"), PS(7, 256, 512), r_("i4b"), ALU.add)
            ts(r_("i4b"), r_("i4a"), W - 1, ALU.bitwise_and)
            cp(r_("o4"), r_("i4b"))
            ts(r_("c4"), r_("i4b"), float(lo), ALU.add)
        if not S4_LATE: offsets4()
        def mark(k, out, a, w):
            if k in O_ACT: act(out, a, AF.Relu, 0.0, w)
            else: ts(out, a, w, ALU.mult, 0.0, ALU.max)
        for n, k in enumerate(S3_ACT[t]):
            a, sb = OFF + lo + 512 * k, 5 + n % 2
            gb = r_("G", 512 * k, 512 * k + 512)
            act(gb, ind("X", xa, xb, "who", 32 * k, 32 * k + 32), AF.Identity)
            mm2([(PS(sb), r_("NID"), r_("X", a, a + 512))], [(PS(sb), r_("ID"), gb)])
            act(r_("cmp", 512 * k, 512 * k + 512), PS(sb), AF.Sign, 0.5)
        def runs(k, other):
            x, y = 2 * k in other, 2 * k + 1 in other
            return [(2 * k, 2 * k + 2, x)] if x == y else [(2 * k, 2 * k + 1, x), (2 * k + 1, 2 * k + 2, y)]
        later = []
        for k in range(4):
            a = OFF + lo + 1024 * k
            dw = r_("DW", d0 + 64 * k, d0 + 64 * k + 64)
            for u, v, on in runs(k, S3_ACT[t]):
                if t and u == 0 and EARLY:
                    tt(r_("cmp", 0, 512), ind("z%d" % (t - 1), 0, S, "who", 0, 32), r_("J", 0, 512), ALU.is_ge, arr=t - 1)
                    u = 1
                if not on:
                    tt(r_("cmp", 512 * u, 512 * v), ind("X", xa, xb, "who", 32 * u, 32 * v), r_("X", OFF + lo + 512 * u, OFF + lo + 512 * v), ALU.is_ge)
            if k == 0: lead = [(ops[-1], LEAD[1])] if t == 0 else []
            bank = k % 2
            if t == 0: mm(wrap(bank, 0, "Z1", "cmp", 1024 * k, 1024))
            else: mm2([(PS(bank, 0, 64), r_("ID32"), dw)], wrap(bank, 0, "Z1", "cmp", 1024 * k, 1024))
            for u, v, on in runs(k, S3_ACT[t]):
                src, dst = PS(bank, 32 * (u - 2 * k), 32 * (v - 2 * k)), r_("DW", d0 + 32 * u, d0 + 32 * v)
                if DW_ACT: act(dst, src, AF.Relu, -5.0 if on else -10.0)
                else: ts(dst, src, -5.0 if on else -10.0, ALU.add, 0.0, ALU.max)
            for p in range(2):
                ub = 2 + (2 * k + p) % 3
                it = [(PS(ub, r // 2, 512, 8), r_("U", 128 * r, 128 * r + 128), dw) for r in range(p, 16, 2)]
                xs, xo = r_("X", a + p, a + 1024, 2), r_("XA", a + p, a + 1024, 2)
                if 2 * k + p in UPD_V[t]:
                    apart(mm(it))
                    tt(xo, PS(ub), xs, ALU.add)
                else:
                    mm2([(PS(ub), r_("ID"), xs)], it)
                    act(xo, PS(ub), AF.Identity)
            for u, v, on in runs(k, PAR_V[t]):
                gx, ch = ind("XA", 0, a + 1024, "cw", 32 * u, 32 * v), r_("par", 512 * u, 512 * v)
                if on: ts(ch, gx, -128.0, ALU.is_lt, -1.0, ALU.mult)
                else: act(ch, gx, AF.Sign, 128.0)
            bank = PAR_BANK[k]
            later.append((k, bank, dw))
        for k, bank, dw in later:
            mm2([(PS(bank, 0, 64), r_("ID32"), dw)], wrap(bank, 0, "Z1", "par", 1024 * k, 1024))
            c1, c2 = 64 * k, 64 * k + 64
            for u, v, sh in ((c1, min(c2, c0), 256 - c0), (max(c1, c0 + 1), c2, -c0)):
                if u < v: mark(k, r_("O", u + sh, v + sh), PS(bank, u - c1, v - c1), -0.0625)
            if c1 <= c0 < c2:
                for q, col in ((0, 8 + 2 * t), (256, 9 + 2 * t)):
                    mark(k, r_("O", q, q + 1), PS(bank, c0 - c1, c0 - c1 + 1), pcol(col))
        if S4_LATE: offsets4()
        for a, e in zip(G4_CUT[:-1], G4_CUT[1:]):
            act(r_("G4", a, e), ind("XA", OFF + lo, xa, "o4", a // 16, e // 16), AF.Identity)
        if not last:
            act(r_("junk"), r_("DW", d0, d0 + 256), AF.Sign, -0.5, 1.0, r_("acc", t, t + 1))
            if t == 0: act(r_("junk", 0, 240), r_("DW", 16, 256), AF.Sign, 0.5, -1.0, r_("acc", 2, 3))
        nc = NS // 16
        mm([(PS(0, 0, 257), r_("BO"), r_("O", 0, 257))])
        mm([(PS(1, 0, 257), r_("SU"), r_("O", 0, 257))])
        scan(r_("I", 0, 257), PS(0, 0, 257), r_("zer", 0, 257), ALU.add, ALU.add)
        scan(r_("e2"), r_("mdB", 0, 16), r_("I", 15, 256, 16), ALU.max, ALU.min)
        ts(r_("L1"), r_("ku"), r_("e2", 15, 16), ALU.is_ge)
        mm(wrap(2, 0, "Z1", "L1", 0, NS))
        scan(r_("E1", 0, 256), r_("mdB"), r_("I", 0, 256), ALU.max, ALU.min)
        ts(r_("of1", 0, nc), PS(2, 0, nc), 16.0, ALU.mult, 15.0, ALU.add)
        ts(r_("lb", 0, nc), PS(2, 0, nc), 16.0, ALU.mult)
        tt(r_("E0", 0, 257), r_("I", 0, 257), PS(1, 0, 257), ALU.subtract)
        for (u, v), bank in zip(CUT2, (3, 0)):
            tt(r_("L2", 16 * u, 16 * v), ind("E1", 0, 272, "of1", u, v), r_("kf", 16 * u, 16 * v), ALU.is_le)
            mm2([(PS(bank, 0, v - u), r_("ID"), r_("lb", u, v))], wrap(bank, 0, "Z1", "L2", 16 * u, 16 * (v - u)))
            cp(r_("of2", u, v), PS(bank, 0, v - u))
            ts(r_("lb", 48 + u, 48 + v), PS(bank, 0, v - u), 16.0, ALU.mult)
        X0 = float(OFF + lo + 16 * c0)
        ts(r_("ca", 0, nc), r_("kw", 0, nc), r_("I", 255 - c0, 256 - c0), ALU.is_ge, -float(W), ALU.mult)
        ts(r_("cb", 0, nc), r_("kw", 0, nc), r_("I", 256, 257), ALU.is_ge)
        scaled(r_("cc", 0, nc), r_("kw", 0, nc), 1.0, -X0)
        tt(r_("cd", 0, nc), r_("cb", 0, nc), r_("cc", 0, nc), ALU.mult)
        for (u, v), bank in zip(CUT3, (4, 2)):
            o3 = PS(bank, 0, v - u)
            tt(r_("L3", 16 * u, 16 * v), ind("E0", 0, 257, "of2", u, v), r_("kf", 16 * u, 16 * v), ALU.is_le)
            mm([(o3, r_("IDF"), r_("cd", u, v)), (o3, r_("ID"), r_("ca", u, v))], True, False)
            mm([(o3, r_("ID"), r_("lb", 48 + u, 48 + v))], False, False)
            mm(wrap(bank, 0, "Z1", "L3", 16 * u, 16 * (v - u)), False, True)
            ts(r_("od", u, v), o3, X0 - DZ, ALU.add, 0.0, ALU.max)
            ts(r_("o", u, v), o3, X0, ALU.add)
            scaled(r_("ofl", u, v), o3, 1.0, X0 - BASE)
        if last:
            it = [(PS(1, 0, 272), Z("Z1", s), r_("XA", OFF + lo + 272 * s, OFF + lo + 272 * s + 272)) for s in range(16)]
            mm2(it[:8], it[8:])
            ts(r_("oa32"), PS(1, 0, 272), 0.0, ALU.is_ge)
            dma("A", ext("ya", 0, W + S), r_("oa32"), 2.5)
            dma("A", ext("yx", W, W + S), r_("X", xa, xb), 2.5)
        for hf in range(2):
            om, a = 18 * hf, 512 * hf
            cp(r_("dm", 16 * om, 16 * om + 272), ind("D", DZ, xa, "od", om, om + 17))
            trans(r_("V", a, a + 256), r_("dm", 16 * om, 16 * om + 256))
            trans(r_("V", a + 256, a + 512), r_("dm", 16 * om + 16, 16 * om + 272))
            ts(r_("oj", 256 * hf, 256 * hf + 256), ind("V", a, a + 512, "LV", 0, 16), BASE, ALU.add, 0.0, ALU.max)
            act(r_("y", a, a + 256), ind("XA", 0, xa, "o", om, om + 16), AF.Identity)
            if Y_V: cp(r_("y", a + 256, a + 512), r_("y", a, a + 256))
            else: act(r_("y", a + 256, a + 512), r_("y", a, a + 256), AF.Identity)
        signs4 = []
        if t == 0:
            mm(wrap(7, 0, "ZC", "C", TW, 2 * S))
            scaled(r_("agw"), PS(7, 0, 32), -1.0, B + 255.0)
        elif not last:
            scaled(r_("agw", 16, 32), r_("agw", 16, 32), 1.0, float(S))
        first4 = len(ops)
        mm([(PS(7, 128 * b, 128 * b + 128), colv(0), row(2 + signed.index(S4_ACT[b]), 128)) for b in range(2)], True, False)
        for k in range(8):
            sb, b, m0 = 6 if last else 5 + k % 2, k // 4, 4 * (k % 4)
            on = m0 >= 16 - S4_ACT[b]
            if not on and S4_TT:
                if k == 0: mm([(PS(6, 0, S), r_("ID"), r_("X", xa, xb))])
                for j in range(4):
                    tt(r_("S4", 512 * k + 128 * j, 512 * k + 128 * j + 128), r_("G4", 2048 * b + m0 + j, 2048 * b + 2048, 16), PS(6, 128 * b, 128 * b + 128), ALU.is_ge)
            else:
                mm([(PS(sb, 128 * j, 128 * j + 128), r_("NID"), r_("X", xa + 128 * b, xa + 128 * b + 128)) for j in range(4)], True, False)
                mm([(PS(sb, 128 * j, 128 * j + 128), r_("ID"), r_("G4", 2048 * b + m0 + j, 2048 * b + 2048, 16)) for j in range(4)], False, True)
                if on: signs4.append(act(r_("S4", 512 * k, 512 * k + 512), PS(sb), AF.Sign, 0.5))
                else: ts(r_("S4", 512 * k, 512 * k + 512), PS(sb), 0.0, ALU.is_ge)
            w = r_("BH") if on else r_("BO", 0, 128, 16)
            mm([(PS(7, 128 * b + m0 + j, 128 * b + 128, 16), r_("S4", 512 * k + 128 * j, 512 * k + 128 * j + 128), w) for j in range(4)], False, False).update(any=(t, 2), close=True)
        youngest(0, S, 7, 11.0, 7, "c4", 0, r_("C", xa, xb))
        if last:
            step4 = ops[first4:]
            del ops[first4:]
        signs5 = []
        if not last:
            scaled(r_("h", 96, 112), r_("kw", 0, 16), 1.0, xa - BASE)
            hop(7, r_("h", 96, 112), "C", xa, 0, r_("w1"), t)
            lead.append((ops[-1], LEAD[0]))
            left(0, S, 7, "c4", 0, r_("D", xa, xb))
            mm([(PS(7, 0, 1), r_("BOF"), r_("acc", k, k + 1)) for k in ((0,), (1, 2))[t]])
            scaled(r_("acc", 8 + t, 9 + t), PS(7, 0, 1), 0.5, (2048.0, 128.0)[t])
        na = 0
        for hf in range(2):
            s0, n, om, c1, c2 = 256 * hf, 256, 18 * hf, 16 * hf, 16 * hf + 16
            y2 = r_("y", 2 * s0, 2 * s0 + 512)
            mm([(PS(hf, 0, n), colv(0), row(2 + signed.index(J_ACT[t][hf]), n))], True, False)
            for m in range(0, 16, 2):
                on, ja = m >= 16 - J_ACT[t][hf], 16 * s0 + n * m
                gx, out = ind("XA", 0, xa, "oj", s0 + 16 * m, s0 + 16 * m + 32), r_("J", ja, ja + 512)
                if on:
                    gb, sb = r_("G", 512 * na, 512 * na + 512), PS(2 + na % 2)
                    na += 1
                    act(gb, gx, AF.Identity)
                    mm2([(sb, r_("NID"), y2)], [(sb, r_("ID"), gb)])
                    signs5.append(act(out, sb, AF.Sign, 0.5))
                else:
                    tt(out, gx, y2, ALU.is_ge)
                mm(count(hf, "J", ja, n, m, on) + count(hf, "J", ja + n, n, m + 1, on), False, False).update(any=(t, hf), close=True)
            youngest(S + s0, n, hf, 11.0, K_BANK[t][hf], "dm", 16 * om, r_("crow", s0, s0 + n))
            if not last: cp(ind("C", 0, xa, "o", om, om + 16), r_("crow", s0, s0 + n))
            mm(wrap(hf, 0, "ZB", "crow", s0, n))
            tt(r_("obf", c1, c2), PS(hf, 0, 16), r_("ofl", om, om + 16), ALU.min)
            ts(r_("ob", c1, c2), r_("obf", c1, c2), BASE, ALU.add)
            if hf in NX_V:
                tt(r_("wi"), ind("XA", 0, xa, "ob", c1, c2), r_("y", 2 * s0, 2 * s0 + n), ALU.add)
                ts(r_("wj"), r_("wi"), 1, ALU.arith_shift_right)
                cp(ind("X", 0, xa, "o", om, om + 16), r_("wj"))
                continue
            act(r_("xb", s0, s0 + n), ind("XA", 0, xa, "ob", c1, c2), AF.Identity)
            halved(hf, r_("y", 2 * s0, 2 * s0 + n), r_("xb", s0, s0 + n), r_("nx", s0, s0 + n))
            cp(ind("X", 0, xa, "o", om, om + 16), r_("nx", s0, s0 + n))
        if last:
            for hf, d in enumerate(([], [ops[-1]])):
                cp(ind("C", 0, xa, "o", 18 * hf, 18 * hf + 16), r_("crow", 256 * hf, 256 * hf + 256)).update(after=d)
            ops.extend(step4)
            for d in signs4[len(signs4) - S4_END:]: d["after"] = signs5
            dma("S", ext("yx", 0, W), r_("X", OFF + lo, xa), 5.0)
            for k in range(2):
                it = [(PS(2 + k, 0, 136), Z("ZC", s), r_("C", OFF + lo + 2176 * k + 136 * s, OFF + lo + 2176 * k + 136 * s + 136)) for s in range(16)]
                mm2(it[:14], it[14:])
                scaled(r_("oc32", 136 * k, 136 * k + 136), PS(2 + k, 0, 136), 1.0)
                dma("A", ext("yc", 2176 * k, 2176 * k + 2176), r_("oc32", 136 * k, 136 * k + 136), 2.5)
            break
        act(r_("gC"), ind("C", 0, xb, "w1", 0, 16), AF.Identity)
        hop(4, r_("h", 1, 32, 2), "gC", 0, 1, r_("w2"), t)
        zs, z = "zs%d" % t, "z%d" % t
        if Q_ACT > 1: act(r_(zs), ind("X", 0, xb, "w2", 0, 16), AF.Identity)
        else: cp(r_(zs), ind("X", 0, xb, "w2", 0, 16))
        add("G", "send", [t], {}, [r_(zs)], [("snd", t, t + 1, 1, None, None)], 0.6, lat=SEND, nosem=True, lead=lead)
        cp(r_(z, 32 * rank, 32 * rank + 32), r_(zs, 32 * rank, 32 * rank + 32))
        who(t + 1, (0, 64, 256))
        if EARLY:
            act(r_("G", 0, 512), ind("cm", S * t + S, S * t + 2 * S, "who", 0, 32), AF.Identity)
            mm2([(PS(1), r_("ID2"), r_("X", OFF + lo + S, OFF + lo + S + 512))], [(PS(1), r_("NID"), r_("G", 0, 512))])
            act(r_("J", 0, 512), PS(1), AF.Identity)
        for k in range(2):
            mm(wrap(2 + k, 0, "ZC", "C", OFF + lo + S + 2048 * k, 2048))
            ts(r_("cw", 128 * k, 128 * k + 128), PS(2 + k, 0, 128), BASE, ALU.add)
        for hf in range(2):
            left(S + 256 * hf, 256, 6 + hf, "dm", 288 * hf, r_("left", 256 * hf, 256 * hf + 256))
            cp(ind("D", 0, xa, "o", 18 * hf, 18 * hf + 16), r_("left", 256 * hf, 256 * hf + 256))
        mset(r_("XA", OFF + lo, OFF + lo + S), -256.0)
    return ops


def is_psum(b):
    return b in SCRATCH and SCRATCH[b][0] == "psum"


def meet(x, y):
    if x[0] >= y[1] or y[0] >= x[1]: return False
    return x[2] != y[2] or (x[0] - y[0]) % x[2] == 0


def schedule(ops):
    seen = {}
    for i, o in enumerate(ops):
        o["i"] = i
        dep = {}
        if "arr" in o:
            for p in ops[:i]:
                if p["calls"][0][0] == "send" and p["calls"][0][1][0] == o["arr"]: dep[p["i"]] = False
        if o.get("behind"): dep[i - 1] = None
        for p in o.get("after", []): dep[p["i"]] = None
        for acc, w in [(x, False) for x in o["rd"]] + [(x, True) for x in o["wr"]]:
            b = acc[0]
            ps = is_psum(b)
            for (run, j, w2) in seen.get(b, []):
                if j == i: continue
                p = ops[j]
                dmaish = "sem" in p or "sem" in o
                same = p["q"] == o["q"] and not dmaish
                if "any" in o and o["any"] == p.get("any"): continue
                if ps:
                    if same and not (w or w2): continue
                elif not (w or w2) or not meet(run, acc[1:]): continue
                need = (not same) or (o["q"] != "P" and ((w2 and not w) or SAME_QUEUE_WAW))
                dep[j] = dep.get(j, False) or need
        for acc, w in [(x, False) for x in o["rd"]] + [(x, True) for x in o["wr"]]:
            b, a, e, st = acc
            lst = seen.setdefault(b, [])
            if w and "any" not in o: lst[:] = [x for x in lst if not (is_psum(b) or (st == 1 and a <= x[0][0] and x[0][1] <= e)) or x[1] == i]
            lst.append((acc[1:], i, w))
        o["dep"] = dep
    if "t0" not in KEPT:
        KEPT["t0"] = best_times(ops)
    for o in ops: o["t0"] = KEPT["t0"][o["i"]]
    return sorted(ops, key=lambda o: (o["t0"], o["i"]))


KEPT = {}


def place(seq, before, q, dur, free, held):
    t, busy = {}, {k: list(v) for k, v in held.items()}
    for i in seq:
        t0 = free[i]
        for j, gap in before[i]:
            if t[j] + gap > t0: t0 = t[j] + gap
        iv = busy.setdefault(q[i], [])
        lo, hi = 0, len(iv)
        while lo < hi:
            mid = (lo + hi) // 2
            if iv[mid][1] <= t0: lo = mid + 1
            else: hi = mid
        k = lo
        while k < len(iv) and iv[k][0] < t0 + dur[i] - 1e-9:
            t0 = max(t0, iv[k][1]); k += 1
        iv.insert(k, (t0, t0 + dur[i]))
        t[i] = t0
    return t


def best_times(ops):
    n = len(ops)
    q = [o["q"] for o in ops]; dur = [o["dur"] for o in ops]; lat = [o["lat"] for o in ops]
    fw = [[] for _ in ops]
    for o in ops:
        for j, need in o["dep"].items():
            fw[o["i"]].append((j, dur[j] + (0.0 if need is None else lat[j]) + (LAT if need else 0.0)))
        for p, us in o.get("lead", []): fw[o["i"]].append((p["i"], p["dur"] + us))
    bl = [dur[i] + lat[i] for i in range(n)]
    for i in reversed(range(n)):
        for j, gap in fw[i]: bl[j] = max(bl[j], gap + bl[i])
    rng = np.random.RandomState(SEED)
    part, sent = [R - 1] * n, 0
    for i in reversed(range(n)):
        if ops[i]["calls"][0][0] == "send": part[i] = ops[i]["calls"][0][1][0]
        for j, gap in fw[i]: part[j] = min(part[j], part[i])
    done, held, end = {}, {}, 0.0
    durs = [[o["dur"] if o["calls"][0][0] in ("send", "dma_start") else f * (o["dur"] + CY * (o["gathers"] * (g - GATH) + o["scatters"] * (s - SCAT))) for o in ops] for f, g, s, x in OTHERS]
    for d, other in zip(durs, OTHERS):
        for o in ops:
            if o["calls"][0][0] == "send": d[o["i"]] += other[3] - SEND
    dones = [{} for _ in OTHERS]
    for r in range(R):
        ids = [i for i in range(n) if part[i] == r]
        near = [i for i in done if done[i] + dur[i] > end]
        both = set(ids + near)
        deps = [{i: [(j, gap - dur[j] + d[j]) for j, gap in fw[i] if j in both] for i in both} for d in durs]
        frees = [{i: max([x.get(i, 0.0)] + [x[j] + gap - dur[j] + d[j] for j, gap in fw[i] if j not in both]) for i in both} for d, x in zip(durs, dones)]
        def replay(t):
            seq = sorted(near + ids, key=lambda i: (t[i] if i in t else done[i], i))
            out = []
            for d, dep, fr in zip(durs, deps, frees):
                x, at = {}, {}
                for i in seq:
                    t0 = max(fr[i], at.get(q[i], 0.0))
                    for j, gap in dep[i]:
                        if x[j] + gap > t0: t0 = x[j] + gap
                    x[i] = t0; at[q[i]] = t0 + d[i]
                out.append(x)
            return out
        free = {i: max([0.0] + [done[j] + gap for j, gap in fw[i] if j in done]) for i in ids}
        inner = {i: [(j, gap) for j, gap in fw[i] if j not in done] for i in ids}
        after = {i: [] for i in ids}
        for i in ids:
            for j, gap in inner[i]: after[j].append((i, gap - dur[j] + dur[i]))
        zero = {i: lat[i] for i in ids}
        first = min(free.values())
        best, bt, key = 1e9, None, {i: -bl[i] for i in ids}
        for it in range(ROUNDS):
            for i in ids:
                for j, gap in inner[i]:
                    if key[j] + 1e-6 > key[i]: key[i] = key[j] + 1e-6
            t = place(sorted(ids, key=key.get), inner, q, dur, free, held)
            span = max(t[i] + dur[i] + lat[i] for i in ids)
            score = 1e9
            if it == 0 or span < cur + 0.8:
                xs = replay(t)
                score = (span + sum(max(x[i] + d[i] + lat[i] for i in ids) / f[0] for x, d, f in zip(xs, durs, OTHERS))) / (1 + len(OTHERS))
            if score < best: best, bt, bx, bspan = score, t, xs, span
            if it == 0 or score < held_score + TEMP * (1.0 - it / ROUNDS) * rng.rand():
                cur, ct, held_score = span, t, score
                tb = place(sorted(ids, key=lambda i: (-(ct[i] + dur[i]), -i)), after, q, dur, zero, {})
                late = {i: cur - (tb[i] + dur[i]) for i in ids}
                ends = {(q[i], round(ct[i] + dur[i], 6)): i for i in ids}
                i, behind = max(ids, key=lambda i: ct[i] + dur[i] + lat[i]), []
                while i is not None:
                    j = next((j for j, gap in inner[i] if ct[j] + gap > ct[i] - 1e-7), None)
                    if j is None:
                        j = ends.get((q[i], round(ct[i], 6)))
                        if j is not None: behind.append((j, i))
                    i = j
            if behind and rng.rand() < 0.5:
                u, v = behind[rng.randint(len(behind))]
                key, step = dict(ct), 0.01 + 3.0 * rng.rand() ** 3
                if rng.rand() < 0.5: key[u] = ct[v] + step
                else:
                    key[v] = ct[u] - step
                    for i in reversed(ids):
                        for j, gap in inner[i]:
                            if key[j] > key[i] - gap: key[j] = key[i] - gap
                continue
            a, w, amp, mix = first + rng.rand() * (cur - first), 1.0 + 12.0 * rng.rand(), 4.0 * rng.rand() ** 2, float(rng.choice([0.0, 0.5, 1.0]))
            noise = (rng.rand(n) * amp).tolist()
            key = {i: (mix * late[i] + (1 - mix) * ct[i] + noise[i]) if a - w <= ct[i] <= a else ct[i] for i in ids}
        done.update(bt)
        for x, y in zip(dones, bx): x.update(y)
        for i in ids: held.setdefault(q[i], []).append((bt[i], bt[i] + dur[i]))
        end = min(bt[i] for i in ids if lat[i] + bt[i] + dur[i] >= bspan - 1e-9) - 8.0
        held = {k: [(0.0, end)] + sorted((max(u, end), v) for u, v in iv if v > end) for k, iv in held.items()}
    return done


def plan(rank):
    ops = program(rank)
    order = schedule(ops)
    pos, n = {}, {}
    for o in {o["any"]: o for o in order if o.get("close")}.values():
        o["calls"][-1][1][4] = True
    for o in order:
        n[o["q"]] = n.get(o["q"], 0) + 1
        o["pos"] = n[o["q"]]
    clock = {q: {} for q in "VAPGS"}
    for o in order:
        ck = clock[o["q"]]
        want = {}
        for j, need in o["dep"].items():
            if need:
                p = ops[j]
                key = p.get("sem", p["q"])
                want[key] = max(want.get(key, (0, None)), (p["pos"], j))
        o["waits"] = []
        for key, (v, j) in sorted(want.items(), key=lambda x: -ops[x[1][1]]["t0"]):
            if ck.get(key, 0) >= v: continue
            o["waits"].append(j); ops[j]["inc"] = True
            ck[key] = v
            for k2, v2 in ops[j]["ck"].items(): ck[k2] = max(ck.get(k2, 0), v2)
        o["ck"] = dict(ck)
    tot = {}
    for o in order:
        if "sem" in o: o["val"] = 16
        elif o.get("inc"):
            tot[o["q"]] = tot.get(o["q"], 0) + 1
            o["val"] = tot[o["q"]]
    return ops, order, tot


def rank_program(g, core, T, topo):
    rank = T.rank_of(core)
    if rank is None:
        return
    ops, order, tot = plan(rank)
    eng = {"V": g.vector, "A": g.scalar, "P": g.tensor, "G": g, "S": g.sync}
    calls = sends(T, topo, core)
    coming = sum(bits(m) for r in range(N) if r != rank for c in sends(T, topo, T.cores[r]) for d, m in c if d == rank)
    going = sum(bits(m) for c in calls for d, m in c)

    def ap(x):
        if not isinstance(x, tuple): return x
        b, a, e, st, p, off = x
        cols = slice(a, e, st) if st != 1 else slice(a, e)
        if p is None: v = T[b][:, cols]
        else: v = T[b][slice(p[0], p[1], p[2]) if p[2] != 1 else slice(p[0], p[1]), cols]
        return v.indirect(T[off[0]][:, off[1]:off[2]]) if off else v

    def sem_of(o):
        return T.sem[o["sem"]] if "sem" in o else T.sem["q" + o["q"]]

    for o in order:
        e = eng[o["q"]]
        for j in o["waits"]:
            e.wait_ge(sem_of(ops[j]), ops[j]["val"])
        if "arr" in o:
            e.wait_ge(T.sem["arr%d" % o["arr"]], coming)
        if o["calls"][0][0] == "send":
            t = o["calls"][0][1][0]
            for c in calls:
                tr = []
                for d, m in c:
                    rid, pid = topo.addr(T.cores[d])[:2]
                    tr.append(RemoteDMATransfer(dst_ids=[DstId(rid=rid, pnc=pid)], dma_engine_mask=m, remote_sem=T.sem["arr%d" % t],
                                                src=T["zs%d" % t][:, 32 * d:32 * d + 32], dst=T["z%d" % t][:, 32 * rank:32 * rank + 32]))
                g.remote_dma_fused(tr, local_sem=T.sem.sent)
            continue
        ins = None
        for name, args, kw in o["calls"]:
            a = [ap(x) for x in args]
            k = {key: ap(x) for key, x in kw.items()}
            if name == "tensor_copy": ins = e.tensor_copy(*a)
            elif name == "tensor_tensor": ins = e.tensor_tensor(*a)
            elif name == "tensor_scalar": ins = e.tensor_scalar(*a)
            elif name == "tensor_tensor_scan": ins = e.tensor_tensor_scan(*a)
            elif name == "transpose": ins = e.transpose(*a)
            elif name == "memset": ins = e.memset(*a)
            elif name == "activation": ins = e.activation(*a, **k)
            elif name == "iota": ins = e.iota(*a, **k)
            elif name == "affine_select": ins = e.affine_select(*a)
            elif name == "matmul": ins = e.matmul(*a)
            elif name == "dma_start": ins = e.dma_start(*a)
        if "sem" in o: ins.then_inc(sem_of(o), 16)
        elif o.get("inc"): ins.then_inc(sem_of(o), 1)
    for q, v in tot.items():
        g.wait_ge(T.sem["q" + q], v)
    g.wait_ge(T.sem.sent, going * (R - 1))
    for o in order:
        if "sem" in o: g.wait_ge(sem_of(o), 16)
